import numpy as np, ml_dtypes
CORES = [9,25,41,57]
N = 4
import mx_ref
BF = ml_dtypes.bfloat16
def gcols(t, e):
    v = np.concatenate([t.reshape(8, 16, -1, 4), np.zeros((8, 16, 1, 4), BF)], axis=2)
    return np.ascontiguousarray(np.stack([v[g][:, e[g]] for g in range(8)])).reshape(128, -1)
def tile(rs):
    return np.stack(rs, axis=2).reshape(128, -1).astype(BF)
def pick(q, e):
    c = np.concatenate([q[0].reshape(128, -1, 4), np.zeros((128, 1, 4), np.uint8)], axis=1); s = np.concatenate([q[1], np.ones((16, 1), np.uint8)], axis=1)
    return (np.ascontiguousarray(c[:, e].reshape(128, -1)), np.ascontiguousarray(s[:, e]))
def join(*qs):
    return (np.concatenate([q[0] for q in qs], axis=1), np.concatenate([q[1] for q in qs], axis=1))
def put(q, e, v):
    c, s = q[0].reshape(128, -1, 4).copy(), q[1].copy(); c[:, e] = v[0].reshape(128, -1, 4); s[:, e] = v[1]
    return (c.reshape(128, -1), s)
def pk(c, s):
    return (np.ascontiguousarray(c), mx_ref.live(s))
def emit(q):
    return q[0], q[1]
def packed(v, rng):
    q = [mx_ref.quantize(np.ascontiguousarray(v[r])) for r in range(N)]
    return np.stack([a for a, b in q]), np.stack([mx_ref.plane(b, rng) for a, b in q])
def values_of_codes():
    e, c = np.zeros((128, 128, 4), np.float32), np.zeros((128, 2, 4), np.uint8)
    e[np.arange(128), np.arange(128), 0] = 1
    c[:127, :, 0] = np.arange(256).reshape(2, 128).T[:127]
    return mx_ref.matmul(mx_ref.quantize(e.reshape(128, 512).astype(BF)), (c.reshape(128, 8), np.full((16, 2), 127, np.uint8))).T.reshape(-1).astype(np.float64)
CODE_VALUE, SCALE_VALUE = values_of_codes(), 2.0 ** (np.arange(256) - 127.0)
def decode(q):
    return (CODE_VALUE[q[0]].reshape(16, 8, -1, 4) * SCALE_VALUE[q[1]][:, None, :, None] + 0.0).reshape(128, -1).astype(np.float32)
def f(rng, *shape):
    return mx_ref.flush((rng.standard_normal(shape, dtype=np.float32) * np.exp2(rng.integers(-2, 3, shape[:-1] + (1,)))).astype(BF))
def wide(rng, *shape, cols=0):
    v = rng.standard_normal(shape, dtype=np.float32) * np.exp2(rng.integers(-12, 13, shape)).astype(np.float32)
    if cols: v *= np.repeat(np.exp2(rng.integers(-cols, cols + 1, shape[:-2] + (1, shape[-1] // 4))) * (rng.random(shape[:-2] + (1, shape[-1] // 4)) > 0.0625), 4, axis=-1).astype(np.float32)
    return mx_ref.flush(v.astype(BF))
C, R = 448, 3
STEP = [1, 2, 1]
DOUBLINGS = 9
def order(p):
    return np.argsort(-(p + np.float32(0.0)), axis=1, kind="stable")
def mates(o):
    m = np.zeros_like(o)
    np.put_along_axis(m, o, np.ascontiguousarray(o.reshape(8, -1, 2)[:, :, ::-1]).reshape(8, -1), axis=1)
    return m
def at(a, e):
    return np.take_along_axis(a, e, axis=1)
def big(v):
    v = v.astype(np.float32)
    v[np.abs(v) < np.float32(2.0 ** -16)] = 0
    return v.astype(BF)
def same(u):
    return np.stack([u.reshape(128, 512)] * N)
def numbers_of(rng):
    return {"x": big(f(rng, N, 128, 4 * C)), "u": same(np.array(f(rng, 128, 512))), "v": np.array(f(rng, N, 128, 512))}
def weights(rng, w):
    c, p = packed(w, rng)
    return {"wc": c, "ws": p}
def still(rng):
    return weights(rng, np.zeros((N, 128, 2048), BF))
def ring(rng):
    v = np.concatenate([rng.permutation(C), C + rng.permutation(C)]).reshape(C, 2)[rng.permutation(C)].reshape(-1)
    a, b = np.zeros(2 * C, int), np.zeros(2 * C, int)
    a[v[v < C]] = np.arange(C)
    a[v[v >= C]] = np.arange(C)
    b[np.roll(v, -1).reshape(C, 2)[rng.permutation(C)].reshape(-1)] = np.arange(2 * C)
    return a, b
def digits(s):
    return (((s[:, None] >> np.arange(12)) & 1) * 2.0 ** (np.arange(12) - 23.0)).reshape(-1, 3, 4).transpose(1, 0, 2)
def setup_inputs(rng):
    return {**numbers_of(rng), **weights(rng, big(f(rng, N, 128, 2048)))}
def setup_inputs_ties(rng):
    d = numbers_of(rng)
    e = rng.permutation(N)
    x = d["x"].reshape(N, 8, 16, C, 4)
    a = x[0][:, :8, :3].copy()
    a[:, :, 2] = 0
    for r in range(N):
        k = np.zeros(C, int) if r == e[0] else rng.permutation(C) % 3
        x[r][:, :8] = a[:, :, k]
    x[e[1]] = 0
    u = d["u"][0].reshape(8, 16, 128, 4).copy()
    u[:, 8:, ::8] = 0
    g = 16 * rng.permutation(8)
    u[:, :, g[:2]] = 0
    u[:, :, g[2:4] + 8] = 0
    u[:, :, [g[4], g[4] + 8]] = 0
    return {"x": x.reshape(N, 128, 4 * C), "u": same(u), "v": d["v"], **weights(rng, big(f(rng, N, 128, 2048)))}
def setup_inputs_near(rng):
    d = numbers_of(rng)
    x = d["x"].astype(np.float32).reshape(N, 8, 16, C, 4)
    o = rng.permutation(8)
    c = np.array([1.0, -1.0, 1.0, -1.0, 1.0, -1.0, 0.0, 0.0])[o]
    k = np.array([1.0, 1.0, 1.0, 1.0, 2.0 ** -30, 2.0 ** -30, 2.0 ** -30, -2.0 ** -30])[o].astype(np.float32).astype(BF)
    x[:, :, 0] = 0
    x[:, :, 0, :, 0] = c[None, :, None]
    x[:, :, 14:] = rng.integers(4, 8, (N, 8, 2, C, 4)) * rng.choice([-1.0, 1.0], (N, 8, 2, C, 4)) * 2.0 ** -20
    for i in range(0, N, 2):
        for g in range(8):
            a, b = ring(rng)
            for s in range(2):
                x[i + s, g, 8:11] = digits(a[C * s:C * s + C])
                x[i + s, g, 11:14] = digits(b[C * s:C * s + C])
    u = d["u"][0].reshape(128, 128, 4).copy()
    u[:, ::8] = 0
    for g in range(8):
        h = 16 * g
        u[h, h, 0] = k[g]
        u[h, h + 8, 0] = k[g]
        u[h + 8:h + 11, h] = k[g]
        u[h + 11:h + 14, h + 8] = k[g]
    return {"x": x.reshape(N, 128, 4 * C).astype(BF), "u": same(u), "v": d["v"], **still(rng)}
def setup_inputs_huge(rng):
    d = numbers_of(rng)
    c = np.ones((N, C))
    for i, k in enumerate(rng.permutation(N // 2) % 3):
        if k == 1: c[2 * i + int(rng.integers(2))] = -1
        if k == 2:
            for s in range(2): c[2 * i + s] = rng.permutation(C) % 2 * 2.0 - 1.0
    x = 2.0 ** 30 * (0.6 + 0.4 * rng.random((N, 128, C, 4))) * c[:, None, :, None]
    g = np.stack([rng.permutation(8) % 2, rng.permutation(8) % 2], axis=1).reshape(16) * 2.0 - 1.0
    u = d["u"][0].reshape(128, 128, 4).copy()
    u[:, ::8] = (2.0 ** 30 * (1 - 0.25 * rng.random((128, 16, 4))) * g[None, :, None]).astype(np.float32).astype(BF)
    return {"x": x.astype(np.float32).reshape(N, 128, 4 * C).astype(BF), "u": same(u), "v": d["v"], **still(rng)}
def setup_inputs_spread(rng):
    d = setup_inputs(rng)
    d["x"] = big(wide(rng, N, 128, 4 * C, cols=6))
    return d
def check_inputs(d):
    b = []
    for k in ("x", "u", "v"):
        a = np.abs(d[k].astype(np.float32))
        if not (np.isfinite(a).all() and ((a == 0) | (a >= 2.0 ** -30) & (a <= 2.0 ** 30)).all()): b.append("a value of " + k)
    if (d["u"] != d["u"][:1]).any(): b.append("u differs between ranks")
    if ((d["wc"] & 127) == 127).any(): b.append("a code of wc is no number")
    a = np.zeros((128, 4, 4), np.float32)
    a[:, 1] = 2.0 ** -30
    a[:, 2] = 2.0 ** 30
    e = emit(mx_ref.quantize(a.reshape(128, 16).astype(BF)))[1][0]
    s = np.stack([mx_ref.live(p) for p in d["ws"]])
    if not ((s == e[0]) | (s >= e[1]) & (s <= e[2])).all(): b.append("a scale of ws")
    return b
def reference(x, u, v, wc, ws):
    qu = mx_ref.quantize(u[0])
    lay = [pk(wc[r], ws[r]) for r in range(N)]
    now = [x[r] for r in range(N)]
    for t in range(R):
        num, s, sent, reds = [], [], [], [None] * N
        for r in range(N):
            q = mx_ref.quantize(now[r])
            num.append(decode(q).astype(BF))
            s.append(mx_ref.matmul(qu, q))
        own = [mates(order(s[r][::16])) for r in range(N)]
        for lo in range(N):
            hi = lo ^ STEP[t]
            if lo < hi:
                a = np.concatenate([own[lo], C + own[hi]], axis=1)
                b = mates(order(np.concatenate([s[lo][8::16], s[hi][8::16]], axis=1)))
                to = at(b, a)
                low = np.tile(np.arange(2 * C), (8, 1))
                for i in range(DOUBLINGS):
                    low = np.minimum(low, at(low, to))
                    to = at(to, to)
                blue = low > at(low, a)
                reds[lo] = np.argsort(blue[:, :C], axis=1, kind="stable")[:, :C // 2]
                reds[hi] = np.argsort(blue[:, C:], axis=1, kind="stable")[:, :C // 2]
        for r in range(N):
            one = gcols(num[r], reds[r]).astype(np.float32)
            two = gcols(num[r], at(own[r], reds[r])).astype(np.float32)
            sent.append(mx_ref.quantize(((one + two) * np.float32(0.5)).astype(BF)))
        for r in range(N):
            e = np.tile(np.arange(C), (8, 1))
            np.put_along_axis(e, reds[r], np.tile(C + np.arange(C // 2), (8, 1)), axis=1)
            came = decode(sent[r ^ STEP[t]]).astype(BF)
            z = mx_ref.quantize(gcols(np.concatenate([num[r], came], axis=1), e))
            d = decode(z).reshape(128, C, 4)
            now[r] = tile([d[:, :, b] + np.maximum(mx_ref.matmul(pick(lay[r], np.arange(128 * b, 128 * b + 128)), z), np.float32(0.0)) * np.float32(0.03125) for b in range(4)])
    y, ol = np.zeros((N, 128, C), np.float32), np.zeros((N, 8, C // 2), np.float32)
    oc, osc = np.zeros((N, 128, 4 * C), np.uint8), np.zeros((N, 16, C), np.uint8)
    for r in range(N):
        q = mx_ref.quantize(now[r])
        y[r] = mx_ref.matmul(mx_ref.quantize(v[r]), q)
        ol[r] = reds[r]
        oc[r], osc[r] = emit(q)
    return {"y": y, "ol": ol, "oc": oc, "osc": osc}

@@ -1,0 +1,548 @@
+from concourse.mybir import dt, AluOpType, ActivationFunctionType
+
+C, H, J, R = 448, 224, 896, 3
+STEP = [1, 2, 1]
+W16 = C // 16
+NS = W16 - 1
+TW = C + C + 32
+DP = 4 * (C + H)
+SC_B, SC_A = 12, 15
+SORT_AT, SEARCH_AT = 2, 10
+HOLD, DROP = 1024.0, -4096.0
+F32, BF, I32, U16, X4, U8 = "float32", "bfloat16", "int32", "uint16", "float8_e4m3fn_x4", "uint8"
+
+_SB = {
+    "x0": (4 * C, BF), "ub": (512, BF), "vb": (512, BF), "xt": (4 * C, BF), "yt": (4 * C, BF), "bt": (4 * H, BF),
+    "qu": (128, X4), "su": (128, U8), "qur": (256, X4), "sur": (256, U8), "qv": (128, X4), "sv": (128, U8),
+    "qw": (512, X4), "sw": (512, U8), "qe": (512, X4), "se": (512, U8), "et": (2048, BF), "one": (128, BF), "idn": (128, BF),
+    "qz": (C, X4), "sz": (C, U8), "qb": (H, X4), "sq": (H, U8), "qt%d" % R: (C, X4), "st%d" % R: (C, U8),
+    "pi": (16, I32), "cf": (32, F32), "upi": (16, I32), "upk": (16, U16), "cl": (2, U16),
+    "r16": (TW + 16, BF), "r4": (C + 4, BF), "md": (C, BF), "kz": (C, BF), "k16": (J, BF), "k4": (C, BF),
+    "k0": (TW, BF), "k27": (W16 * NS, BF),
+    "ka": (J, BF), "kb": (J, BF), "iot": (J, F32), "jf": (C, F32), "jw": (W16, F32), "j4": (112, F32),
+    "msk": (C, F32), "ha": (C, F32), "hb": (C, F32), "eq": (C, BF), "ea": (C, BF), "eb": (C, BF),
+    "fl": (3 * C, BF), "ca": (W16 * H, BF), "cb": (W16 * H, BF), "sg": (2 * C, BF), "lha": (96, F32), "lhb": (96, F32),
+    "t1": (112, F32), "t2": (112, F32), "ii": (256, I32), "l1": (56, U16), "l2": (84, U16), "rs": (64, F32),
+    "tb": (C, F32), "zp": (C + 32, F32), "zt": (TW, F32), "fp": (C + 32, BF), "ft": (TW, BF), "fs": (TW, BF),
+    "f1": (W16 * NS, BF), "s1": (W16 * NS, BF),
+    "inv": (J, F32), "bm": (J, F32), "am": (C, F32), "vp": (C, F32), "scn": (J, F32), "j0": (J, F32), "j1": (J, F32),
+    "w0": (J, F32), "w1": (J, F32), "wd": (J, F32), "pk": (112, U16), "red": (J, F32), "cum": (J, F32), "mm": (J, F32),
+    "ew": (C + H, F32), "lb": (112, U16), "ly": (112, U16), "dw": (DP + 4 * C, BF), "bh": (4 * H, F32),
+    "rl": (2 * C, F32), "yo": (C, F32),
+}
+for _t in range(R):
+    for _n, _w, _d in (("z", 64, F32), ("rb", W16, U16), ("aml", W16, U16), ("qt", C, X4), ("st", C, U8)):
+        _SB["%s%d" % (_n, _t)] = (_w, _d)
+        _SB["%sp%d" % (_n, _t)] = (_w, _d)
+SCRATCH = {k: ("sbuf", [128, n], d) for k, (n, d) in _SB.items()}
+SCRATCH["ps"] = ("psum", [128, 4096], F32)
+SEMAPHORES = ["cp", "cv", "cs", "cg", "sent", "dx", "du", "dv", "dl", "dol", "doc", "dy"] + \
+    ["m%d_%d" % (m, t) for m in range(4) for t in range(R)]
+
+ADD, SUB, MUL, MAX, MIN = AluOpType.add, AluOpType.subtract, AluOpType.mult, AluOpType.max, AluOpType.min
+GE, GT, EQ, NE, LT = AluOpType.is_ge, AluOpType.is_gt, AluOpType.is_equal, AluOpType.not_equal, AluOpType.is_lt
+AND, SHR = AluOpType.bitwise_and, AluOpType.logical_shift_right
+FN = ActivationFunctionType
+
+
+def A(name, a=0, b=None, s=1):
+    return (name, a, _SB[name][0] if b is None else b, s)
+
+
+def PS(bank, n=C):
+    return ("ps", 512 * bank, 512 * bank + n, 1)
+
+
+def IND(win, off):
+    return ("ind", win, off)
+
+
+def bits(v):
+    if v[0] == "ps":
+        return 1 << (v[1] // 512)
+    if v[3] == 1:
+        return ((1 << (v[2] - v[1])) - 1) << v[1]
+    m = 0
+    for i in range(v[1], v[2], v[3]):
+        m |= 1 << i
+    return m
+
+
+def emit(ops, g, T):
+    queue = {"p": g.tensor, "v": g.vector, "s": g.scalar, "g": g, "y": g.sync}
+    log, known, count = {}, {e: {} for e in queue}, {}
+    for o in ops:
+        e = o["q"]
+        deps = {}
+        for v, wr in [(v, False) for v in o["r"]] + [(v, True) for v in o["w"]]:
+            m = bits(v)
+            for (m2, wr2, d) in log.get(v[0], []):
+                if m & m2 and (wr or wr2 or (v[0] == "ps" and d["lane"] != o["lane"])) and d is not o:
+                    if d["lane"] not in deps or deps[d["lane"]]["n"] < d["n"]:
+                        deps[d["lane"]] = d
+        for d in o.get("after", []):
+            deps[d["lane"]] = d
+        count[o["lane"]] = count.get(o["lane"], 0) + 1
+        o["n"] = count[o["lane"]]
+        o["waits"] = []
+        if e is not None:
+            for d in sorted(deps.values(), key=lambda d: -d["k"]):
+                if known[e].get(d["lane"], 0) < d["n"]:
+                    o["waits"].append(d)
+                    d["inc"] = True
+                    for l, n in d["clock"].items():
+                        if known[e].get(l, 0) < n:
+                            known[e][l] = n
+            o["clock"] = dict(known[e])
+        else:
+            o["clock"] = {}
+        o["clock"][o["lane"]] = o["n"]
+        for v, wr in [(v, False) for v in o["r"]] + [(v, True) for v in o["w"]]:
+            m = bits(v)
+            old = log.get(v[0], [])
+            if wr:
+                old = [x for x in old if x[0] & ~m]
+            else:
+                old = [x for x in old if not (x[2]["lane"] == o["lane"] and not x[1] and not x[0] & ~m)]
+            log[v[0]] = old + [(m, wr, o)]
+    total = {}
+    for o in ops:
+        if o["lane"] in queue:
+            if o.get("inc"):
+                total[o["lane"]] = total.get(o["lane"], 0) + 1
+                o["sem"], o["val"] = "c" + o["lane"], total[o["lane"]]
+        elif o["lane"] != "none":
+            total[o["lane"]] = total.get(o["lane"], 0) + o["add"]
+            o["sem"] = o["lane"]
+    for o in ops:
+        if o["q"] is None:
+            continue
+        q = queue[o["q"]]
+        for d in o["waits"]:
+            q.wait_ge(T.sem[d["sem"]], d["val"] if d["lane"] in queue else total[d["lane"]])
+        if o["fn"] is None:
+            continue
+        ins = o["fn"](q)
+        if o["lane"] in queue:
+            if o.get("inc"):
+                ins.then_inc(T.sem[o["sem"]], 1)
+        elif o.get("dma"):
+            ins.then_inc(T.sem[o["sem"]], 16)
+
+
+def rank_program(g, core, T, topo):
+    rank = T.rank_of(core)
+    if rank is None:
+        return
+    ops = []
+
+    def ap(v):
+        if not isinstance(v, tuple):
+            return v
+        if v[0] == "ind":
+            return ap(v[1]).indirect(ap(v[2]))
+        return T[v[0]][:, v[1]:v[2]:v[3]] if v[3] > 1 else T[v[0]][:, v[1]:v[2]]
+
+    def flat(vs):
+        out = []
+        for v in vs:
+            if isinstance(v, tuple):
+                out += [v[1], v[2]] if v[0] == "ind" else [v]
+        return out
+
+    def rec(q, fn, r, w, lane=None, **kw):
+        r, w2 = flat(r), []
+        for v in w:
+            if v[0] == "ind":
+                w2.append(v[1])
+                r.append(v[2])
+            else:
+                w2.append(v)
+        o = dict(q=q, fn=fn, r=r, w=w2, lane=lane or q, k=len(ops), **kw)
+        ops.append(o)
+        return o
+
+    def copy(out, in_):
+        return rec("v", lambda q: q.tensor_copy(ap(out), ap(in_)), [in_], [out])
+
+    def turn(out, in_):
+        return rec("v", lambda q: q.transpose(ap(out), ap(in_)), [in_], [out])
+
+    def tt(out, a, b, op):
+        return rec("v", lambda q: q.tensor_tensor(ap(out), ap(a), ap(b), op), [a, b], [out])
+
+    def ts(out, a, s1, op0, s2=None, op1=None):
+        if s2 is None:
+            return rec("v", lambda q: q.tensor_scalar(ap(out), ap(a), ap(s1), None, op0), [a, s1], [out])
+        return rec("v", lambda q: q.tensor_scalar(ap(out), ap(a), ap(s1), ap(s2), op0, op1), [a, s1, s2], [out])
+
+    def scan(out, d0, d1, init, op0, op1):
+        return rec("v", lambda q: q.tensor_tensor_scan(ap(out), ap(d0), ap(d1), init, op0, op1), [d0, d1], [out])
+
+    def fill(out, c):
+        return rec("v", lambda q: q.memset(ap(out), c), [], [out])
+
+    def quant(codes, scales, in_):
+        return rec("v", lambda q: q.quantize_mx(ap(codes), ap(scales), ap(in_)), [in_], [codes, scales])
+
+    def act(out, in_, fn, bias=0.0, scale=1.0, acc=None):
+        if acc is None:
+            return rec("s", lambda q: q.activation(ap(out), ap(in_), fn, bias=ap(bias), scale=scale), [in_, bias], [out])
+        return rec("s", lambda q: q.activation(ap(out), ap(in_), fn, bias=ap(bias), scale=scale, accum_out=ap(acc)),
+                   [in_, bias], [out, acc])
+
+    def mm(out, lc, ls, rc, rs):
+        return rec("p", lambda q: q.matmul_mx(ap(out), ap(lc), ap(ls), ap(rc), ap(rs), True, True), [lc, ls, rc, rs], [out])
+
+    def iota(out, pattern, base, cm):
+        if _SB[out[0]][1] == I32:
+            return rec("g", lambda q: q.iota(ap(out), pattern, base, cm), [], [out])
+        return rec("g", lambda q: q.iota(ap(out), pattern, base, cm, allow_small_or_imprecise_dtypes=True), [], [out])
+
+    def dma(q, sem, mk, r, w):
+        return rec(q, lambda e: e.dma_start(*mk()), r, w, lane=sem, dma=True, add=16)
+
+    def u8(v):
+        return ap(v).bitcast(dt.uint8) if _SB[v[0]][1] == X4 else ap(v)
+
+    def exchange(peer, m, t, names, width=None):
+        rid, pid, _ = topo.addr(peer)
+        mask, n = topo.mask(core, peer), len(topo.engines(core, peer))
+        sem = "m%d_%d" % (m, t)
+        for name in names:
+            src, dst = A("%s%d" % (name, t), 0, width), A("%sp%d" % (name, t), 0, width)
+            rec("g", lambda q, src=src, dst=dst: q.remote_dma(u8(dst), u8(src), T.sem[sem], T.sem.sent, pid, rid, mask),
+                [src], [], lane="sent", add=n)
+        rec(None, None, [], [A("%sp%d" % (name, t), 0, width) for name in names], lane=sem,
+            add=len(topo.engines(peer, core)) * len(names))
+
+    def col(k):
+        return A("cf", k, k + 1)
+
+    def I(a, n):
+        return A("ii", a, a + n)
+
+    def half(name, a):
+        return A(name, a, a + C)
+
+    dma("y", "dx", lambda: (ap(A("x0")), T.x[:]), [], [A("x0")])
+    dma("s", "du", lambda: (ap(A("ub")), T.u[:]), [], [A("ub")])
+    dma("y", "dv", lambda: (ap(A("vb")), T.v[:]), [A("x0")], [A("vb")])
+    dma("y", "dl", lambda: (u8(A("qw")), T.wc[:]), [], [A("qw")])
+    dma("y", "dl", lambda: (ap(A("sw")), T.ws[:]), [], [A("sw")])
+
+    Q, TT, RR, PAR, ODD, QHALF, H16, H4, QH, RH, YC, BC, X1, X2, X3 = range(15)
+    iota(A("pi", 0, 1), [[1, 1]], 0, 1)
+    iota(A("upi"), [[-8, 2], [16, 8]], 8, 0)
+    iota(A("r16"), [[0, TW // 16 + 1], [1, 16]], 0, 0)
+    fill(A("one"), 1.0)
+    fill(A("et"), 0.0)
+    for name in ("lha", "lhb", "rs", "zp", "fp"):
+        fill(A(name), 0.0)
+    p = A("pi", 0, 1)
+    ts(A("pi", 1, 2), p, 15, AND)
+    ts(A("pi", 2, 3), p, 3, AND)
+    ts(A("pi", 3, 4), p, 2, SHR, 3, AND)
+    ts(A("pi", 4, 5), p, 4, SHR, 1, AND)
+    ts(A("pi", 5, 6), p, 1, AND)
+    ts(A("pi", 6, 7), p, 1, SHR, 7, AND)
+    copy(A("upk"), A("upi"))
+    copy(A("cf", 0, 6), A("pi", 1, 7))
+    iota(A("iot"), [[1, J]], 0, 0)
+    ts(col(H16), col(Q), 15.0, LT, HOLD, MUL)
+    ts(col(H4), col(RR), 3.0, LT, HOLD, MUL)
+    tt(col(X1), col(ODD), col(PAR), NE)
+    tt(col(X2), col(ODD), col(PAR), GT)
+    ts(col(X3), col(QHALF), 32.0, MUL, 15.0, ADD)
+    quant(A("qu"), A("su"), A("ub"))
+    ts(A("md"), A("r16", 16, 16 + C), col(Q), EQ)
+    ts(A("kz"), A("r16", 16, 16 + C), col(Q), NE)
+    rec("v", lambda q: q.tensor_copy(ap(A("qur")).bitcast(dt.uint32), ap(A("qu")).bitcast(dt.uint32).indirect(ap(A("upk")))),
+        [A("qu"), A("upk")], [A("qur")])
+    rec("s", lambda q: q.activation(ap(A("sur")), ap(IND(A("su"), A("upk"))), FN.Copy), [A("su"), A("upk")], [A("sur")])
+
+    def late_constants():
+        rec("g", lambda q: q.affine_select(ap(A("idn")), ap(A("one")), [[-1, 128]], EQ, 0.0, 0, 1), [A("one")], [A("idn")])
+        iota(A("r4"), [[0, C // 4 + 1], [1, 4]], 0, 0)
+        iota(A("kb", 0, W16 * NS), [[0, W16], [1, NS]], 0, 0)
+        ts(col(X1), col(X1), float(C), MUL, col(X3), ADD)
+        ts(col(X2), col(X2), 2.0, MUL, col(PAR), ADD)
+        tt(col(QH), col(Q), col(H16), ADD)
+        tt(col(RH), col(RR), col(H4), ADD)
+        yield
+        ts(col(X1), col(X2), 16.0, MUL, col(X1), ADD)
+        ts(col(YC), col(H4), 4.0, MUL, col(TT), SUB)
+        ts(col(X3), col(TT), 2049.0, MUL)
+        yield
+        ts(A("t1", 0, 2), A("iot", 0, 512, 256), col(X1), ADD, float(TW - 1), MIN)
+        ts(col(BC), col(H4), 8192.0, MUL, col(X3), SUB)
+        ts(A("ka"), A("r16", 16, 16 + J), col(Q), EQ, DROP, MUL)
+        yield
+        copy(A("cl"), A("t1", 0, 2))
+        ts(A("k16"), A("r16", 15, 15 + J), col(Q), EQ, HOLD, MUL)
+        yield
+        ts(A("jw"), A("iot", 0, C, 16), col(QH), ADD)
+        ts(A("j4"), A("iot", 0, C, 4), col(RH), ADD)
+        ts(A("k0"), A("r16", 0, TW), 1.0, MIN)
+        yield
+        tt(A("k16"), A("k16"), A("ka"), ADD)
+        for b in range(4):
+            copy(A("et", 512 * b + b, 512 * (b + 1), 4), A("idn"))
+        yield
+        ts(A("ka", 0, C), A("r4", 4, 4 + C), col(RR), EQ, DROP, MUL)
+        ts(A("k4"), A("r4", 3, 3 + C), col(RR), EQ, HOLD, MUL)
+        quant(A("qe"), A("se"), A("et"))
+        yield
+        tt(A("k4"), A("k4"), A("ka", 0, C), ADD)
+        quant(A("qv"), A("sv"), A("vb"))
+        ts(A("jf"), A("iot", 0, C), 1.0 / 2048, MUL)
+        yield
+        ts(A("k27"), A("kb", 0, W16 * NS), 1.0, MIN)
+        yield
+
+    def stat(name, b):
+        return A("q" + name, 128 * b, 128 * b + 128), A("s" + name, 128 * b, 128 * b + 128)
+
+    def chain(*gens):
+        for x in gens:
+            for _ in x:
+                yield
+
+    def idle(n):
+        for _ in range(n):
+            yield
+
+    def run(x):
+        for _ in x:
+            pass
+
+    def vector_counts(src, h, out, blocks, side):
+        last = None
+        for n, c in enumerate(list(range(blocks)) + [None]):
+            f = C * (n % 3)
+            if c is not None:
+                cut, own = 16 * c + 16, A(h, 16 * c + 15, 16 * c + 16)
+                ts(A("fl", f, f + cut), (src[0], src[1], src[1] + cut, 1), own, GE, 0.5, SUB)
+                ts(A("fl", f + cut, f + C), (src[0], src[1] + cut, src[2], 1), own, GT, 0.5, SUB)
+            next(side, None)
+            if last is not None:
+                scan(A(out, last[1] * H, last[1] * H + H), A("fl", last[0], last[0] + H), A("fl", last[0] + H, last[0] + C),
+                     0.0, ADD, ADD)
+                next(side, None)
+            last = (f, c)
+        run(side)
+
+    def scalar_counts(src, h, lh, blocks):
+        last = None
+        for n, c in enumerate(list(range(W16 - blocks, W16)) + [None]):
+            f = C * (n % 2)
+            if c is not None:
+                act(half("sg", f), src, FN.Sign, bias=A(h, 16 * c + 15, 16 * c + 16), scale=-1.0)
+            if last is not None:
+                a, cut = last[0], last[0] + 16 * last[1] + 16
+                act(A("sg", a, cut), A("sg", a, cut), FN.Sign, bias=0.5, scale=-1.0, acc=A(lh, last[1], last[1] + 1))
+                if cut < a + C:
+                    act(A("sg", cut, a + C), A("sg", cut, a + C), FN.Sign, bias=-0.5, scale=-1.0,
+                        acc=A(lh, 32 + last[1], 33 + last[1]))
+            last = (f, c)
+
+    def places(counts, lh, blocks, equal):
+        a = W16 - blocks
+        tt(A(lh, 64 + a, 64 + W16), A(lh, a, W16), A(lh, 32 + a, 32 + W16), ADD)
+        yield
+        ts(A(counts, a * H + H - 1, W16 * H, H), A(lh, 64 + a, 64 + W16), 0.5, MUL)
+        yield
+        tt(A("t1", 0, W16), A(counts, H - 1, W16 * H, H), A(equal, 15, C, 16), SUB)
+        yield
+
+    def own_scores(src, h):
+        tt(A("msk"), src, A("md"), MUL)
+        yield
+        scan(A(h), A("kz"), A("msk"), 0.0, MUL, ADD)
+        yield
+
+    def ties(src, h, out):
+        tt(A("eq"), src, A(h), EQ)
+        yield
+        scan(A(out), A("kz"), A("eq"), 0.0, MUL, ADD)
+        yield
+
+    def unpack(codes, scales, at):
+        for b in range(4):
+            mm(PS(4 + b), *stat("e", b), codes, scales)
+        for b in range(4):
+            act(A("dw", at + b, at + 4 * C, 4), PS(4 + b), FN.Copy, scale=0.5)
+
+    quant(A("qt0"), A("st0"), A("x0"))
+    for t in range(R):
+        peer_rank = rank ^ STEP[t]
+        peer = T.cores[peer_rank]
+        up = 1 if rank > peer_rank else 0
+        me, other = C * up, C * (1 - up)
+        before = GE if up else GT
+        z, zp, rb, rbp, aml, amp = ["%s%d" % (n, t) for n in ("z", "zp", "rb", "rbp", "aml", "amlp")]
+        QT = (A("qt%d" % t), A("st%d" % t))
+        SBV, SBS, SAV, SAS = PS(0), PS(1), PS(2), PS(3)
+        exchange(peer, 3, t, ["qt", "st"])
+        mm(SBV, *stat("ur", 0), *QT)
+        mm(SBS, *stat("ur", 0), *QT)
+        mm(SAV, *stat("ur", 1), *QT)
+        mm(SAS, *stat("ur", 1), *QT)
+
+        def sort_b():
+            for _ in places("cb", "lhb", SC_B, "eb"):
+                yield
+            ts(A("l1", 0, W16), A("t1", 0, W16), float(H), ADD)
+            ts(A("rs", 0, W16), A("t1", 0, W16), float(H), ADD)
+            yield
+            copy(IND(half("zp", 16), A("l1", 0, W16)), A("tb"))
+            yield
+            turn(half("zt", 0), half("zp", 16))
+            turn(A("zt", C, TW), A("zp"))
+            yield
+            copy(A(z, 0, 32), IND(A("zt"), A("cl")))
+            yield
+            copy(A(z, W16, W16 + NS), A("zp", 31, C, 16))
+            exchange(peer, 0, t, ["z"], W16 + NS)
+            yield
+
+        def search():
+            for c in range(W16):
+                ts(A("f1", NS * c, NS * c + NS), A(zp, W16, W16 + NS), A("hb", 16 * c + 15, 16 * c + 16), before)
+            scan(A("s1"), A("k27"), A("f1"), 0.0, MUL, ADD)
+            yield
+            copy(A("l2", 0, W16), A("s1", NS - 1, W16 * NS, NS))
+            ts(A("t2", 0, W16), A("s1", NS - 1, W16 * NS, NS), 16.0, MUL)
+            yield
+            tt(half("fp", 16), IND(A(zp, 0, W16), A("l2", 0, W16)), A("tb"), before)
+            tt(A("rs", 32, 32 + W16), A("t2", 0, W16), A("rs", 0, W16), ADD)
+            turn(half("ft", 0), half("fp", 16))
+            turn(A("ft", C, TW), A("fp"))
+            yield
+            scan(A("fs"), A("k0"), A("ft"), 0.0, MUL, ADD)
+            yield
+            tt(I(W16, 32), IND(A("fs"), A("cl")), A("rs", 32, 64), ADD)
+            yield
+            copy(A(rb), I(W16, W16))
+            exchange(peer, 2, t, ["rb"])
+
+        act(A("tb"), SBS, FN.Copy)
+        run(own_scores(SBV, "hb"))
+        scalar_counts(SBS, "hb", "lhb", SC_B)
+        side = [own_scores(SAV, "ha"), ties(SBV, "hb", "eb"), ties(SAV, "ha", "ea")]
+        if t == 0:
+            side.append(late_constants())
+        vector_counts(SBV, "hb", "cb", W16 - SC_B, chain(*side))
+        scalar_counts(SAS, "ha", "lha", SC_A)
+        vector_counts(SAV, "ha", "ca", W16 - SC_A, chain(idle(SORT_AT), sort_b(), idle(SEARCH_AT), search()))
+        unpack(*QT, 0)
+        act(A("wd"), A("iot"), FN.Copy)
+        unpack(A("qtp%d" % t), A("stp%d" % t), DP)
+
+        run(places("ca", "lha", SC_A, "ea"))
+        ts(A("l1", 0, W16), A("t1", 0, W16), float(H), ADD)
+        ts(I(0, W16), A("t1", 0, W16), float(H), ADD)
+        copy(IND(half("inv", 0), A("l1", 0, W16)), half("iot", 0))
+        n = 3 * W16
+        copy(I(2 * W16, W16), A(rbp))
+        ts(I(128, n), I(0, n), 1, AND)
+        ts(A("t1", 0, n), I(128, n), -2.0, MUL, 1.0, ADD)
+        tt(A("t2", 0, n), A("t1", 0, n), I(0, n), ADD)
+        copy(A("l2"), A("t2", 0, n))
+        copy(A("am"), IND(half("inv", 0), A("l2", 0, W16)))
+        scan(half("scn", 0), half("k16", 0), A("am"), 0.0, ADD, MAX)
+        ts(A(aml), A("scn", 15, C, 16), col(H16), SUB)
+        exchange(peer, 1, t, ["aml"])
+
+        copy(IND(A("inv"), A(rb)), half("iot", me))
+        copy(IND(A("inv"), A(rbp)), half("iot", other))
+        act(half("bm", other), IND(A("inv"), A("l2", 2 * W16, 3 * W16)), FN.Copy)
+        copy(half("bm", me), IND(A("inv"), A("l2", W16, 2 * W16)))
+        act(half("j0", other), IND(half("bm", other), A(amp)), FN.Copy)
+        copy(half("j0", me), IND(half("bm", me), A(aml)))
+
+        low = "iot"
+        for k in range(9):
+            jc, jn, pk = "j%d" % (k % 2), "j%d" % (1 - k % 2), 56 * (k % 2)
+            nxt = "w%d" % (k % 2)
+            scan(A("scn"), A("k16"), A(jc), 0.0, ADD, MAX)
+            ts(A("pk", pk, pk + 56), A("scn", 15, J, 16), col(H16), SUB)
+            if k < 8:
+                act(A(jn), IND(A(jc), A("pk", pk, pk + 56)), FN.Copy)
+                tt(A(nxt), IND(A(low), A("pk", pk, pk + 56)), A("wd"), MIN)
+                act(A("wd"), A(nxt), FN.Copy)
+            else:
+                for a in (other, me):
+                    tt(half(nxt, a), IND(A(low), A("pk", pk + a // 16, pk + a // 16 + W16)), half("wd", a), MIN)
+                    act(half("wd", a), half(nxt, a), FN.Copy)
+            if k == 0:
+                tt(A("vp"), IND(half("iot", 0), A(amp)), A("jf"), ADD)
+            low = nxt
+
+        tt(half("red", 0), IND(half(low, other), A(amp)), half("wd", other), GT)
+        scan(half("cum", 0), half("red", 0), half("red", 0), float(C - 1), ADD, MAX)
+        tt(half("mm", 0), half("cum", 0), half("red", 0), MUL)
+        scan(half("scn", 0), half("k16", 0), half("mm", 0), 0.0, ADD, MAX)
+        tt(A("t1", 0, W16), A("scn", 15, C, 16), A("jw"), MAX)
+        tt(half("red", C), IND(half(low, me), A(aml)), half("wd", me), GT)
+        ts(A("l1", 0, W16), A("t1", 0, W16), col(H16), SUB)
+        scan(half("cum", C), half("red", C), half("red", C), float(C - 1), ADD, MAX)
+        copy(IND(A("ew"), A("l1", 0, W16)), A("vp"))
+        scan(A("scn", 0, H), A("k4", 0, H), A("ew", C, C + H), 0.0, ADD, MAX)
+        ts(I(0, 56), A("scn", 3, H, 4), 8192.0, MUL, col(BC), SUB)
+        ts(I(56, 56), I(0, 56), 2047, AND)
+        ts(I(112, 56), I(0, 56), 11, SHR)
+        copy(A("lb"), I(56, 112))
+        theirs = A("dw", DP, DP + 4 * C)
+        for h in range(2):
+            act(half("bh", C * h), IND(theirs, A("lb", W16 * h, W16 * h + W16)), FN.Copy)
+        tt(half("mm", C), half("cum", C), half("red", C), MUL)
+        for h in range(2):
+            tt(half("bt", C * h), IND(theirs, A("lb", 56 + W16 * h, 56 + W16 * h + W16)), half("bh", C * h), ADD)
+        quant(A("qb"), A("sq"), A("bt"))
+        for b in range(4):
+            mm(PS(b, H), *stat("e", b), A("qb"), A("sq"))
+        scan(half("scn", 0), A("k4"), half("mm", C), 0.0, ADD, MAX)
+        tt(A("t1"), A("scn", 3, C, 4), A("j4"), MAX)
+        for b in range(4):
+            out = A("dw", 4 * C + b, DP, 4)
+            if b == 3:
+                ts(A("ly"), A("t1"), 4.0, MUL, col(YC), SUB)
+                ts(out, PS(b, H), 0.5, MUL)
+            else:
+                act(out, PS(b, H), FN.Copy, scale=0.5)
+        act(A("yt", J, 2 * J), IND(A("dw", 0, DP), A("ly", 56, 112)), FN.Copy, scale=2.0)
+        ts(A("yt", 0, J), IND(A("dw", 0, DP), A("ly", 0, 56)), 2.0, MUL)
+
+        quant(A("qz"), A("sz"), A("yt"))
+        for b in range(4):
+            mm(PS(4 + b), *stat("w", b), A("qz"), A("sz"))
+            mm(PS(b), *stat("e", b), A("qz"), A("sz"))
+        if t == R - 1:
+            scan(half("scn", 0), half("k16", 0), half("mm", C), 0.0, ADD, MAX)
+        for b in range(4):
+            rl = half("rl", C * (b % 2))
+            act(rl, PS(4 + b), FN.Relu, scale=0.03125)
+            tt(A("xt", b, 4 * C, 4), PS(b), rl, ADD)
+            if t == R - 1 and b == 0:
+                tt(A("t1", 0, W16), A("scn", 15, C, 16), A("jw"), MAX)
+            if t == R - 1 and b == 1:
+                ts(A("l1", 0, W16), A("t1", 0, W16), col(H16), SUB)
+        quant(A("qt%d" % (t + 1)), A("st%d" % (t + 1)), A("xt"))
+
+    QT = (A("qt%d" % R), A("st%d" % R))
+    mm(PS(4), A("qv"), A("sv"), *QT)
+    dma("y", "doc", lambda: (T.oc[:], u8(QT[0])), [QT[0]], [])
+    for k in range(4):
+        dma("y", "doc", lambda k=k: (T.osc[4 * k:4 * k + 4, :], T["st%d" % R][32 * k:32 * k + 4, :]), [QT[1]], [])
+    copy(IND(A("ew"), A("l1", 0, W16)), half("iot", 0))
+    act(A("yo"), PS(4), FN.Copy)
+    dma("s", "dy", lambda: (T.y[:], ap(A("yo"))), [A("yo")], [])
+    for k in range(8):
+        dma("y" if k % 2 else "s", "dol", lambda k=k: (T.ol[k:k + 1, :], T.ew[16 * k:16 * k + 1, C:C + H]), [A("ew")], [])
+    ends = {}
+    for o in ops:
+        if o["lane"] in ("dol", "doc", "dy", "sent"):
+            ends[o["lane"]] = o
+    rec("y", None, [], [], lane="none", after=list(ends.values()))
+    emit(ops, g, T)

@@ -6,8 +6,8 @@ W16 = C // 16
 NS = W16 - 1
 TW = C + C + 32
 DP = 4 * (C + H)
-SC_B, SC_A = 12, 15
-SORT_AT, SEARCH_AT = 2, 10
+SC_B, SC_A = 10, 13
+SORT_AT, SEARCH_AT = 2, 12
 HOLD, DROP = 1024.0, -4096.0
 F32, BF, I32, U16, X4, U8 = "float32", "bfloat16", "int32", "uint16", "float8_e4m3fn_x4", "uint8"
 
@@ -21,7 +21,7 @@ _SB = {
     "k0": (TW, BF), "k27": (W16 * NS, BF),
     "ka": (J, BF), "kb": (J, BF), "iot": (J, F32), "jf": (C, F32), "jw": (W16, F32), "j4": (112, F32),
     "msk": (C, F32), "ha": (C, F32), "hb": (C, F32), "eq": (C, BF), "ea": (C, BF), "eb": (C, BF),
-    "fl": (3 * C, BF), "ca": (W16 * H, BF), "cb": (W16 * H, BF), "sg": (2 * C, BF), "lha": (96, F32), "lhb": (96, F32),
+    "fl": (4 * C, BF), "ca": (W16 * H, BF), "cb": (W16 * H, BF), "sg": (3 * C, BF), "lha": (96, F32), "lhb": (96, F32),
     "t1": (112, F32), "t2": (112, F32), "ii": (256, I32), "l1": (56, U16), "l2": (84, U16), "rs": (64, F32),
     "tb": (C, F32), "zp": (C + 32, F32), "zt": (TW, F32), "fp": (C + 32, BF), "ft": (TW, BF), "fs": (TW, BF),
     "f1": (W16 * NS, BF), "s1": (W16 * NS, BF),
@@ -37,7 +37,7 @@ for _t in range(R):
 SCRATCH = {k: ("sbuf", [128, n], d) for k, (n, d) in _SB.items()}
 SCRATCH["ps"] = ("psum", [128, 4096], F32)
 SEMAPHORES = ["cp", "cv", "cs", "cg", "sent", "dx", "du", "dv", "dl", "dol", "doc", "dy"] + \
-    ["m%d_%d" % (m, t) for m in range(4) for t in range(R)]
+    ["m%d_%d" % (m, t) for m in range(5) for t in range(R)]
 
 ADD, SUB, MUL, MAX, MIN = AluOpType.add, AluOpType.subtract, AluOpType.mult, AluOpType.max, AluOpType.min
 GE, GT, EQ, NE, LT = AluOpType.is_ge, AluOpType.is_gt, AluOpType.is_equal, AluOpType.not_equal, AluOpType.is_lt
@@ -254,12 +254,16 @@ def rank_program(g, core, T, topo):
     tt(col(X1), col(ODD), col(PAR), NE)
     tt(col(X2), col(ODD), col(PAR), GT)
     ts(col(X3), col(QHALF), 32.0, MUL, 15.0, ADD)
-    quant(A("qu"), A("su"), A("ub"))
     ts(A("md"), A("r16", 16, 16 + C), col(Q), EQ)
     ts(A("kz"), A("r16", 16, 16 + C), col(Q), NE)
+    quant(A("qu"), A("su"), A("ub"))
+    ts(A("ka"), A("r16", 16, 16 + J), col(Q), EQ, DROP, MUL)
     rec("v", lambda q: q.tensor_copy(ap(A("qur")).bitcast(dt.uint32), ap(A("qu")).bitcast(dt.uint32).indirect(ap(A("upk")))),
         [A("qu"), A("upk")], [A("qur")])
     rec("s", lambda q: q.activation(ap(A("sur")), ap(IND(A("su"), A("upk"))), FN.Copy), [A("su"), A("upk")], [A("sur")])
+    act(A("k0"), A("r16", 0, TW), FN.Sign)
+    act(A("jf"), A("iot", 0, C), FN.Copy, scale=1.0 / 2048)
+    ts(A("k16"), A("r16", 15, 15 + J), col(Q), EQ, HOLD, MUL)
 
     def late_constants():
         rec("g", lambda q: q.affine_select(ap(A("idn")), ap(A("one")), [[-1, 128]], EQ, 0.0, 0, 1), [A("one")], [A("idn")])
@@ -276,14 +280,10 @@ def rank_program(g, core, T, topo):
         yield
         ts(A("t1", 0, 2), A("iot", 0, 512, 256), col(X1), ADD, float(TW - 1), MIN)
         ts(col(BC), col(H4), 8192.0, MUL, col(X3), SUB)
-        ts(A("ka"), A("r16", 16, 16 + J), col(Q), EQ, DROP, MUL)
         yield
         copy(A("cl"), A("t1", 0, 2))
-        ts(A("k16"), A("r16", 15, 15 + J), col(Q), EQ, HOLD, MUL)
-        yield
         ts(A("jw"), A("iot", 0, C, 16), col(QH), ADD)
         ts(A("j4"), A("iot", 0, C, 4), col(RH), ADD)
-        ts(A("k0"), A("r16", 0, TW), 1.0, MIN)
         yield
         tt(A("k16"), A("k16"), A("ka"), ADD)
         for b in range(4):
@@ -295,7 +295,6 @@ def rank_program(g, core, T, topo):
         yield
         tt(A("k4"), A("k4"), A("ka", 0, C), ADD)
         quant(A("qv"), A("sv"), A("vb"))
-        ts(A("jf"), A("iot", 0, C), 1.0 / 2048, MUL)
         yield
         ts(A("k27"), A("kb", 0, W16 * NS), 1.0, MIN)
         yield
@@ -319,7 +318,7 @@ def rank_program(g, core, T, topo):
     def vector_counts(src, h, out, blocks, side):
         last = None
         for n, c in enumerate(list(range(blocks)) + [None]):
-            f = C * (n % 3)
+            f = C * (n % 4)
             if c is not None:
                 cut, own = 16 * c + 16, A(h, 16 * c + 15, 16 * c + 16)
                 ts(A("fl", f, f + cut), (src[0], src[1], src[1] + cut, 1), own, GE, 0.5, SUB)
@@ -335,7 +334,7 @@ def rank_program(g, core, T, topo):
     def scalar_counts(src, h, lh, blocks):
         last = None
         for n, c in enumerate(list(range(W16 - blocks, W16)) + [None]):
-            f = C * (n % 2)
+            f = C * (n % 3)
             if c is not None:
                 act(half("sg", f), src, FN.Sign, bias=A(h, 16 * c + 15, 16 * c + 16), scale=-1.0)
             if last is not None:
@@ -373,6 +372,9 @@ def rank_program(g, core, T, topo):
         for b in range(4):
             act(A("dw", at + b, at + 4 * C, 4), PS(4 + b), FN.Copy, scale=0.5)
 
+    def numbered(a):
+        scan(half("mm", a), half("cum", a), half("red", a), 0.0, MAX, MUL)
+
     quant(A("qt0"), A("st0"), A("x0"))
     for t in range(R):
         peer_rank = rank ^ STEP[t]
@@ -409,6 +411,7 @@ def rank_program(g, core, T, topo):
         def search():
             for c in range(W16):
                 ts(A("f1", NS * c, NS * c + NS), A(zp, W16, W16 + NS), A("hb", 16 * c + 15, 16 * c + 16), before)
+            yield
             scan(A("s1"), A("k27"), A("f1"), 0.0, MUL, ADD)
             yield
             copy(A("l2", 0, W16), A("s1", NS - 1, W16 * NS, NS))
@@ -416,6 +419,7 @@ def rank_program(g, core, T, topo):
             yield
             tt(half("fp", 16), IND(A(zp, 0, W16), A("l2", 0, W16)), A("tb"), before)
             tt(A("rs", 32, 32 + W16), A("t2", 0, W16), A("rs", 0, W16), ADD)
+            yield
             turn(half("ft", 0), half("fp", 16))
             turn(A("ft", C, TW), A("fp"))
             yield
@@ -440,17 +444,21 @@ def rank_program(g, core, T, topo):
         unpack(A("qtp%d" % t), A("stp%d" % t), DP)
 
         run(places("ca", "lha", SC_A, "ea"))
-        ts(A("l1", 0, W16), A("t1", 0, W16), float(H), ADD)
         ts(I(0, W16), A("t1", 0, W16), float(H), ADD)
+        ts(A("l1", 0, W16), A("t1", 0, W16), float(H), ADD)
+        ts(I(128, W16), I(0, W16), 1, AND)
         copy(IND(half("inv", 0), A("l1", 0, W16)), half("iot", 0))
-        n = 3 * W16
-        copy(I(2 * W16, W16), A(rbp))
-        ts(I(128, n), I(0, n), 1, AND)
-        ts(A("t1", 0, n), I(128, n), -2.0, MUL, 1.0, ADD)
-        tt(A("t2", 0, n), A("t1", 0, n), I(0, n), ADD)
-        copy(A("l2"), A("t2", 0, n))
+        n = 2 * W16
+        ts(A("t1", 0, W16), I(128, W16), -2.0, MUL, 1.0, ADD)
+        copy(I(n, W16), A(rbp))
+        tt(A("t2", 0, W16), A("t1", 0, W16), I(0, W16), ADD)
+        ts(I(128 + W16, n), I(W16, n), 1, AND)
+        copy(A("l2", 0, W16), A("t2", 0, W16))
+        ts(A("t1", W16, W16 + n), I(128 + W16, n), -2.0, MUL, 1.0, ADD)
         copy(A("am"), IND(half("inv", 0), A("l2", 0, W16)))
+        tt(A("t2", W16, W16 + n), A("t1", W16, W16 + n), I(W16, n), ADD)
         scan(half("scn", 0), half("k16", 0), A("am"), 0.0, ADD, MAX)
+        copy(A("l2", W16, W16 + n), A("t2", W16, W16 + n))
         ts(A(aml), A("scn", 15, C, 16), col(H16), SUB)
         exchange(peer, 1, t, ["aml"])
 
@@ -460,6 +468,9 @@ def rank_program(g, core, T, topo):
         copy(half("bm", me), IND(A("inv"), A("l2", W16, 2 * W16)))
         act(half("j0", other), IND(half("bm", other), A(amp)), FN.Copy)
         copy(half("j0", me), IND(half("bm", me), A(aml)))
+        act(A("vp"), IND(half("iot", 0), A(amp)), FN.Copy)
+        rec("g", lambda q: q.dma_start(ap(A("vp")), ap(A("jf")), accum_op=ADD), [A("jf")], [A("vp")],
+            lane="m4_%d" % t, dma=True, add=16)
 
         low = "iot"
         for k in range(9):
@@ -475,18 +486,15 @@ def rank_program(g, core, T, topo):
                 for a in (other, me):
                     tt(half(nxt, a), IND(A(low), A("pk", pk + a // 16, pk + a // 16 + W16)), half("wd", a), MIN)
                     act(half("wd", a), half(nxt, a), FN.Copy)
-            if k == 0:
-                tt(A("vp"), IND(half("iot", 0), A(amp)), A("jf"), ADD)
             low = nxt
 
         tt(half("red", 0), IND(half(low, other), A(amp)), half("wd", other), GT)
         scan(half("cum", 0), half("red", 0), half("red", 0), float(C - 1), ADD, MAX)
-        tt(half("mm", 0), half("cum", 0), half("red", 0), MUL)
+        tt(half("red", C), IND(half(low, me), A(aml)), half("wd", me), GT)
+        numbered(0)
         scan(half("scn", 0), half("k16", 0), half("mm", 0), 0.0, ADD, MAX)
         tt(A("t1", 0, W16), A("scn", 15, C, 16), A("jw"), MAX)
-        tt(half("red", C), IND(half(low, me), A(aml)), half("wd", me), GT)
         ts(A("l1", 0, W16), A("t1", 0, W16), col(H16), SUB)
-        scan(half("cum", C), half("red", C), half("red", C), float(C - 1), ADD, MAX)
         copy(IND(A("ew"), A("l1", 0, W16)), A("vp"))
         scan(A("scn", 0, H), A("k4", 0, H), A("ew", C, C + H), 0.0, ADD, MAX)
         ts(I(0, 56), A("scn", 3, H, 4), 8192.0, MUL, col(BC), SUB)
@@ -496,38 +504,43 @@ def rank_program(g, core, T, topo):
         theirs = A("dw", DP, DP + 4 * C)
         for h in range(2):
             act(half("bh", C * h), IND(theirs, A("lb", W16 * h, W16 * h + W16)), FN.Copy)
-        tt(half("mm", C), half("cum", C), half("red", C), MUL)
+        scan(half("cum", C), half("red", C), half("red", C), float(C - 1), ADD, MAX)
+        numbered(C)
         for h in range(2):
             tt(half("bt", C * h), IND(theirs, A("lb", 56 + W16 * h, 56 + W16 * h + W16)), half("bh", C * h), ADD)
         quant(A("qb"), A("sq"), A("bt"))
         for b in range(4):
             mm(PS(b, H), *stat("e", b), A("qb"), A("sq"))
         scan(half("scn", 0), A("k4"), half("mm", C), 0.0, ADD, MAX)
+        if t == R - 1:
+            scan(half("scn", C), half("k16", 0), half("mm", C), 0.0, ADD, MAX)
         tt(A("t1"), A("scn", 3, C, 4), A("j4"), MAX)
+        if t == R - 1:
+            tt(A("t2", 0, W16), A("scn", C + 15, J, 16), A("jw"), MAX)
         for b in range(4):
             out = A("dw", 4 * C + b, DP, 4)
-            if b == 3:
-                ts(A("ly"), A("t1"), 4.0, MUL, col(YC), SUB)
+            if b == 2:
                 ts(out, PS(b, H), 0.5, MUL)
+                ts(A("ly"), A("t1"), 4.0, MUL, col(YC), SUB)
             else:
                 act(out, PS(b, H), FN.Copy, scale=0.5)
         act(A("yt", J, 2 * J), IND(A("dw", 0, DP), A("ly", 56, 112)), FN.Copy, scale=2.0)
         ts(A("yt", 0, J), IND(A("dw", 0, DP), A("ly", 0, 56)), 2.0, MUL)
+        if t == R - 1:
+            ts(A("l1", 0, W16), A("t2", 0, W16), col(H16), SUB)
 
         quant(A("qz"), A("sz"), A("yt"))
         for b in range(4):
             mm(PS(4 + b), *stat("w", b), A("qz"), A("sz"))
             mm(PS(b), *stat("e", b), A("qz"), A("sz"))
         if t == R - 1:
-            scan(half("scn", 0), half("k16", 0), half("mm", C), 0.0, ADD, MAX)
+            copy(IND(A("ew"), A("l1", 0, W16)), half("iot", 0))
+            for k in range(8):
+                dma("y", "dol", lambda k=k: (T.ol[k:k + 1, :], T.ew[16 * k:16 * k + 1, C:C + H]), [A("ew")], [])
         for b in range(4):
             rl = half("rl", C * (b % 2))
             act(rl, PS(4 + b), FN.Relu, scale=0.03125)
             tt(A("xt", b, 4 * C, 4), PS(b), rl, ADD)
-            if t == R - 1 and b == 0:
-                tt(A("t1", 0, W16), A("scn", 15, C, 16), A("jw"), MAX)
-            if t == R - 1 and b == 1:
-                ts(A("l1", 0, W16), A("t1", 0, W16), col(H16), SUB)
         quant(A("qt%d" % (t + 1)), A("st%d" % (t + 1)), A("xt"))
 
     QT = (A("qt%d" % R), A("st%d" % R))
@@ -535,11 +548,8 @@ def rank_program(g, core, T, topo):
     dma("y", "doc", lambda: (T.oc[:], u8(QT[0])), [QT[0]], [])
     for k in range(4):
         dma("y", "doc", lambda k=k: (T.osc[4 * k:4 * k + 4, :], T["st%d" % R][32 * k:32 * k + 4, :]), [QT[1]], [])
-    copy(IND(A("ew"), A("l1", 0, W16)), half("iot", 0))
-    act(A("yo"), PS(4), FN.Copy)
+    copy(A("yo"), PS(4))
     dma("s", "dy", lambda: (T.y[:], ap(A("yo"))), [A("yo")], [])
-    for k in range(8):
-        dma("y" if k % 2 else "s", "dol", lambda k=k: (T.ol[k:k + 1, :], T.ew[16 * k:16 * k + 1, C:C + H]), [A("ew")], [])
     ends = {}
     for o in ops:
         if o["lane"] in ("dol", "doc", "dy", "sent"):

@@ -3,12 +3,18 @@ from concourse.mybir import dt, AluOpType, ActivationFunctionType
 C, H, J, R = 448, 224, 896, 3
 STEP = [1, 2, 1]
 W16 = C // 16
-NS = W16 - 1
+RUN = W16 // 2
+NS = 3 * RUN
+ZP = 48
+ULP, TINY, FARTHEST = 0.6 * 2.0 ** -23, 2.0 ** -124, 2.0 ** 96
 TW = C + C + 32
 DP = 4 * (C + H)
-SC_B, SC_A = 10, 13
-SORT_AT, SEARCH_AT = 2, 12
-HOLD, DROP = 1024.0, -4096.0
+SC_B, SC_A = 11, (19, 18, 18)
+SORT_EVERY, SEARCH_AT, SEARCH_EVERY = 3, 5, 4
+WW = 16 + C + 16 + C + 32
+STEPS = 8
+BIG = 65536.0
+LO, HL, HU, EN, JH, JL, PL, EH, EL, EV = range(10)
 F32, BF, I32, U16, X4, U8 = "float32", "bfloat16", "int32", "uint16", "float8_e4m3fn_x4", "uint8"
 
 _SB = {
@@ -16,22 +22,29 @@ _SB = {
     "qu": (128, X4), "su": (128, U8), "qur": (256, X4), "sur": (256, U8), "qv": (128, X4), "sv": (128, U8),
     "qw": (512, X4), "sw": (512, U8), "qe": (512, X4), "se": (512, U8), "et": (2048, BF), "one": (128, BF), "idn": (128, BF),
     "qz": (C, X4), "sz": (C, U8), "qb": (H, X4), "sq": (H, U8), "qt%d" % R: (C, X4), "st%d" % R: (C, U8),
-    "pi": (16, I32), "cf": (32, F32), "upi": (16, I32), "upk": (16, U16), "cl": (2, U16),
-    "r16": (TW + 16, BF), "r4": (C + 4, BF), "md": (C, BF), "kz": (C, BF), "k16": (J, BF), "k4": (C, BF),
-    "k0": (TW, BF), "k27": (W16 * NS, BF),
-    "ka": (J, BF), "kb": (J, BF), "iot": (J, F32), "jf": (C, F32), "jw": (W16, F32), "j4": (112, F32),
+    "pi": (16, I32), "cf": (32, F32), "upi": (16, I32), "upk": (16, U16),
+    "r16": (C + 16, BF), "md": (C, BF), "kz": (C, BF), "k0": (TW, BF), "k27": (W16 * NS, BF), "kb": (W16 * NS, BF),
+    "iot": (512, F32), "sm": (192, F32), "tab": (J, BF), "cc": (J, BF),
     "msk": (C, F32), "ha": (C, F32), "hb": (C, F32), "eq": (C, BF), "ea": (C, BF), "eb": (C, BF),
     "fl": (4 * C, BF), "ca": (W16 * H, BF), "cb": (W16 * H, BF), "sg": (3 * C, BF), "lha": (96, F32), "lhb": (96, F32),
-    "t1": (112, F32), "t2": (112, F32), "ii": (256, I32), "l1": (56, U16), "l2": (84, U16), "rs": (64, F32),
-    "tb": (C, F32), "zp": (C + 32, F32), "zt": (TW, F32), "fp": (C + 32, BF), "ft": (TW, BF), "fs": (TW, BF),
-    "f1": (W16 * NS, BF), "s1": (W16 * NS, BF),
-    "inv": (J, F32), "bm": (J, F32), "am": (C, F32), "vp": (C, F32), "scn": (J, F32), "j0": (J, F32), "j1": (J, F32),
-    "w0": (J, F32), "w1": (J, F32), "wd": (J, F32), "pk": (112, U16), "red": (J, F32), "cum": (J, F32), "mm": (J, F32),
-    "ew": (C + H, F32), "lb": (112, U16), "ly": (112, U16), "dw": (DP + 4 * C, BF), "bh": (4 * H, F32),
-    "rl": (2 * C, F32), "yo": (C, F32),
+    "ii": (128, I32), "tb": (C, F32), "zp": (C + 32, F32), "zt": (TW, F32), "fp": (C + 32, BF), "ft": (TW, BF), "fs": (TW, BF),
+    "f1": (W16 * NS, BF), "s1": (W16 * NS, BF), "fq": (3 * C, BF),
+    "r1": (C, BF), "r2": (C, BF), "inv": (C, BF), "w9": (J, BF), "x9": (J, BF), "x2": (C, BF), "xx": (1024, BF),
+    "w0": (WW, BF), "w1": (WW, BF), "wd": (C, BF),
+    "red": (C, BF), "cum": (C, BF), "mm": (C + 32, BF), "ew": (C + H + 32, BF), "x3": (C, BF), "eo": (C + H, F32),
+    "dw": (DP + 4 * C, BF), "bh": (4 * H, F32), "rl": (4 * C, F32), "yo": (C, F32),
 }
+_PART = {}
+for _b, _d, _names in (("sf", F32, "rs64 sp64 sq64 sr88 sb88 yy64 kw64 ka64 kr64 cs64 ff128 t164 t264 jw32"),
+                       ("lu", U16, "cl2 se16 l132 l284 lw32 lp32 la32 lx32 lv32 lb32 ly32 pk64")):
+    _at = 0
+    for _x in _names.split():
+        _PART[_x[:2] + "_"] = (_b, _at, int(_x[2:]))
+        _at += int(_x[2:])
+    _SB[_b] = (_at, _d)
 for _t in range(R):
-    for _n, _w, _d in (("z", 64, F32), ("rb", W16, U16), ("aml", W16, U16), ("qt", C, X4), ("st", C, U8)):
+    _SB["z%d" % _t] = (96, F32)
+    for _n, _w, _d in (("rb", 32, U16), ("pa", 32, U16), ("rr", 32, U16), ("qt", C, X4), ("st", C, U8)):
         _SB["%s%d" % (_n, _t)] = (_w, _d)
         _SB["%sp%d" % (_n, _t)] = (_w, _d)
 SCRATCH = {k: ("sbuf", [128, n], d) for k, (n, d) in _SB.items()}
@@ -46,6 +59,9 @@ FN = ActivationFunctionType
 
 
 def A(name, a=0, b=None, s=1):
+    if name in _PART:
+        buf, at, n = _PART[name]
+        return (buf, at + a, at + (n if b is None else b), s)
     return (name, a, _SB[name][0] if b is None else b, s)
 
 
@@ -187,7 +203,7 @@ def rank_program(g, core, T, topo):
 
     def act(out, in_, fn, bias=0.0, scale=1.0, acc=None):
         if acc is None:
-            return rec("s", lambda q: q.activation(ap(out), ap(in_), fn, bias=ap(bias), scale=scale), [in_, bias], [out])
+            return rec("s", lambda q: q.activation(ap(out), ap(in_), fn, bias=ap(bias), scale=ap(scale)), [in_, bias, scale], [out])
         return rec("s", lambda q: q.activation(ap(out), ap(in_), fn, bias=ap(bias), scale=scale, accum_out=ap(acc)),
                    [in_, bias], [out, acc])
 
@@ -209,12 +225,12 @@ def rank_program(g, core, T, topo):
         rid, pid, _ = topo.addr(peer)
         mask, n = topo.mask(core, peer), len(topo.engines(core, peer))
         sem = "m%d_%d" % (m, t)
-        for name in names:
-            src, dst = A("%s%d" % (name, t), 0, width), A("%sp%d" % (name, t), 0, width)
+        pairs = [x if width is None and len(x[0]) == 4 else (A("%s%d" % (x, t), 0, width), A("%sp%d" % (x, t), 0, width))
+                 for x in names]
+        for src, dst in pairs:
             rec("g", lambda q, src=src, dst=dst: q.remote_dma(u8(dst), u8(src), T.sem[sem], T.sem.sent, pid, rid, mask),
                 [src], [], lane="sent", add=n)
-        rec(None, None, [], [A("%sp%d" % (name, t), 0, width) for name in names], lane=sem,
-            add=len(topo.engines(peer, core)) * len(names))
+        rec(None, None, [], [dst for _, dst in pairs], lane=sem, add=len(topo.engines(peer, core)) * len(names))
 
     def col(k):
         return A("cf", k, k + 1)
@@ -225,78 +241,140 @@ def rank_program(g, core, T, topo):
     def half(name, a):
         return A(name, a, a + C)
 
+    def t1(a, n):
+        return A("t1_", a, a + n)
+
+    def t2(a, n):
+        return A("t2_", a, a + n)
+
     dma("y", "dx", lambda: (ap(A("x0")), T.x[:]), [], [A("x0")])
     dma("s", "du", lambda: (ap(A("ub")), T.u[:]), [], [A("ub")])
     dma("y", "dv", lambda: (ap(A("vb")), T.v[:]), [A("x0")], [A("vb")])
     dma("y", "dl", lambda: (u8(A("qw")), T.wc[:]), [], [A("qw")])
     dma("y", "dl", lambda: (ap(A("sw")), T.ws[:]), [], [A("sw")])
 
-    Q, TT, RR, PAR, ODD, QHALF, H16, H4, QH, RH, YC, BC, X1, X2, X3 = range(15)
+    ups = [1 if rank & STEP[t] else 0 for t in range(R)]
+    Q, P32, PAR, ODD, QHALF, KEEP, FAR, X1, X2, X3, X5, X6 = range(12)
+    SD, SM, SH, SK, SS = 0, 2, 4, 6, 8
+
+    def sel(k, up=0):
+        k += 6 * up
+        return A("se_", k, k + 2)
+
     iota(A("pi", 0, 1), [[1, 1]], 0, 1)
     iota(A("upi"), [[-8, 2], [16, 8]], 8, 0)
-    iota(A("r16"), [[0, TW // 16 + 1], [1, 16]], 0, 0)
+    iota(A("r16", 0, C + 16), [[0, W16 + 1], [1, 16]], 0, 0)
     fill(A("one"), 1.0)
-    fill(A("et"), 0.0)
-    for name in ("lha", "lhb", "rs", "zp", "fp"):
+    for name in ("lha", "lhb"):
         fill(A(name), 0.0)
     p = A("pi", 0, 1)
     ts(A("pi", 1, 2), p, 15, AND)
-    ts(A("pi", 2, 3), p, 3, AND)
-    ts(A("pi", 3, 4), p, 2, SHR, 3, AND)
-    ts(A("pi", 4, 5), p, 4, SHR, 1, AND)
-    ts(A("pi", 5, 6), p, 1, AND)
-    ts(A("pi", 6, 7), p, 1, SHR, 7, AND)
+    ts(A("pi", 2, 3), p, 31, AND)
+    ts(A("pi", 3, 4), p, 4, SHR, 1, AND)
+    ts(A("pi", 4, 5), p, 1, AND)
+    ts(A("pi", 5, 6), p, 1, SHR, 7, AND)
     copy(A("upk"), A("upi"))
-    copy(A("cf", 0, 6), A("pi", 1, 7))
-    iota(A("iot"), [[1, J]], 0, 0)
-    ts(col(H16), col(Q), 15.0, LT, HOLD, MUL)
-    ts(col(H4), col(RR), 3.0, LT, HOLD, MUL)
+    copy(A("cf", 0, 5), A("pi", 1, 6))
+    iota(A("iot"), [[1, 512]], 0, 0)
     tt(col(X1), col(ODD), col(PAR), NE)
     tt(col(X2), col(ODD), col(PAR), GT)
     ts(col(X3), col(QHALF), 32.0, MUL, 15.0, ADD)
     ts(A("md"), A("r16", 16, 16 + C), col(Q), EQ)
     ts(A("kz"), A("r16", 16, 16 + C), col(Q), NE)
     quant(A("qu"), A("su"), A("ub"))
-    ts(A("ka"), A("r16", 16, 16 + J), col(Q), EQ, DROP, MUL)
     rec("v", lambda q: q.tensor_copy(ap(A("qur")).bitcast(dt.uint32), ap(A("qu")).bitcast(dt.uint32).indirect(ap(A("upk")))),
         [A("qu"), A("upk")], [A("qur")])
     rec("s", lambda q: q.activation(ap(A("sur")), ap(IND(A("su"), A("upk"))), FN.Copy), [A("su"), A("upk")], [A("sur")])
-    act(A("k0"), A("r16", 0, TW), FN.Sign)
-    act(A("jf"), A("iot", 0, C), FN.Copy, scale=1.0 / 2048)
-    ts(A("k16"), A("r16", 15, 15 + J), col(Q), EQ, HOLD, MUL)
+    for a in (0, C + 16):
+        act(A("k0", a, a + C + 16), A("r16"), FN.Sign)
+    fill(("sf", _PART["yy_"][1], _PART["jw_"][1], 1), 0.0)
+
+    def zeros(*views):
+        for v in views:
+            iota(v, [[0, v[2] - v[1]]], 0, 0)
+
+    def later_constants():
+        zeros(A("et"))
+        for b in range(4):
+            out = A("et", 512 * b + b, 512 * (b + 1), 4)
+            rec("g", lambda q, out=out: q.affine_select(ap(out), ap(A("one")), [[-1, 128]], EQ, 0.0, 0, 1), [A("one")], [out])
+        zeros(A("x2"), A("xx"), A("mm"), A("ew", C - 16), *[A(w, a, a + 16) for w in ("w0", "w1") for a in (0, C + 16)])
+
+    def side_lists(up):
+        ts(col(X1), col(PAR), float(up), NE, 32.0, MUL)
+        ts(col(X2), col(ODD), float(up), NE, 14.0, MUL)
+        ts(col(X3), col(PAR), float(up), EQ)
+        ts(col(X5), col(PAR), float(up), NE)
+        yield
+        ts(sel(SH, up), A("jw_", 0, 2), col(X1), ADD)
+        tt(col(X2), col(X2), col(ODD), SUB)
+        ts(A("sm", 2, 4), A("jw_", 0, 2), 64.0, ADD, col(X5), MUL)
+        yield
+        ts(sel(SK, up), A("sm", 0, 2), col(X2), ADD, float(1 - up), ADD)
+        ts(A("sm", 4, 6), A("sm", 0, 2), col(X2), ADD, float(up), ADD)
+        yield
+        ts(A("sm", 6, 8), A("sm", 4, 6), col(X3), MUL)
+        yield
+        tt(A("sm", 4, 6), A("sm", 6, 8), A("sm", 2, 4), ADD)
+        yield
+        copy(sel(SS, up), A("sm", 4, 6))
 
     def late_constants():
-        rec("g", lambda q: q.affine_select(ap(A("idn")), ap(A("one")), [[-1, 128]], EQ, 0.0, 0, 1), [A("one")], [A("idn")])
-        iota(A("r4"), [[0, C // 4 + 1], [1, 4]], 0, 0)
-        iota(A("kb", 0, W16 * NS), [[0, W16], [1, NS]], 0, 0)
+        iota(A("sm", 112, 140), [[32, 14], [C, 2]], -C, 0)
+        zeros(A("w9"), A("x9"))
+        iota(A("w9", HL, J, 16), [[32, 14], [-C - 48, 2], [0, 2]], C + 48, 0)
+        iota(A("w9", HU, J, 16), [[32, 14], [C + 16, 2], [0, 2]], 0, 0)
+        iota(A("w9", EV, J, 16), [[0, 14], [1, 2], [0, 2]], 0, 0)
+        for a, hi in ((0, JH), (C, EH)):
+            iota(A("x9", a + hi, a + C, 16), [[32, 14], [0, 2]], 0, 0)
+        zeros(A("rs_", 48, 64), A("zp", 0, 16), A("zp", C + 16), A("fp", 0, 16), A("fp", C + 16))
+        iota(A("sb_", 0, 84), [[RUN, 2], [0, RUN], [RUN, 3]], 2, 0)
+        zeros(*[A("z%d" % t, a, a + 8) for t in range(R) for a in (32, 88)])
+        iota(A("kb"), [[0, 3 * W16], [1, RUN]], 0, 0)
         ts(col(X1), col(X1), float(C), MUL, col(X3), ADD)
         ts(col(X2), col(X2), 2.0, MUL, col(PAR), ADD)
-        tt(col(QH), col(Q), col(H16), ADD)
-        tt(col(RH), col(RR), col(H4), ADD)
+        ts(A("jw_"), A("iot", 0, 512, 16), col(Q), ADD)
+        ts(col(X5), col(ODD), -31.0, MUL, 47.0, ADD)
+        ts(col(X6), col(ODD), 16.0, MUL, col(QHALF), ADD)
         yield
         ts(col(X1), col(X2), 16.0, MUL, col(X1), ADD)
-        ts(col(YC), col(H4), 4.0, MUL, col(TT), SUB)
-        ts(col(X3), col(TT), 2049.0, MUL)
+        ts(col(X5), col(X5), col(PAR), MUL, col(X6), ADD)
+        ts(col(X3), col(PAR), -1008.0, MUL, 16.0 + EV, ADD)
+        ts(t2(0, 2), A("jw_", 0, 2), 14.0, GE, 18.0, MUL)
         yield
-        ts(A("t1", 0, 2), A("iot", 0, 512, 256), col(X1), ADD, float(TW - 1), MIN)
-        ts(col(BC), col(H4), 8192.0, MUL, col(X3), SUB)
+        ts(t1(0, 2), A("iot", 0, 512, 256), col(X1), ADD, float(TW - 1), MIN)
+        ts(t1(2, 2), A("iot", 0, 16, 8), col(X5), ADD)
+        tt(A("sm", 0, 2), t2(0, 2), A("jw_", 0, 2), ADD)
+        ts(col(KEEP), col(Q), float(EN), EQ)
+        ts(col(X2), col(Q), float(PL), EQ)
         yield
-        copy(A("cl"), A("t1", 0, 2))
-        ts(A("jw"), A("iot", 0, C, 16), col(QH), ADD)
-        ts(A("j4"), A("iot", 0, C, 4), col(RH), ADD)
+        copy(A("cl_"), t1(0, 2))
+        copy(sel(SD), t1(2, 2))
+        ts(sel(SM), t1(2, 2), 32.0, MUL, col(X3), ADD)
+        tt(col(KEEP), col(KEEP), col(X2), ADD)
         yield
-        tt(A("k16"), A("k16"), A("ka"), ADD)
-        for b in range(4):
-            copy(A("et", 512 * b + b, 512 * (b + 1), 4), A("idn"))
+        ts(col(FAR), col(KEEP), -BIG, MUL, BIG, ADD)
         yield
-        ts(A("ka", 0, C), A("r4", 4, 4 + C), col(RR), EQ, DROP, MUL)
-        ts(A("k4"), A("r4", 3, 3 + C), col(RR), EQ, HOLD, MUL)
-        quant(A("qe"), A("se"), A("et"))
+        for _ in side_lists(ups[0]):
+            yield
+        ts(A("w9", LO, J, 16), A("iot", 0, 56), 0.0, MUL, col(P32), ADD)
+        ts(A("sm", 112, 140), A("sm", 112, 140), col(P32), ADD)
         yield
-        tt(A("k4"), A("k4"), A("ka", 0, C), ADD)
-        quant(A("qv"), A("sv"), A("vb"))
+        turn(A("tab"), A("w9"))
+        y = A("sm", 112, 140)
+        ts(t1(0, W16), y, -256.0, MAX, 256.0, MIN)
+        ts(t1(32, W16), y, -384.0, MAX, 384.0, MIN)
+        ts(t2(32, W16), y, 4.0, MUL)
+        for a, lo in ((0, JL), (C, EL)):
+            ts(A("x9", a + lo, a + C, 16), A("iot", 0, W16), 0.0, MUL, col(P32), ADD)
         yield
-        ts(A("k27"), A("kb", 0, W16 * NS), 1.0, MIN)
+        tt(t1(0, W16), t1(0, W16), t1(32, W16), ADD)
+        tt(t2(32, W16), t2(32, W16), t1(32, W16), SUB)
+        yield
+        tt(A("x9", EN, C, 16), t2(32, W16), t1(0, W16), SUB)
+        ts(A("k27"), A("kb"), 1.0, MIN)
+        yield
+        turn(A("cc"), A("x9"))
         yield
 
     def stat(name, b):
@@ -315,43 +393,53 @@ def rank_program(g, core, T, topo):
         for _ in x:
             pass
 
-    def vector_counts(src, h, out, blocks, side):
-        last = None
+    def part(src, a, b):
+        return (src[0], src[1] + a, src[1] + b, 1)
+
+    def vector_counts(src, h, out, blocks, w):
+        last, m = None, w // 2
         for n, c in enumerate(list(range(blocks)) + [None]):
             f = C * (n % 4)
             if c is not None:
-                cut, own = 16 * c + 16, A(h, 16 * c + 15, 16 * c + 16)
-                ts(A("fl", f, f + cut), (src[0], src[1], src[1] + cut, 1), own, GE, 0.5, SUB)
-                ts(A("fl", f + cut, f + C), (src[0], src[1] + cut, src[2], 1), own, GT, 0.5, SUB)
-            next(side, None)
+                a, own = 16 * c // w * w, A(h, 16 * c + 15, 16 * c + 16)
+                cut = 16 * c + 16 - a
+                ts(A("fl", f, f + cut), part(src, a, a + cut), own, GE, 0.5, SUB)
+                if cut < w:
+                    ts(A("fl", f + cut, f + w), part(src, a + cut, a + w), own, GT, 0.5, SUB)
+            yield
             if last is not None:
-                scan(A(out, last[1] * H, last[1] * H + H), A("fl", last[0], last[0] + H), A("fl", last[0] + H, last[0] + C),
+                scan(A(out, last[1] * m, last[1] * m + m), A("fl", last[0], last[0] + m), A("fl", last[0] + m, last[0] + w),
                      0.0, ADD, ADD)
-                next(side, None)
+                yield
             last = (f, c)
-        run(side)
 
-    def scalar_counts(src, h, lh, blocks):
+    def weave(steps, filler, every):
+        for n, _ in enumerate(steps):
+            if n % every == every - 1:
+                next(filler, None)
+
+    def scalar_counts(src, h, lh, blocks, w):
         last = None
         for n, c in enumerate(list(range(W16 - blocks, W16)) + [None]):
             f = C * (n % 3)
             if c is not None:
-                act(half("sg", f), src, FN.Sign, bias=A(h, 16 * c + 15, 16 * c + 16), scale=-1.0)
+                a = 16 * c // w * w
+                act(A("sg", f, f + w), part(src, a, a + w), FN.Sign, bias=A(h, 16 * c + 15, 16 * c + 16), scale=-1.0)
             if last is not None:
-                a, cut = last[0], last[0] + 16 * last[1] + 16
+                a, cut = last[0], last[0] + (16 * last[1]) % w + 16
                 act(A("sg", a, cut), A("sg", a, cut), FN.Sign, bias=0.5, scale=-1.0, acc=A(lh, last[1], last[1] + 1))
-                if cut < a + C:
-                    act(A("sg", cut, a + C), A("sg", cut, a + C), FN.Sign, bias=-0.5, scale=-1.0,
+                if cut < a + w:
+                    act(A("sg", cut, a + w), A("sg", cut, a + w), FN.Sign, bias=-0.5, scale=-1.0,
                         acc=A(lh, 32 + last[1], 33 + last[1]))
             last = (f, c)
 
-    def places(counts, lh, blocks, equal):
-        a = W16 - blocks
+    def places(counts, lh, blocks, equal, w):
+        a, m = W16 - blocks, w // 2
         tt(A(lh, 64 + a, 64 + W16), A(lh, a, W16), A(lh, 32 + a, 32 + W16), ADD)
         yield
-        ts(A(counts, a * H + H - 1, W16 * H, H), A(lh, 64 + a, 64 + W16), 0.5, MUL)
+        ts(A(counts, a * m + m - 1, W16 * m, m), A(lh, 64 + a, 64 + W16), 0.5, MUL)
         yield
-        tt(A("t1", 0, W16), A(counts, H - 1, W16 * H, H), A(equal, 15, C, 16), SUB)
+        tt(t1(0, W16), A(counts, m - 1, W16 * m, m), A(equal, 15, C, 16), SUB)
         yield
 
     def own_scores(src, h):
@@ -366,23 +454,27 @@ def rank_program(g, core, T, topo):
         scan(A(out), A("kz"), A("eq"), 0.0, MUL, ADD)
         yield
 
-    def unpack(codes, scales, at):
+    def unpack(codes, scales, at, step):
         for b in range(4):
             mm(PS(4 + b), *stat("e", b), codes, scales)
-        for b in range(4):
-            act(A("dw", at + b, at + 4 * C, 4), PS(4 + b), FN.Copy, scale=0.5)
+            act(half("dw", at + step * b), PS(4 + b), FN.Copy, scale=0.5)
+            yield
 
-    def numbered(a):
-        scan(half("mm", a), half("cum", a), half("red", a), 0.0, MAX, MUL)
+    def cross(out, src, to):
+        turn(A("yy_", 16, 48), src)
+        yield
+        turn(out, A("yy_", 32 - 32 * to, 64 - 32 * to))
+        yield
+
+    def lane(h, l):
+        return A("xx", 16 + 16 * h + l, 16 + C, 32)
 
     quant(A("qt0"), A("st0"), A("x0"))
     for t in range(R):
-        peer_rank = rank ^ STEP[t]
-        peer = T.cores[peer_rank]
-        up = 1 if rank > peer_rank else 0
-        me, other = C * up, C * (1 - up)
+        peer = T.cores[rank ^ STEP[t]]
+        up = ups[t]
         before = GE if up else GT
-        z, zp, rb, rbp, aml, amp = ["%s%d" % (n, t) for n in ("z", "zp", "rb", "rbp", "aml", "amlp")]
+        z, rb, rbp, pa, pap, rr, rrp = ["%s%d" % (n, t) for n in ("z", "rb", "rbp", "pa", "pap", "rr", "rrp")]
         QT = (A("qt%d" % t), A("st%d" % t))
         SBV, SBS, SAV, SAS = PS(0), PS(1), PS(2), PS(3)
         exchange(peer, 3, t, ["qt", "st"])
@@ -392,155 +484,221 @@ def rank_program(g, core, T, topo):
         mm(SAS, *stat("ur", 1), *QT)
 
         def sort_b():
-            for _ in places("cb", "lhb", SC_B, "eb"):
+            for _ in places("cb", "lhb", SC_B, "eb", H):
                 yield
-            ts(A("l1", 0, W16), A("t1", 0, W16), float(H), ADD)
-            ts(A("rs", 0, W16), A("t1", 0, W16), float(H), ADD)
+            for r in range(2):
+                ts(A("l1_", RUN * r, RUN * r + RUN), t1(RUN * r, RUN), float(H // 2 + H * r), ADD)
+            ts(A("rs_", 0, W16), t1(0, W16), float(H // 2), ADD)
             yield
-            copy(IND(half("zp", 16), A("l1", 0, W16)), A("tb"))
+            copy(IND(half("zp", 16), A("l1_", 0, W16)), A("tb"))
             yield
             turn(half("zt", 0), half("zp", 16))
             turn(A("zt", C, TW), A("zp"))
             yield
-            copy(A(z, 0, 32), IND(A("zt"), A("cl")))
+            copy(A(z, 0, 32), IND(A("zt"), A("cl_")))
+            exchange(peer, 0, t, [(A(z, 0, W16), A(z, ZP, ZP + W16))])
             yield
-            copy(A(z, W16, W16 + NS), A("zp", 31, C, 16))
-            exchange(peer, 0, t, ["z"], W16 + NS)
+            moved, home = A(z, RUN * up, RUN * up + RUN), [ZP + W16, ZP - RUN]
+            ts(t2(0, RUN), moved, ULP, MUL, TINY, ADD)
+            ts(t2(16, RUN), moved, -ULP, MUL, TINY, ADD)
+            copy(A(z, home[1 - up], home[1 - up] + RUN), A(z, RUN * (1 - up), RUN * (2 - up)))
+            yield
+            tt(t2(32, RUN), t2(0, RUN), t2(16, RUN), MAX)
+            yield
+            tt(A(z, home[up], home[up] + RUN), moved, t2(32, RUN), SUB if up else ADD)
             yield
 
         def search():
+            turn(A("sp_", 0, 64), A(z, 32, 96))
+            yield
+            for k in range(4):
+                ts(A("sq_", 16 * k, 16 * k + 16), A("iot", 0, 16), 0.0, MUL, A("sp_", 16 * k + 15, 16 * k + 16), ADD)
+            yield
+            turn(A("sp_", 0, 64), A("sq_", 0, 64))
+            yield
+            fill(A("sp_", 1 + RUN, 64, RUN), -FARTHEST)
+            yield
             for c in range(W16):
-                ts(A("f1", NS * c, NS * c + NS), A(zp, W16, W16 + NS), A("hb", 16 * c + 15, 16 * c + 16), before)
+                a = 2 + c // RUN * RUN
+                ts(A("f1", NS * c, NS * c + NS), A("sp_", a, a + NS), A("hb", 16 * c + 15, 16 * c + 16), before)
             yield
             scan(A("s1"), A("k27"), A("f1"), 0.0, MUL, ADD)
             yield
-            copy(A("l2", 0, W16), A("s1", NS - 1, W16 * NS, NS))
-            ts(A("t2", 0, W16), A("s1", NS - 1, W16 * NS, NS), 16.0, MUL)
+            found = [A("s1", RUN * s + RUN - 1, W16 * NS, NS) for s in range(3)]
+            tt(A("sr_", 0, 84), A("s1", RUN - 1, W16 * NS, RUN), A("sb_", 0, 84), ADD)
+            tt(t2(0, W16), found[0], found[1], ADD)
             yield
-            tt(half("fp", 16), IND(A(zp, 0, W16), A("l2", 0, W16)), A("tb"), before)
-            tt(A("rs", 32, 32 + W16), A("t2", 0, W16), A("rs", 0, W16), ADD)
+            for s in range(3):
+                copy(A("l2_", W16 * s, W16 * s + W16), A("sr_", s, 84, 3))
+            tt(t2(0, W16), t2(0, W16), found[2], ADD)
+            yield
+            win = A(z, 32, 96)
+            tt(half("fq", 0), IND(win, A("l2_", 0, W16)), A("tb"), before)
+            ts(t2(0, W16), t2(0, W16), 16.0, MUL)
+            yield
+            tt(half("fq", C), IND(win, A("l2_", W16, 2 * W16)), A("tb"), before)
+            tt(A("rs_", 32, 32 + W16), t2(0, W16), A("rs_", 0, W16), ADD)
+            yield
+            tt(half("fq", 2 * C), IND(win, A("l2_", 2 * W16, 3 * W16)), A("tb"), before)
+            tt(half("fq", 0), half("fq", 0), half("fq", C), ADD)
+            yield
+            tt(half("fp", 16), half("fq", 0), half("fq", 2 * C), ADD)
             yield
             turn(half("ft", 0), half("fp", 16))
             turn(A("ft", C, TW), A("fp"))
             yield
             scan(A("fs"), A("k0"), A("ft"), 0.0, MUL, ADD)
             yield
-            tt(I(W16, 32), IND(A("fs"), A("cl")), A("rs", 32, 64), ADD)
+            tt(A("kw_", 0, 32), IND(A("fs"), A("cl_")), A("rs_", 32, 64), ADD)
             yield
-            copy(A(rb), I(W16, W16))
-            exchange(peer, 2, t, ["rb"])
+            for _ in cross(t2(0, 32), A("kw_", 0, 32), up):
+                yield
+            copy(A(rb, 0, W16), t2(0, W16))
+            exchange(peer, 2, t, ["rb"], W16)
 
         act(A("tb"), SBS, FN.Copy)
         run(own_scores(SBV, "hb"))
-        scalar_counts(SBS, "hb", "lhb", SC_B)
-        side = [own_scores(SAV, "ha"), ties(SBV, "hb", "eb"), ties(SAV, "ha", "ea")]
+        scalar_counts(SBS, "hb", "lhb", SC_B, H)
+        side = [own_scores(SAV, "ha"), ties(SBV, "hb", "eb")]
         if t == 0:
             side.append(late_constants())
-        vector_counts(SBV, "hb", "cb", W16 - SC_B, chain(*side))
-        scalar_counts(SAS, "ha", "lha", SC_A)
-        vector_counts(SAV, "ha", "ca", W16 - SC_A, chain(idle(SORT_AT), sort_b(), idle(SEARCH_AT), search()))
-        unpack(*QT, 0)
-        act(A("wd"), A("iot"), FN.Copy)
-        unpack(A("qtp%d" % t), A("stp%d" % t), DP)
+        side = chain(*side)
+        weave(vector_counts(SBV, "hb", "cb", W16 - SC_B, H), side, 1)
+        run(side)
+        va = W16 - SC_A[t]
+        scalar_counts(SAS, "ha", "lha", W16 - va, C)
+        counts = vector_counts(SAV, "ha", "ca", va, C)
+        weave(sort_b(), counts, SORT_EVERY)
+        if t == 0:
+            later_constants()
+        weave(chain(ties(SAV, "ha", "ea"), idle(SEARCH_AT)), counts, 1)
+        ts(A("lha", 64 + va, 64 + W16), A("ea", 16 * va + 15, C, 16), -2.0, MUL)
+        weave(search(), counts, SEARCH_EVERY)
+        run(counts)
+        if t == 0:
+            act(A("w9"), A("tab"), FN.Copy, scale=0.0)
+        theirs = chain(unpack(*QT, 0, C + H), unpack(A("qtp%d" % t), A("stp%d" % t), DP, C))
 
-        run(places("ca", "lha", SC_A, "ea"))
-        ts(I(0, W16), A("t1", 0, W16), float(H), ADD)
-        ts(A("l1", 0, W16), A("t1", 0, W16), float(H), ADD)
-        ts(I(128, W16), I(0, W16), 1, AND)
-        copy(IND(half("inv", 0), A("l1", 0, W16)), half("iot", 0))
-        n = 2 * W16
-        ts(A("t1", 0, W16), I(128, W16), -2.0, MUL, 1.0, ADD)
-        copy(I(n, W16), A(rbp))
-        tt(A("t2", 0, W16), A("t1", 0, W16), I(0, W16), ADD)
-        ts(I(128 + W16, n), I(W16, n), 1, AND)
-        copy(A("l2", 0, W16), A("t2", 0, W16))
-        ts(A("t1", W16, W16 + n), I(128 + W16, n), -2.0, MUL, 1.0, ADD)
-        copy(A("am"), IND(half("inv", 0), A("l2", 0, W16)))
-        tt(A("t2", W16, W16 + n), A("t1", W16, W16 + n), I(W16, n), ADD)
-        scan(half("scn", 0), half("k16", 0), A("am"), 0.0, ADD, MAX)
-        copy(A("l2", W16, W16 + n), A("t2", W16, W16 + n))
-        ts(A(aml), A("scn", 15, C, 16), col(H16), SUB)
-        exchange(peer, 1, t, ["aml"])
+        tt(A("lha", va, W16), A("lha", va, W16), A("lha", 32 + va, 32 + W16), ADD)
+        tt(t1(0, va), A("ca", H - 1, va * H, H), A("ea", 15, 16 * va, 16), SUB)
+        tt(t1(va, W16 - va), A("lha", va, W16), A("lha", 64 + va, 64 + W16), ADD)
+        run(cross(t2(0, 32), t1(0, 32), up))
+        for out, src in ((pa, "t2_"), ("ka_", "t1_")):
+            ts(A(out, 0, va), A(src, 0, va), float(H), ADD)
+            ts(A(out, va, W16), A(src, va, W16), 0.5, MUL, float(H), ADD)
+            if out == pa:
+                exchange(peer, 1, t, ["pa"], W16)
+        copy(A("kw_", 32, 32 + W16), A(rbp, 0, W16))
+        copy(I(0, 32), IND(A("kw_"), sel(SH, up)))
+        ts(I(32, 32), I(0, 32), 1, AND)
+        ts(I(64, 32), I(0, 32), 1, SHR, 31, AND)
+        ts(I(96, 32), I(0, 32), 1, SHR)
+        ts(t2(0, 32), I(32, 32), 31.0, MUL)
+        tt(t2(32, 32), I(0, 32), I(64, 32), SUB)
+        copy(A("lp_"), I(96, 32))
+        tt(t1(32, 32), t2(0, 32), t2(32, 32), ADD)
+        copy(A("lw_"), t1(32, 32))
+        lw = A("lw_", 0, W16)
+        tt(A("r1"), IND(A("tab"), lw), half("cc", 0), ADD)
+        if t == 0:
+            quant(A("qe"), A("se"), A("et"))
 
-        copy(IND(A("inv"), A(rb)), half("iot", me))
-        copy(IND(A("inv"), A(rbp)), half("iot", other))
-        act(half("bm", other), IND(A("inv"), A("l2", 2 * W16, 3 * W16)), FN.Copy)
-        copy(half("bm", me), IND(A("inv"), A("l2", W16, 2 * W16)))
-        act(half("j0", other), IND(half("bm", other), A(amp)), FN.Copy)
-        copy(half("j0", me), IND(half("bm", me), A(aml)))
-        act(A("vp"), IND(half("iot", 0), A(amp)), FN.Copy)
-        rec("g", lambda q: q.dma_start(ap(A("vp")), ap(A("jf")), accum_op=ADD), [A("jf")], [A("vp")],
-            lane="m4_%d" % t, dma=True, add=16)
-
-        low = "iot"
-        for k in range(9):
-            jc, jn, pk = "j%d" % (k % 2), "j%d" % (1 - k % 2), 56 * (k % 2)
-            nxt = "w%d" % (k % 2)
-            scan(A("scn"), A("k16"), A(jc), 0.0, ADD, MAX)
-            ts(A("pk", pk, pk + 56), A("scn", 15, J, 16), col(H16), SUB)
-            if k < 8:
-                act(A(jn), IND(A(jc), A("pk", pk, pk + 56)), FN.Copy)
-                tt(A(nxt), IND(A(low), A("pk", pk, pk + 56)), A("wd"), MIN)
-                act(A("wd"), A(nxt), FN.Copy)
-            else:
-                for a in (other, me):
-                    tt(half(nxt, a), IND(A(low), A("pk", pk + a // 16, pk + a // 16 + W16)), half("wd", a), MIN)
-                    act(half("wd", a), half(nxt, a), FN.Copy)
-            low = nxt
-
-        tt(half("red", 0), IND(half(low, other), A(amp)), half("wd", other), GT)
-        scan(half("cum", 0), half("red", 0), half("red", 0), float(C - 1), ADD, MAX)
-        tt(half("red", C), IND(half(low, me), A(aml)), half("wd", me), GT)
-        numbered(0)
-        scan(half("scn", 0), half("k16", 0), half("mm", 0), 0.0, ADD, MAX)
-        tt(A("t1", 0, W16), A("scn", 15, C, 16), A("jw"), MAX)
-        ts(A("l1", 0, W16), A("t1", 0, W16), col(H16), SUB)
-        copy(IND(A("ew"), A("l1", 0, W16)), A("vp"))
-        scan(A("scn", 0, H), A("k4", 0, H), A("ew", C, C + H), 0.0, ADD, MAX)
-        ts(I(0, 56), A("scn", 3, H, 4), 8192.0, MUL, col(BC), SUB)
-        ts(I(56, 56), I(0, 56), 2047, AND)
-        ts(I(112, 56), I(0, 56), 11, SHR)
-        copy(A("lb"), I(56, 112))
-        theirs = A("dw", DP, DP + 4 * C)
+        copy(A("ka_", 32, 32 + W16), A(pap, 0, W16))
+        copy(I(0, 32), IND(A("ka_"), sel(SH, up)))
+        copy(A("la_"), IND(A("ka_"), sel(SH, up)))
+        ts(I(32, 32), I(0, 32), 510, AND)
+        copy(IND(A("inv"), A("la_", 0, W16)), A("r1"))
+        ts(t1(0, 32), I(32, 32), 2.0, MUL, 1.0, ADD)
+        tt(t1(32, 32), t1(0, 32), I(0, 32), SUB)
+        copy(A("lx_"), t1(32, 32))
+        tt(A("r2"), IND(A("inv"), A("lx_", 0, W16)), half("cc", C), ADD)
+        copy(IND(A("w9"), lw), A("r2"))
+        turn(A("x9"), A("w9"))
+        for l in (LO, HL, HU, EN):
+            tt(A("xx", 16 + l, 16 + C, 16), A("x9", l, J, 32), A("x9", 16 + l, J, 32), ADD)
         for h in range(2):
-            act(half("bh", C * h), IND(theirs, A("lb", W16 * h, W16 * h + W16)), FN.Copy)
-        scan(half("cum", C), half("red", C), half("red", C), float(C - 1), ADD, MAX)
-        numbered(C)
+            a = 32 * (1 - h) + EN
+            tt(lane(h, PL), A("x9", a, J, 64), A("x9", a + 16, J, 64), ADD)
+        turn(half("w0", 16), half("xx", 16))
+
+        for k in range(STEPS):
+            wc, wn, a = "w%d" % (k % 2), "w%d" % (1 - k % 2), 32 * (k % 2)
+            act(A("wd"), half(wc, 16), FN.Identity, bias=col(FAR), scale=col(KEEP))
+            next(theirs, None)
+            turn(A("xx", 496, 976), A(wc, 0, 480))
+            turn(A(wc, 32 + C, WW), A("xx", 0, 480))
+            tt(A("cs_", 0, 30), A("xx", 16 + HL, 976, 32), A("xx", 16 + LO, 976, 32), ADD)
+            tt(A("cs_", 32, 62), A("xx", 32 + HU, 992, 32), A("xx", 32 + LO, 992, 32), ADD)
+            copy(A("pk_", a, a + 32), IND(A("cs_"), sel(SD)))
+            tt(half(wn, 16), IND(A(wc, 16), A("pk_", a, a + W16)), A("wd"), MIN)
+            turn(half("xx", 16), half(wn, 16))
+
+        tt(t1(0, 14), lane(0, PL), lane(1, EN), MIN)
+        tt(t1(14, 14), lane(0, EN), lane(1, PL), MIN)
         for h in range(2):
-            tt(half("bt", C * h), IND(theirs, A("lb", 56 + W16 * h, 56 + W16 * h + W16)), half("bh", C * h), ADD)
+            tt(A("x2", 16 * h + EV, C, 32), t1(0, 14), t1(14, 14), LT)
+        turn(A("inv"), A("x2"))
+        tt(A("red"), IND(A("inv"), A("lp_", 0, W16)), A("r1"), NE)
+        if t < R - 1:
+            act(A("w9"), A("tab"), FN.Copy, scale=0.0)
+        scan(A("cum"), A("red"), A("red"), 0.0, ADD, MAX)
+        scan(half("mm", 16), A("cum"), A("red"), 0.0, MAX, MUL)
+        turn(half("xx", 16), half("mm", 16))
+        turn(A("xx", 496, 976), A("mm"))
+        ts(t1(0, 32), IND(A("xx"), sel(SM)), 1024.0, MUL, float(C - 1), MIN)
+        tt(t1(32, 32), IND(A("xx"), sel(SM)), t1(0, 32), ADD)
+        tt(A("ff_", 64, 96), t1(32, 32), A("jw_"), MAX)
+        copy(A("lv_"), A("ff_", 64, 96))
+        copy(IND(A("ew", 0, C + H), A("lv_", 0, W16)), A("r2"))
+        turn(A("x3", 0, H), A("ew", C, C + H))
+        a = C + 16 - 32 * up
+        turn(A("x3", H, C), A("ew", a, a + H))
+        tt(A("ff_", 0, W16), A("x3", EH, C, 16), A("x3", EL, C, 16), ADD)
+        tt(A("ff_", 32, 32 + W16), A("x3", JH, C, 16), A("x3", JL, C, 16), ADD)
+        copy(A(rr), IND(A("ff_", 0, 96), sel(SS, up)))
+        exchange(peer, 4, t, ["rr"], W16)
+        copy(A("kr_", 0, 32), IND(A("ff_", 0, 96), sel(SK, up)))
+        if t == 0:
+            quant(A("qv"), A("sv"), A("vb"))
+            if ups[1] != up:
+                run(side_lists(ups[1]))
+        copy(A("kr_", 32, 32 + W16), A(rrp, 0, W16))
+        copy(A("lb_"), IND(A("kr_"), sel(SH, up)))
+
+        for b in range(4):
+            act(A("bh", H * b, H * b + H), IND(half("dw", DP + C * b), A("lb_", 0, 14)), FN.Copy)
+        run(cross(A("ff_", 96, 128), A("kr_", 32, 64), 1 - up))
+        for b in range(4):
+            tt(A("bt", b, 4 * H, 4), IND(half("dw", DP + C * b), A("lb_", 14, W16)), A("bh", H * b, H * b + H), ADD)
         quant(A("qb"), A("sq"), A("bt"))
         for b in range(4):
             mm(PS(b, H), *stat("e", b), A("qb"), A("sq"))
-        scan(half("scn", 0), A("k4"), half("mm", C), 0.0, ADD, MAX)
-        if t == R - 1:
-            scan(half("scn", C), half("k16", 0), half("mm", C), 0.0, ADD, MAX)
-        tt(A("t1"), A("scn", 3, C, 4), A("j4"), MAX)
-        if t == R - 1:
-            tt(A("t2", 0, W16), A("scn", C + 15, J, 16), A("jw"), MAX)
+        copy(A("ly_"), IND(A("ff_", 64, 128), sel(SH, up)))
         for b in range(4):
-            out = A("dw", 4 * C + b, DP, 4)
-            if b == 2:
-                ts(out, PS(b, H), 0.5, MUL)
-                ts(A("ly"), A("t1"), 4.0, MUL, col(YC), SUB)
+            a = (C + H) * b
+            came, win, out = A("dw", a + C, a + C + H), IND(A("dw", a, a + C + H), A("ly_", 0, W16)), A("yt", b, 4 * C, 4)
+            if b % 2 == 0:
+                ts(came, PS(b, H), 0.5, MUL)
+                ts(out, win, 2.0, MUL)
             else:
-                act(out, PS(b, H), FN.Copy, scale=0.5)
-        act(A("yt", J, 2 * J), IND(A("dw", 0, DP), A("ly", 56, 112)), FN.Copy, scale=2.0)
-        ts(A("yt", 0, J), IND(A("dw", 0, DP), A("ly", 0, 56)), 2.0, MUL)
-        if t == R - 1:
-            ts(A("l1", 0, W16), A("t2", 0, W16), col(H16), SUB)
+                act(came, PS(b, H), FN.Copy, scale=0.5)
+                act(out, win, FN.Copy, scale=2.0)
 
         quant(A("qz"), A("sz"), A("yt"))
-        for b in range(4):
-            mm(PS(4 + b), *stat("w", b), A("qz"), A("sz"))
-            mm(PS(b), *stat("e", b), A("qz"), A("sz"))
+        for name, b in (("w", 0), ("w", 1), ("e", 0), ("w", 2), ("e", 1), ("w", 3), ("e", 2), ("e", 3)):
+            mm(PS(b + (4 if name == "w" else 0)), *stat(name, b), A("qz"), A("sz"))
         if t == R - 1:
-            copy(IND(A("ew"), A("l1", 0, W16)), half("iot", 0))
+            copy(IND(A("eo"), A("ly_", 0, W16)), half("iot", 0))
             for k in range(8):
-                dma("y", "dol", lambda k=k: (T.ol[k:k + 1, :], T.ew[16 * k:16 * k + 1, C:C + H]), [A("ew")], [])
+                dma("y", "dol", lambda k=k: (T.ol[k:k + 1, :], T.eo[16 * k:16 * k + 1, C:C + H]), [A("eo")], [])
         for b in range(4):
-            rl = half("rl", C * (b % 2))
-            act(rl, PS(4 + b), FN.Relu, scale=0.03125)
-            tt(A("xt", b, 4 * C, 4), PS(b), rl, ADD)
+            rl = half("rl", C * b)
+            if b == 0 and t < R - 1:
+                ts(rl, PS(4), 0.0, MAX, 0.03125, MUL)
+            else:
+                act(rl, PS(4 + b), FN.Relu, scale=0.03125)
+        for b in range(4):
+            tt(A("xt", b, 4 * C, 4), PS(b), half("rl", C * b), ADD)
         quant(A("qt%d" % (t + 1)), A("st%d" % (t + 1)), A("xt"))
 
     QT = (A("qt%d" % R), A("st%d" % R))

@@ -8,35 +8,38 @@ NS = 3 * RUN
 ZP = 48
 ULP, TINY, FARTHEST = 0.6 * 2.0 ** -23, 2.0 ** -124, 2.0 ** 96
 TW = C + C + 32
-DP = 4 * (C + H)
-SC_B, SC_A = 11, (19, 18, 18)
-SORT_EVERY, SEARCH_AT, SEARCH_EVERY = 3, 5, 4
-WW = 16 + C + 16 + C + 32
+PW = 2304
+DP = 4 * PW
+SC_B, SC_A = 12, (20, 20, 20)
+SORT_EVERY, SEARCH_AT, SEARCH_EVERY = 1, 2, 2
+MID, OWN, WW = 1024, 784, 2816
+RUNS = ((0, 192, 0, 4), (192, 384, 1280, 4), (384, 480, 2048, 8))
+GL = 256
 STEPS = 8
 BIG = 65536.0
-LO, HL, HU, EN, JH, JL, PL, EH, EL, EV = range(10)
+HL, HU, EN, PL, JA, JE, EV, ER = range(8)
 F32, BF, I32, U16, X4, U8 = "float32", "bfloat16", "int32", "uint16", "float8_e4m3fn_x4", "uint8"
 
 _SB = {
     "x0": (4 * C, BF), "ub": (512, BF), "vb": (512, BF), "xt": (4 * C, BF), "yt": (4 * C, BF), "bt": (4 * H, BF),
     "qu": (128, X4), "su": (128, U8), "qur": (256, X4), "sur": (256, U8), "qv": (128, X4), "sv": (128, U8),
-    "qw": (512, X4), "sw": (512, U8), "qe": (512, X4), "se": (512, U8), "et": (2048, BF), "one": (128, BF), "idn": (128, BF),
+    "qw": (512, X4), "sw": (512, U8), "qe": (512, X4), "se": (512, U8), "et": (2048, BF), "one": (128, BF),
     "qz": (C, X4), "sz": (C, U8), "qb": (H, X4), "sq": (H, U8), "qt%d" % R: (C, X4), "st%d" % R: (C, U8),
     "pi": (16, I32), "cf": (32, F32), "upi": (16, I32), "upk": (16, U16),
-    "r16": (C + 16, BF), "md": (C, BF), "kz": (C, BF), "k0": (TW, BF), "k27": (W16 * NS, BF), "kb": (W16 * NS, BF),
-    "iot": (512, F32), "sm": (192, F32), "tab": (J, BF), "cc": (J, BF),
+    "r16": (C, BF), "md": (C, BF), "kz": (C, BF), "k0": (TW, BF), "kb": (W16 * NS, BF),
+    "iot": (C, F32), "sm": (192, F32), "tab": (J, BF), "cc": (J, BF),
     "msk": (C, F32), "ha": (C, F32), "hb": (C, F32), "eq": (C, BF), "ea": (C, BF), "eb": (C, BF),
-    "fl": (4 * C, BF), "ca": (W16 * H, BF), "cb": (W16 * H, BF), "sg": (3 * C, BF), "lha": (96, F32), "lhb": (96, F32),
-    "ii": (128, I32), "tb": (C, F32), "zp": (C + 32, F32), "zt": (TW, F32), "fp": (C + 32, BF), "ft": (TW, BF), "fs": (TW, BF),
+    "fl": (4 * C, BF), "ca": (W16 * H, BF), "cb": (W16 * H, BF), "sg": (3 * C, BF), "lha": (32, F32), "lhb": (32, F32),
+    "ii": (128, I32), "wa": (J, F32), "wb": (J, F32), "gap": (J, F32), "zp": (C + 32, F32), "zt": (TW, F32), "fp": (C + 32, BF), "ft": (TW, BF), "fs": (TW, BF),
     "f1": (W16 * NS, BF), "s1": (W16 * NS, BF), "fq": (3 * C, BF),
-    "r1": (C, BF), "r2": (C, BF), "inv": (C, BF), "w9": (J, BF), "x9": (J, BF), "x2": (C, BF), "xx": (1024, BF),
+    "r1": (C, BF), "r2": (C, BF), "inv": (C, BF), "vni": (C, BF), "ks": (C, BF), "yb": (64, BF), "w9": (J, BF), "x9": (J, BF), "x2": (C, BF), "xx": (1024, BF),
     "w0": (WW, BF), "w1": (WW, BF), "wd": (C, BF),
-    "red": (C, BF), "cum": (C, BF), "mm": (C + 32, BF), "ew": (C + H + 32, BF), "x3": (C, BF), "eo": (C + H, F32),
+    "red": (C, BF), "mm": (C + 32, BF), "ew": (PW + 128, BF), "x3": (C + 64, BF), "eo": (H, F32),
     "dw": (DP + 4 * C, BF), "bh": (4 * H, F32), "rl": (4 * C, F32), "yo": (C, F32),
 }
-_PART = {}
-for _b, _d, _names in (("sf", F32, "rs64 sp64 sq64 sr88 sb88 yy64 kw64 ka64 kr64 cs64 ff128 t164 t264 jw32"),
-                       ("lu", U16, "cl2 se16 l132 l284 lw32 lp32 la32 lx32 lv32 lb32 ly32 pk64")):
+_PART = {"tb_": ("wb", H, C)}
+for _b, _d, _names in (("sf", F32, "rs64 sp64 sq64 sr88 sb88 yy64 kw64 t164 t264 jw32"),
+                       ("lu", U16, "cl2 se18 l132 l284 lw32 lp32 la32 lv32 lb32 ly32 pk64")):
     _at = 0
     for _x in _names.split():
         _PART[_x[:2] + "_"] = (_b, _at, int(_x[2:]))
@@ -44,12 +47,14 @@ for _b, _d, _names in (("sf", F32, "rs64 sp64 sq64 sr88 sb88 yy64 kw64 ka64 kr64
     _SB[_b] = (_at, _d)
 for _t in range(R):
     _SB["z%d" % _t] = (96, F32)
-    for _n, _w, _d in (("rb", 32, U16), ("pa", 32, U16), ("rr", 32, U16), ("qt", C, X4), ("st", C, U8)):
+    _SB["pa%d" % _t] = (96, BF)
+    _SB["rr%d" % _t] = (128, BF)
+    for _n, _w, _d in (("rb", 32, U16), ("qt", C, X4), ("st", C, U8)):
         _SB["%s%d" % (_n, _t)] = (_w, _d)
         _SB["%sp%d" % (_n, _t)] = (_w, _d)
 SCRATCH = {k: ("sbuf", [128, n], d) for k, (n, d) in _SB.items()}
 SCRATCH["ps"] = ("psum", [128, 4096], F32)
-SEMAPHORES = ["cp", "cv", "cs", "cg", "sent", "dx", "du", "dv", "dl", "dol", "doc", "dy"] + \
+SEMAPHORES = ["cp", "cv", "cs", "cg", "sent", "dx", "dz", "du", "dv", "dl", "dol", "doc", "dy", "m5_%d" % (R - 1)] + \
     ["m%d_%d" % (m, t) for m in range(5) for t in range(R)]
 
 ADD, SUB, MUL, MAX, MIN = AluOpType.add, AluOpType.subtract, AluOpType.mult, AluOpType.max, AluOpType.min
@@ -247,15 +252,16 @@ def rank_program(g, core, T, topo):
     def t2(a, n):
         return A("t2_", a, a + n)
 
-    dma("y", "dx", lambda: (ap(A("x0")), T.x[:]), [], [A("x0")])
     dma("s", "du", lambda: (ap(A("ub")), T.u[:]), [], [A("ub")])
+    dma("y", "dx", lambda: (ap(A("x0", 0, J)), T.x[:, 0:J]), [], [A("x0", 0, J)])
+    dma("s", "dz", lambda: (ap(A("x0", J)), T.x[:, J:2 * J]), [], [A("x0", J)])
     dma("y", "dv", lambda: (ap(A("vb")), T.v[:]), [A("x0")], [A("vb")])
     dma("y", "dl", lambda: (u8(A("qw")), T.wc[:]), [], [A("qw")])
     dma("y", "dl", lambda: (ap(A("sw")), T.ws[:]), [], [A("sw")])
 
     ups = [1 if rank & STEP[t] else 0 for t in range(R)]
     Q, P32, PAR, ODD, QHALF, KEEP, FAR, X1, X2, X3, X5, X6 = range(12)
-    SD, SM, SH, SK, SS = 0, 2, 4, 6, 8
+    SD, SM, SR, SH, SK, SS = 0, 2, 4, 6, 8, 10
 
     def sel(k, up=0):
         k += 6 * up
@@ -263,10 +269,10 @@ def rank_program(g, core, T, topo):
 
     iota(A("pi", 0, 1), [[1, 1]], 0, 1)
     iota(A("upi"), [[-8, 2], [16, 8]], 8, 0)
-    iota(A("r16", 0, C + 16), [[0, W16 + 1], [1, 16]], 0, 0)
-    fill(A("one"), 1.0)
-    for name in ("lha", "lhb"):
-        fill(A(name), 0.0)
+    iota(A("r16"), [[0, W16], [1, 16]], 0, 0)
+    iota(A("sm", 8, 40), [[16, 32]], 0, 0)
+    iota(A("iot"), [[1, C]], 0, 0)
+    iota(A("one"), [[0, 128]], 1, 0)
     p = A("pi", 0, 1)
     ts(A("pi", 1, 2), p, 15, AND)
     ts(A("pi", 2, 3), p, 31, AND)
@@ -275,43 +281,41 @@ def rank_program(g, core, T, topo):
     ts(A("pi", 5, 6), p, 1, SHR, 7, AND)
     copy(A("upk"), A("upi"))
     copy(A("cf", 0, 5), A("pi", 1, 6))
-    iota(A("iot"), [[1, 512]], 0, 0)
+    fill(("sf", _PART["yy_"][1], _PART["jw_"][1], 1), 0.0)
     tt(col(X1), col(ODD), col(PAR), NE)
     tt(col(X2), col(ODD), col(PAR), GT)
     ts(col(X3), col(QHALF), 32.0, MUL, 15.0, ADD)
-    ts(A("md"), A("r16", 16, 16 + C), col(Q), EQ)
-    ts(A("kz"), A("r16", 16, 16 + C), col(Q), NE)
-    quant(A("qu"), A("su"), A("ub"))
-    rec("v", lambda q: q.tensor_copy(ap(A("qur")).bitcast(dt.uint32), ap(A("qu")).bitcast(dt.uint32).indirect(ap(A("upk")))),
-        [A("qu"), A("upk")], [A("qur")])
-    rec("s", lambda q: q.activation(ap(A("sur")), ap(IND(A("su"), A("upk"))), FN.Copy), [A("su"), A("upk")], [A("sur")])
-    for a in (0, C + 16):
-        act(A("k0", a, a + C + 16), A("r16"), FN.Sign)
-    fill(("sf", _PART["yy_"][1], _PART["jw_"][1], 1), 0.0)
+    ts(A("md"), A("r16"), col(Q), EQ)
+    ts(A("kz"), A("r16"), col(Q), NE)
 
     def zeros(*views):
         for v in views:
             iota(v, [[0, v[2] - v[1]]], 0, 0)
 
     def later_constants():
+        iota(A("k0"), [[0, TW // 16], [64, 16]], 0, 0)
+        zeros(A("yb"), *[A("pa%d" % t, 56, 64) for t in range(R)])
         zeros(A("et"))
         for b in range(4):
             out = A("et", 512 * b + b, 512 * (b + 1), 4)
             rec("g", lambda q, out=out: q.affine_select(ap(out), ap(A("one")), [[-1, 128]], EQ, 0.0, 0, 1), [A("one")], [out])
-        zeros(A("x2"), A("xx"), A("mm"), A("ew", C - 16), *[A(w, a, a + 16) for w in ("w0", "w1") for a in (0, C + 16)])
+        zeros(A("x2"), A("xx"), A("mm"), A("ew", 384, 512), A("ew", PW), A("rr%d" % (R - 1), 112),
+              *[A(w, a, a + 16) for w in ("w0", "w1") for a in (OWN - 16, OWN + C)])
 
     def side_lists(up):
         ts(col(X1), col(PAR), float(up), NE, 32.0, MUL)
         ts(col(X2), col(ODD), float(up), NE, 14.0, MUL)
         ts(col(X3), col(PAR), float(up), EQ)
         ts(col(X5), col(PAR), float(up), NE)
-        yield
         ts(sel(SH, up), A("jw_", 0, 2), col(X1), ADD)
         tt(col(X2), col(X2), col(ODD), SUB)
-        ts(A("sm", 2, 4), A("jw_", 0, 2), 64.0, ADD, col(X5), MUL)
+        ts(A("sm", 2, 4), A("jw_", 0, 2), float(C), ADD, col(X5), MUL)
         yield
-        ts(sel(SK, up), A("sm", 0, 2), col(X2), ADD, float(1 - up), ADD)
-        ts(A("sm", 4, 6), A("sm", 0, 2), col(X2), ADD, float(up), ADD)
+        ts(col(X6), col(X2), 16.0, MUL, 16.0 * (1 - up) + JE, ADD)
+        ts(col(X2), col(X2), 16.0, MUL, 16.0 * up + JE, ADD)
+        yield
+        ts(sel(SK, up), A("sm", 0, 2), col(X6), ADD, float(C), MIN)
+        ts(A("sm", 4, 6), A("sm", 0, 2), col(X2), ADD, float(C), MIN)
         yield
         ts(A("sm", 6, 8), A("sm", 4, 6), col(X3), MUL)
         yield
@@ -321,61 +325,81 @@ def rank_program(g, core, T, topo):
 
     def late_constants():
         iota(A("sm", 112, 140), [[32, 14], [C, 2]], -C, 0)
+        iota(A("sm", 140, 168), [[32, 14], [0, 2]], -256, 0)
+        iota(A("sm", 88, 102), [[32, 14]], OWN - MID, 0)
+        for a, b, to, step in RUNS:
+            iota(A("sm", 40 + a // 32, 40 + b // 32), [[32 * step, (b - a) // 32]], to - MID, 0)
+            iota(A("sm", 56 + a // 32, 56 + b // 32), [[0, (b - a) // 32]], step, 0)
+        zeros(A("zp", 0, 16), A("zp", C + 16), *[A("z%d" % t, a, a + 8) for t in range(R) for a in (32, 88)])
         zeros(A("w9"), A("x9"))
-        iota(A("w9", HL, J, 16), [[32, 14], [-C - 48, 2], [0, 2]], C + 48, 0)
-        iota(A("w9", HU, J, 16), [[32, 14], [C + 16, 2], [0, 2]], 0, 0)
-        iota(A("w9", EV, J, 16), [[0, 14], [1, 2], [0, 2]], 0, 0)
-        for a, hi in ((0, JH), (C, EH)):
-            iota(A("x9", a + hi, a + C, 16), [[32, 14], [0, 2]], 0, 0)
-        zeros(A("rs_", 48, 64), A("zp", 0, 16), A("zp", C + 16), A("fp", 0, 16), A("fp", C + 16))
+        for l in (EV, ER):
+            iota(A("w9", l, J, 16), [[0, 14], [1, 2], [0, 2]], 0, 0)
+        zeros(A("rs_", 48, 64), A("fp", 0, 16), A("fp", C + 16))
         iota(A("sb_", 0, 84), [[RUN, 2], [0, RUN], [RUN, 3]], 2, 0)
-        zeros(*[A("z%d" % t, a, a + 8) for t in range(R) for a in (32, 88)])
-        iota(A("kb"), [[0, 3 * W16], [1, RUN]], 0, 0)
+        iota(A("kb"), [[0, 3 * W16], [64, RUN]], 0, 0)
+
+    def fixed_lists():
         ts(col(X1), col(X1), float(C), MUL, col(X3), ADD)
         ts(col(X2), col(X2), 2.0, MUL, col(PAR), ADD)
-        ts(A("jw_"), A("iot", 0, 512, 16), col(Q), ADD)
+        ts(A("jw_"), A("sm", 8, 40), col(Q), ADD)
         ts(col(X5), col(ODD), -31.0, MUL, 47.0, ADD)
         ts(col(X6), col(ODD), 16.0, MUL, col(QHALF), ADD)
-        yield
         ts(col(X1), col(X2), 16.0, MUL, col(X1), ADD)
+        ts(col(X3), col(PAR), -1008.0, MUL, 16.0, ADD)
+        ts(t2(0, 2), A("jw_", 0, 2), 14.0, GE, float(JA - JE - H), MUL)
+        ts(t2(2, 2), A("jw_", 0, 2), 16.0, MUL)
         ts(col(X5), col(X5), col(PAR), MUL, col(X6), ADD)
-        ts(col(X3), col(PAR), -1008.0, MUL, 16.0 + EV, ADD)
-        ts(t2(0, 2), A("jw_", 0, 2), 14.0, GE, 18.0, MUL)
-        yield
-        ts(t1(0, 2), A("iot", 0, 512, 256), col(X1), ADD, float(TW - 1), MIN)
-        ts(t1(2, 2), A("iot", 0, 16, 8), col(X5), ADD)
-        tt(A("sm", 0, 2), t2(0, 2), A("jw_", 0, 2), ADD)
+        ts(t1(0, 2), A("sm", 8, 40, 16), col(X1), ADD, float(TW - 1), MIN)
         ts(col(KEEP), col(Q), float(EN), EQ)
         ts(col(X2), col(Q), float(PL), EQ)
-        yield
+        tt(A("sm", 0, 2), t2(0, 2), t2(2, 2), ADD)
+        ts(t1(2, 2), A("sm", 8, 10), 0.5, MUL, col(X5), ADD)
         copy(A("cl_"), t1(0, 2))
-        copy(sel(SD), t1(2, 2))
-        ts(sel(SM), t1(2, 2), 32.0, MUL, col(X3), ADD)
         tt(col(KEEP), col(KEEP), col(X2), ADD)
-        yield
+        ts(col(X6), col(Q), float(EV), EQ)
+        ts(t1(4, 2), t1(2, 2), 32.0, MUL, col(X3), ADD)
+        ts(A("ks"), A("r16"), 0.0, MUL, col(X6), ADD)
         ts(col(FAR), col(KEEP), -BIG, MUL, BIG, ADD)
+        ts(sel(SD), t1(4, 2), col(PAR), ADD)
+        ts(sel(SM), t1(4, 2), float(EV), ADD)
+        ts(sel(SR), t1(4, 2), float(ER), ADD)
+
+    def tables():
+        ts(A("sm", 72, 87), A("sm", 56, 71), col(P32), MUL)
+        ts(A("sm", 88, 102), A("sm", 88, 102), col(P32), ADD)
+        ts(A("sm", 112, 168), A("sm", 112, 168), col(P32), ADD)
         yield
-        for _ in side_lists(ups[0]):
-            yield
-        ts(A("w9", LO, J, 16), A("iot", 0, 56), 0.0, MUL, col(P32), ADD)
-        ts(A("sm", 112, 140), A("sm", 112, 140), col(P32), ADD)
-        yield
-        turn(A("tab"), A("w9"))
+        tt(A("sm", 72, 87), A("sm", 72, 87), A("sm", 40, 55), ADD)
+        for h in range(2):
+            copy(A("w9", 32 + 16 * h + HL, J, 64), A("sm", 88, 102))
+            copy(A("w9", 16 * h + HU, J, 64), A("sm", 88, 102))
         y = A("sm", 112, 140)
         ts(t1(0, W16), y, -256.0, MAX, 256.0, MIN)
         ts(t1(32, W16), y, -384.0, MAX, 384.0, MIN)
         ts(t2(32, W16), y, 4.0, MUL)
-        for a, lo in ((0, JL), (C, EL)):
-            ts(A("x9", a + lo, a + C, 16), A("iot", 0, W16), 0.0, MUL, col(P32), ADD)
-        yield
+        for h in range(2):
+            copy(A("w9", 16 * h + HL, J, 64), A("sm", 73, 87))
+            copy(A("w9", 32 + 16 * h + HU, J, 64), A("sm", 72, 86))
         tt(t1(0, W16), t1(0, W16), t1(32, W16), ADD)
         tt(t2(32, W16), t2(32, W16), t1(32, W16), SUB)
-        yield
+        for a in (JA, C + JE):
+            copy(A("x9", a, a // C * C + C, 16), A("sm", 140, 168))
+        turn(A("tab"), A("w9"))
         tt(A("x9", EN, C, 16), t2(32, W16), t1(0, W16), SUB)
-        ts(A("k27"), A("kb"), 1.0, MIN)
         yield
         turn(A("cc"), A("x9"))
-        yield
+        for _ in side_lists(ups[0]):
+            yield
+
+    def run(x):
+        for _ in x:
+            pass
+
+    fixed_lists()
+    quant(A("qu"), A("su"), A("ub"))
+    rec("v", lambda q: q.tensor_copy(ap(A("qur")).bitcast(dt.uint32), ap(A("qu")).bitcast(dt.uint32).indirect(ap(A("upk")))),
+        [A("qu"), A("upk")], [A("qur")])
+    rec("s", lambda q: q.activation(ap(A("sur")), ap(IND(A("su"), A("upk"))), FN.Copy), [A("su"), A("upk")], [A("sur")])
 
     def stat(name, b):
         return A("q" + name, 128 * b, 128 * b + 128), A("s" + name, 128 * b, 128 * b + 128)
@@ -389,23 +413,20 @@ def rank_program(g, core, T, topo):
         for _ in range(n):
             yield
 
-    def run(x):
-        for _ in x:
-            pass
-
     def part(src, a, b):
         return (src[0], src[1] + a, src[1] + b, 1)
+
+    def rivals(src, c, w):
+        a = 16 * c + 16 + 16 * c // w * w
+        return A(src, a, a + w), 16 * c < w
 
     def vector_counts(src, h, out, blocks, w):
         last, m = None, w // 2
         for n, c in enumerate(list(range(blocks)) + [None]):
             f = C * (n % 4)
             if c is not None:
-                a, own = 16 * c // w * w, A(h, 16 * c + 15, 16 * c + 16)
-                cut = 16 * c + 16 - a
-                ts(A("fl", f, f + cut), part(src, a, a + cut), own, GE, 0.5, SUB)
-                if cut < w:
-                    ts(A("fl", f + cut, f + w), part(src, a + cut, a + w), own, GT, 0.5, SUB)
+                row, first = rivals(src, c, w)
+                ts(A("fl", f, f + w), row, A(h, 16 * c + 15, 16 * c + 16), GE if first else GT, 0.5, SUB)
             yield
             if last is not None:
                 scan(A(out, last[1] * m, last[1] * m + m), A("fl", last[0], last[0] + m), A("fl", last[0] + m, last[0] + w),
@@ -418,29 +439,18 @@ def rank_program(g, core, T, topo):
             if n % every == every - 1:
                 next(filler, None)
 
-    def scalar_counts(src, h, lh, blocks, w):
+    def scalar_counts(src, h, lh, out, blocks, w):
         last = None
         for n, c in enumerate(list(range(W16 - blocks, W16)) + [None]):
             f = C * (n % 3)
             if c is not None:
-                a = 16 * c // w * w
-                act(A("sg", f, f + w), part(src, a, a + w), FN.Sign, bias=A(h, 16 * c + 15, 16 * c + 16), scale=-1.0)
+                act(A("sg", f, f + w), rivals(src, c, w)[0], FN.Sign, bias=A(h, 16 * c + 15, 16 * c + 16), scale=-1.0)
             if last is not None:
-                a, cut = last[0], last[0] + (16 * last[1]) % w + 16
-                act(A("sg", a, cut), A("sg", a, cut), FN.Sign, bias=0.5, scale=-1.0, acc=A(lh, last[1], last[1] + 1))
-                if cut < a + w:
-                    act(A("sg", cut, a + w), A("sg", cut, a + w), FN.Sign, bias=-0.5, scale=-1.0,
-                        acc=A(lh, 32 + last[1], 33 + last[1]))
+                a = A("sg", last[0], last[0] + w)
+                act(a, a, FN.Sign, bias=0.5 if rivals(src, last[1], w)[1] else -0.5, scale=-1.0, acc=A(lh, last[1], last[1] + 1))
             last = (f, c)
-
-    def places(counts, lh, blocks, equal, w):
         a, m = W16 - blocks, w // 2
-        tt(A(lh, 64 + a, 64 + W16), A(lh, a, W16), A(lh, 32 + a, 32 + W16), ADD)
-        yield
-        ts(A(counts, a * m + m - 1, W16 * m, m), A(lh, 64 + a, 64 + W16), 0.5, MUL)
-        yield
-        tt(t1(0, W16), A(counts, m - 1, W16 * m, m), A(equal, 15, C, 16), SUB)
-        yield
+        act(A(out, a * m + m - 1, W16 * m, m), A(lh, a, W16), FN.Copy, scale=0.5)
 
     def own_scores(src, h):
         tt(A("msk"), src, A("md"), MUL)
@@ -460,37 +470,51 @@ def rank_program(g, core, T, topo):
             act(half("dw", at + step * b), PS(4 + b), FN.Copy, scale=0.5)
             yield
 
-    def cross(out, src, to):
-        turn(A("yy_", 16, 48), src)
+    def cross(out, src, to, via):
+        turn(A(via, 16, 48), src)
         yield
-        turn(out, A("yy_", 32 - 32 * to, 64 - 32 * to))
+        turn(out, A(via, 32 - 32 * to, 64 - 32 * to))
         yield
 
     def lane(h, l):
         return A("xx", 16 + 16 * h + l, 16 + C, 32)
 
-    quant(A("qt0"), A("st0"), A("x0"))
+    def cols(name, s):
+        return A("q" + name, H * s, H * s + H), A("s" + name, H * s, H * s + H)
+
+    SBV, SBS, SAV, SAS = [PS(4, H), PS(6, H)], [PS(5, H), PS(7, H)], PS(0), PS(1)
+
+    def scores_b(t, s):
+        mm(SBS[s], *stat("ur", 0), *cols("t%d" % t, s))
+        mm(SBV[s], *stat("ur", 0), *cols("t%d" % t, s))
+
+    def store(s):
+        codes, scales = cols("t%d" % R, s)
+        mm(PS(4 + s, H), A("qv"), A("sv"), codes, scales)
+        dma("y", "doc", lambda: (T.oc[:, J * s:J * s + J], u8(codes)), [codes], [])
+
+    quant(*cols("t0", 0), A("x0", 0, J))
+    scores_b(0, 0)
+    quant(*cols("t0", 1), A("x0", J, 2 * J))
     for t in range(R):
         peer = T.cores[rank ^ STEP[t]]
         up = ups[t]
         before = GE if up else GT
-        z, rb, rbp, pa, pap, rr, rrp = ["%s%d" % (n, t) for n in ("z", "rb", "rbp", "pa", "pap", "rr", "rrp")]
+        z, rb, rbp, pa, rr = ["%s%d" % (n, t) for n in ("z", "rb", "rbp", "pa", "rr")]
         QT = (A("qt%d" % t), A("st%d" % t))
-        SBV, SBS, SAV, SAS = PS(0), PS(1), PS(2), PS(3)
         exchange(peer, 3, t, ["qt", "st"])
-        mm(SBV, *stat("ur", 0), *QT)
-        mm(SBS, *stat("ur", 0), *QT)
-        mm(SAV, *stat("ur", 1), *QT)
+        scores_b(t, 1)
         mm(SAS, *stat("ur", 1), *QT)
+        mm(SAV, *stat("ur", 1), *QT)
 
         def sort_b():
-            for _ in places("cb", "lhb", SC_B, "eb", H):
-                yield
+            tt(t1(0, W16), A("cb", H // 2 - 1, W16 * H // 2, H // 2), A("eb", 15, C, 16), SUB)
+            yield
             for r in range(2):
                 ts(A("l1_", RUN * r, RUN * r + RUN), t1(RUN * r, RUN), float(H // 2 + H * r), ADD)
             ts(A("rs_", 0, W16), t1(0, W16), float(H // 2), ADD)
             yield
-            copy(IND(half("zp", 16), A("l1_", 0, W16)), A("tb"))
+            copy(IND(half("zp", 16), A("l1_", 0, W16)), A("tb_"))
             yield
             turn(half("zt", 0), half("zp", 16))
             turn(A("zt", C, TW), A("zp"))
@@ -522,7 +546,7 @@ def rank_program(g, core, T, topo):
                 a = 2 + c // RUN * RUN
                 ts(A("f1", NS * c, NS * c + NS), A("sp_", a, a + NS), A("hb", 16 * c + 15, 16 * c + 16), before)
             yield
-            scan(A("s1"), A("k27"), A("f1"), 0.0, MUL, ADD)
+            scan(A("s1"), A("kb"), A("f1"), 0.0, MIN, ADD)
             yield
             found = [A("s1", RUN * s + RUN - 1, W16 * NS, NS) for s in range(3)]
             tt(A("sr_", 0, 84), A("s1", RUN - 1, W16 * NS, RUN), A("sb_", 0, 84), ADD)
@@ -533,13 +557,13 @@ def rank_program(g, core, T, topo):
             tt(t2(0, W16), t2(0, W16), found[2], ADD)
             yield
             win = A(z, 32, 96)
-            tt(half("fq", 0), IND(win, A("l2_", 0, W16)), A("tb"), before)
+            tt(half("fq", 0), IND(win, A("l2_", 0, W16)), A("tb_"), before)
             ts(t2(0, W16), t2(0, W16), 16.0, MUL)
             yield
-            tt(half("fq", C), IND(win, A("l2_", W16, 2 * W16)), A("tb"), before)
+            tt(half("fq", C), IND(win, A("l2_", W16, 2 * W16)), A("tb_"), before)
             tt(A("rs_", 32, 32 + W16), t2(0, W16), A("rs_", 0, W16), ADD)
             yield
-            tt(half("fq", 2 * C), IND(win, A("l2_", 2 * W16, 3 * W16)), A("tb"), before)
+            tt(half("fq", 2 * C), IND(win, A("l2_", 2 * W16, 3 * W16)), A("tb_"), before)
             tt(half("fq", 0), half("fq", 0), half("fq", C), ADD)
             yield
             tt(half("fp", 16), half("fq", 0), half("fq", 2 * C), ADD)
@@ -547,49 +571,63 @@ def rank_program(g, core, T, topo):
             turn(half("ft", 0), half("fp", 16))
             turn(A("ft", C, TW), A("fp"))
             yield
-            scan(A("fs"), A("k0"), A("ft"), 0.0, MUL, ADD)
+            scan(A("fs"), A("k0"), A("ft"), 0.0, MIN, ADD)
             yield
             tt(A("kw_", 0, 32), IND(A("fs"), A("cl_")), A("rs_", 32, 64), ADD)
             yield
-            for _ in cross(t2(0, 32), A("kw_", 0, 32), up):
+            for _ in cross(t2(0, 32), A("kw_", 0, 32), up, "yy_"):
                 yield
             copy(A(rb, 0, W16), t2(0, W16))
             exchange(peer, 2, t, ["rb"], W16)
 
-        act(A("tb"), SBS, FN.Copy)
-        run(own_scores(SBV, "hb"))
-        scalar_counts(SBS, "hb", "lhb", SC_B, H)
-        side = [own_scores(SAV, "ha"), ties(SBV, "hb", "eb")]
+        for s in range(2):
+            act(A("gap", H * s, H * s + H), SBS[s], FN.Abs, bias=TINY, scale=ULP)
+            act(A("tb_", H * s, H * s + H), SBS[s], FN.Copy)
+        act(half("gap", C), SAS, FN.Abs, bias=TINY, scale=ULP)
+        act(half("wa", C), SAS, FN.Copy)
+        tt(A("msk", 0, H), SBV[0], A("md", 0, H), MUL)
+        tt(A("wb", 0, H), SBV[0], A("gap", 0, H), SUB)
+        tt(A("msk", H, C), SBV[1], A("md", H, C), MUL)
+        tt(A("wb", 3 * H, J), SBV[1], A("gap", H, C), ADD)
+        scan(A("hb"), A("kz"), A("msk"), 0.0, MUL, ADD)
+        scalar_counts("wb", "hb", "lhb", "cb", SC_B, H)
+
+        def moved_a():
+            tt(half("wa", 0), SAV, half("gap", C), SUB)
+            yield
+
+        def ties_b():
+            for s in range(2):
+                tt(A("eq", H * s, H * s + H), SBV[s], A("hb", H * s, H * s + H), EQ)
+            yield
+            scan(A("eb"), A("kz"), A("eq"), 0.0, MUL, ADD)
+            yield
+        side = [own_scores(SAV, "ha"), moved_a(), ties_b()]
         if t == 0:
-            side.append(late_constants())
+            late_constants()
         side = chain(*side)
-        weave(vector_counts(SBV, "hb", "cb", W16 - SC_B, H), side, 1)
+        weave(vector_counts("wb", "hb", "cb", W16 - SC_B, H), side, 1)
         run(side)
         va = W16 - SC_A[t]
-        scalar_counts(SAS, "ha", "lha", W16 - va, C)
-        counts = vector_counts(SAV, "ha", "ca", va, C)
+        scalar_counts("wa", "ha", "lha", "ca", W16 - va, C)
+        counts = vector_counts("wa", "ha", "ca", va, C)
         weave(sort_b(), counts, SORT_EVERY)
         if t == 0:
             later_constants()
-        weave(chain(ties(SAV, "ha", "ea"), idle(SEARCH_AT)), counts, 1)
-        ts(A("lha", 64 + va, 64 + W16), A("ea", 16 * va + 15, C, 16), -2.0, MUL)
+        weave(chain(ties(SAV, "ha", "ea"), tables() if t == 0 else idle(SEARCH_AT)), counts, 1)
         weave(search(), counts, SEARCH_EVERY)
         run(counts)
         if t == 0:
             act(A("w9"), A("tab"), FN.Copy, scale=0.0)
-        theirs = chain(unpack(*QT, 0, C + H), unpack(A("qtp%d" % t), A("stp%d" % t), DP, C))
+        theirs = chain(unpack(*QT, 0, PW), unpack(A("qtp%d" % t), A("stp%d" % t), DP, C))
 
-        tt(A("lha", va, W16), A("lha", va, W16), A("lha", 32 + va, 32 + W16), ADD)
-        tt(t1(0, va), A("ca", H - 1, va * H, H), A("ea", 15, 16 * va, 16), SUB)
-        tt(t1(va, W16 - va), A("lha", va, W16), A("lha", 64 + va, 64 + W16), ADD)
-        run(cross(t2(0, 32), t1(0, 32), up))
-        for out, src in ((pa, "t2_"), ("ka_", "t1_")):
-            ts(A(out, 0, va), A(src, 0, va), float(H), ADD)
-            ts(A(out, va, W16), A(src, va, W16), 0.5, MUL, float(H), ADD)
-            if out == pa:
-                exchange(peer, 1, t, ["pa"], W16)
+        tt(A(pa, 32, 32 + W16), A("ca", H - 1, W16 * H, H), A("ea", 15, C, 16), SUB)
         copy(A("kw_", 32, 32 + W16), A(rbp, 0, W16))
+        x = cross(A(pa, 0, 32), A(pa, 32, 64), up, "yb")
+        next(x)
         copy(I(0, 32), IND(A("kw_"), sel(SH, up)))
+        next(x)
+        exchange(peer, 1, t, [(A(pa, 0, 32), A(pa, 64, 96))])
         ts(I(32, 32), I(0, 32), 1, AND)
         ts(I(64, 32), I(0, 32), 1, SHR, 31, AND)
         ts(I(96, 32), I(0, 32), 1, SHR)
@@ -603,111 +641,130 @@ def rank_program(g, core, T, topo):
         if t == 0:
             quant(A("qe"), A("se"), A("et"))
 
-        copy(A("ka_", 32, 32 + W16), A(pap, 0, W16))
-        copy(I(0, 32), IND(A("ka_"), sel(SH, up)))
-        copy(A("la_"), IND(A("ka_"), sel(SH, up)))
-        ts(I(32, 32), I(0, 32), 510, AND)
-        copy(IND(A("inv"), A("la_", 0, W16)), A("r1"))
-        ts(t1(0, 32), I(32, 32), 2.0, MUL, 1.0, ADD)
-        tt(t1(32, 32), t1(0, 32), I(0, 32), SUB)
-        copy(A("lx_"), t1(32, 32))
-        tt(A("r2"), IND(A("inv"), A("lx_", 0, W16)), half("cc", C), ADD)
+        la = A("la_", 0, W16)
+        ts(A("la_"), IND(A(pa, 32, 96), sel(SH, up)), float(H), ADD)
+        copy(IND(A("inv"), la), A("r1"))
+        act(A("vni", 1, C, 2), A("inv", 0, C, 2), FN.Copy)
+        copy(A("vni", 0, C, 2), A("inv", 1, C, 2))
+        tt(A("r2"), IND(A("vni"), la), half("cc", C), ADD)
         copy(IND(A("w9"), lw), A("r2"))
         turn(A("x9"), A("w9"))
-        for l in (LO, HL, HU, EN):
+        for l in (HL, HU, EN):
             tt(A("xx", 16 + l, 16 + C, 16), A("x9", l, J, 32), A("x9", 16 + l, J, 32), ADD)
         for h in range(2):
             a = 32 * (1 - h) + EN
             tt(lane(h, PL), A("x9", a, J, 64), A("x9", a + 16, J, 64), ADD)
-        turn(half("w0", 16), half("xx", 16))
+        turn(half("w0", OWN), half("xx", 16))
 
+        parts = ((0, GL), (GL, C))
         for k in range(STEPS):
-            wc, wn, a = "w%d" % (k % 2), "w%d" % (1 - k % 2), 32 * (k % 2)
-            act(A("wd"), half(wc, 16), FN.Identity, bias=col(FAR), scale=col(KEEP))
+            wc, wn, pk = "w%d" % (k % 2), "w%d" % (1 - k % 2), 32 * (k % 2)
+            for a, b in parts:
+                act(A("wd", a, b), A(wc, OWN + a, OWN + b), FN.Identity, bias=col(FAR), scale=col(KEEP))
             next(theirs, None)
-            turn(A("xx", 496, 976), A(wc, 0, 480))
-            turn(A(wc, 32 + C, WW), A("xx", 0, 480))
-            tt(A("cs_", 0, 30), A("xx", 16 + HL, 976, 32), A("xx", 16 + LO, 976, 32), ADD)
-            tt(A("cs_", 32, 62), A("xx", 32 + HU, 992, 32), A("xx", 32 + LO, 992, 32), ADD)
-            copy(A("pk_", a, a + 32), IND(A("cs_"), sel(SD)))
-            tt(half(wn, 16), IND(A(wc, 16), A("pk_", a, a + W16)), A("wd"), MIN)
-            turn(half("xx", 16), half(wn, 16))
+            turn(A("xx", 496, 976), A(wc, OWN - 16, OWN + C + 16))
+            if k:
+                turn(A("xx", 16 + GL, 16 + C), A(wc, OWN + GL, OWN + C))
+            for n, (a, b, to, step) in enumerate(RUNS):
+                turn(A(wc, to, to + step * (b - a), step), A("xx", a, b))
+                if n == 0:
+                    ts(A("pk_", pk, pk + 32), IND(A("xx"), sel(SD)), float(MID), ADD)
+            for a, b in parts:
+                tt(A(wn, OWN + a, OWN + b), IND(A(wc), A("pk_", pk + a // 16, pk + b // 16)), A("wd", a, b), MIN)
+            turn(A("xx", 16, 16 + GL), A(wn, OWN, OWN + GL))
+        turn(A("xx", 16 + GL, 16 + C), A(wn, OWN + GL, OWN + C))
 
         tt(t1(0, 14), lane(0, PL), lane(1, EN), MIN)
         tt(t1(14, 14), lane(0, EN), lane(1, PL), MIN)
-        for h in range(2):
-            tt(A("x2", 16 * h + EV, C, 32), t1(0, 14), t1(14, 14), LT)
+        for a in (EV, ER, 16 + EV, 16 + ER):
+            tt(A("x2", a, C, 32), t1(0, 14), t1(14, 14), LT)
         turn(A("inv"), A("x2"))
         tt(A("red"), IND(A("inv"), A("lp_", 0, W16)), A("r1"), NE)
         if t < R - 1:
             act(A("w9"), A("tab"), FN.Copy, scale=0.0)
-        scan(A("cum"), A("red"), A("red"), 0.0, ADD, MAX)
-        scan(half("mm", 16), A("cum"), A("red"), 0.0, MAX, MUL)
+        scan(half("mm", 16), A("ks"), A("red"), 0.0, MUL, ADD)
         turn(half("xx", 16), half("mm", 16))
         turn(A("xx", 496, 976), A("mm"))
-        ts(t1(0, 32), IND(A("xx"), sel(SM)), 1024.0, MUL, float(C - 1), MIN)
-        tt(t1(32, 32), IND(A("xx"), sel(SM)), t1(0, 32), ADD)
-        tt(A("ff_", 64, 96), t1(32, 32), A("jw_"), MAX)
-        copy(A("lv_"), A("ff_", 64, 96))
-        copy(IND(A("ew", 0, C + H), A("lv_", 0, W16)), A("r2"))
-        turn(A("x3", 0, H), A("ew", C, C + H))
-        a = C + 16 - 32 * up
-        turn(A("x3", H, C), A("ew", a, a + H))
-        tt(A("ff_", 0, W16), A("x3", EH, C, 16), A("x3", EL, C, 16), ADD)
-        tt(A("ff_", 32, 32 + W16), A("x3", JH, C, 16), A("x3", JL, C, 16), ADD)
-        copy(A(rr), IND(A("ff_", 0, 96), sel(SS, up)))
-        exchange(peer, 4, t, ["rr"], W16)
-        copy(A("kr_", 0, 32), IND(A("ff_", 0, 96), sel(SK, up)))
+        ts(t1(0, 32), IND(A("xx"), sel(SM)), 8.0, MUL, 504.0, ADD)
+        tt(t1(32, 32), IND(A("xx"), sel(SR)), t1(0, 32), MUL)
+        tt(t2(0, 32), t1(32, 32), A("jw_"), MAX)
+        copy(A("lv_"), t2(0, 32))
+        ts(A("x3", C, C + 32), t2(0, 32), 256.0, SUB)
+        copy(IND(A("ew", 0, PW), A("lv_", 0, W16)), A("r2"))
+        turn(A("x3", 0, H), A("ew", 512, PW, 8))
+        a = 640 - 256 * up
+        turn(A("x3", H, C), A("ew", a, a + 8 * H, 8))
+        copy(A(rr, 64, 96), IND(A("x3", 0, C + 32), sel(SS, up)))
+        exchange(peer, 4, t, [(A(rr, 64, 96), A(rr, 32, 64))])
+        copy(A(rr, 0, 32), IND(A("x3", 0, C + 32), sel(SK, up)))
+        if t == R - 1:
+            exchange(peer, 5, t, [(A(rr, 0, 16), A(rr, 96, 112))])
         if t == 0:
             quant(A("qv"), A("sv"), A("vb"))
             if ups[1] != up:
                 run(side_lists(ups[1]))
-        copy(A("kr_", 32, 32 + W16), A(rrp, 0, W16))
-        copy(A("lb_"), IND(A("kr_"), sel(SH, up)))
+        ts(A("lb_"), IND(A(rr, 0, 64), sel(SH, up)), 256.0, ADD)
 
         for b in range(4):
             act(A("bh", H * b, H * b + H), IND(half("dw", DP + C * b), A("lb_", 0, 14)), FN.Copy)
-        run(cross(A("ff_", 96, 128), A("kr_", 32, 64), 1 - up))
+        run(cross(A("x3", C + 32, C + 64), A(rr, 32, 64), 1 - up, "yb"))
         for b in range(4):
             tt(A("bt", b, 4 * H, 4), IND(half("dw", DP + C * b), A("lb_", 14, W16)), A("bh", H * b, H * b + H), ADD)
         quant(A("qb"), A("sq"), A("bt"))
         for b in range(4):
             mm(PS(b, H), *stat("e", b), A("qb"), A("sq"))
-        copy(A("ly_"), IND(A("ff_", 64, 128), sel(SH, up)))
-        for b in range(4):
-            a = (C + H) * b
-            came, win, out = A("dw", a + C, a + C + H), IND(A("dw", a, a + C + H), A("ly_", 0, W16)), A("yt", b, 4 * C, 4)
+        ts(A("ly_"), IND(A("x3", C, C + 64), sel(SH, up)), 256.0, ADD)
+
+        def pick(b, s):
+            a = PW * b
+            came = A("dw", a + 512, a + PW, 8)
+            win, out = IND(A("dw", a, a + PW), A("ly_", RUN * s, RUN * s + RUN)), A("yt", J * s + b, J * s + J, 4)
             if b % 2 == 0:
-                ts(came, PS(b, H), 0.5, MUL)
+                if s == 0:
+                    ts(came, PS(b, H), 0.5, MUL)
                 ts(out, win, 2.0, MUL)
             else:
-                act(came, PS(b, H), FN.Copy, scale=0.5)
+                if s == 0:
+                    act(came, PS(b, H), FN.Copy, scale=0.5)
                 act(out, win, FN.Copy, scale=2.0)
 
-        quant(A("qz"), A("sz"), A("yt"))
-        for name, b in (("w", 0), ("w", 1), ("e", 0), ("w", 2), ("e", 1), ("w", 3), ("e", 2), ("e", 3)):
-            mm(PS(b + (4 if name == "w" else 0)), *stat(name, b), A("qz"), A("sz"))
-        if t == R - 1:
-            copy(IND(A("eo"), A("ly_", 0, W16)), half("iot", 0))
-            for k in range(8):
-                dma("y", "dol", lambda k=k: (T.ol[k:k + 1, :], T.eo[16 * k:16 * k + 1, C:C + H]), [A("eo")], [])
-        for b in range(4):
-            rl = half("rl", C * b)
-            if b == 0 and t < R - 1:
-                ts(rl, PS(4), 0.0, MAX, 0.03125, MUL)
-            else:
-                act(rl, PS(4 + b), FN.Relu, scale=0.03125)
-        for b in range(4):
-            tt(A("xt", b, 4 * C, 4), PS(b), half("rl", C * b), ADD)
-        quant(A("qt%d" % (t + 1)), A("st%d" % (t + 1)), A("xt"))
+        def products(s, order):
+            for name, b in order:
+                mm(PS(b + (4 if name == "w" else 0), H), *stat(name, b), *cols("z", s))
 
-    QT = (A("qt%d" % R), A("st%d" % R))
-    mm(PS(4), A("qv"), A("sv"), *QT)
-    dma("y", "doc", lambda: (T.oc[:], u8(QT[0])), [QT[0]], [])
+        for b, s in ((0, 0), (1, 0), (2, 0), (3, 0), (0, 1), (1, 1), (3, 1)):
+            pick(b, s)
+        quant(*cols("z", 0), A("yt", 0, J))
+        products(0, [("w", 0), ("e", 0), ("w", 1), ("e", 1), ("w", 2), ("e", 2), ("w", 3), ("e", 3)])
+        pick(2, 1)
+        quant(*cols("z", 1), A("yt", J, 2 * J))
+        if t == R - 1:
+            ts(A("lv_"), IND(A(rr, 64, 128), sel(SH, up)), 256.0, ADD)
+        for s in range(2):
+            for b in range(4):
+                rl = A("rl", C * b + H * s, C * b + H * s + H)
+                act(rl, PS(4 + b, H), FN.Relu, scale=0.03125)
+                tt(A("xt", J * s + b, J * s + J, 4), PS(b, H), rl, ADD)
+                if s == 0:
+                    products(1, [("w", b), ("e", b)])
+                if (s, b) == (1, 0):
+                    quant(*cols("t%d" % (t + 1), 0), A("xt", 0, J))
+        if t < R - 1:
+            scores_b(t + 1, 0)
+        else:
+            act(A("eo"), IND(A("iot"), A("lv_", 0, RUN)), FN.Copy)
+            for k in range(8):
+                dma("y", "dol", lambda k=k: (T.ol[k:k + 1, :], T.eo[16 * k:16 * k + 1, :]), [A("eo")], [])
+            store(0)
+            act(A("yo", 0, H), PS(4, H), FN.Copy)
+            dma("s", "dy", lambda: (T.y[:, 0:H], ap(A("yo", 0, H))), [A("yo", 0, H)], [])
+        quant(*cols("t%d" % (t + 1), 1), A("xt", J, 2 * J))
+
+    store(1)
     for k in range(4):
-        dma("y", "doc", lambda k=k: (T.osc[4 * k:4 * k + 4, :], T["st%d" % R][32 * k:32 * k + 4, :]), [QT[1]], [])
-    copy(A("yo"), PS(4))
-    dma("s", "dy", lambda: (T.y[:], ap(A("yo"))), [A("yo")], [])
+        dma("ys"[k % 2], "doc", lambda k=k: (T.osc[4 * k:4 * k + 4, :], T["st%d" % R][32 * k:32 * k + 4, :]), [A("st%d" % R)], [])
+    copy(A("yo", H, C), PS(5, H))
+    dma("s", "dy", lambda: (T.y[:, H:C], ap(A("yo", H, C))), [A("yo", H, C)], [])
     ends = {}
     for o in ops:
         if o["lane"] in ("dol", "doc", "dy", "sent"):

@@ -6,12 +6,13 @@ W16 = C // 16
 RUN = W16 // 2
 NS = 3 * RUN
 ZP = 48
-ULP, TINY, FARTHEST = 0.6 * 2.0 ** -23, 2.0 ** -124, 2.0 ** 96
+ULP, TINY = 0.6 * 2.0 ** -23, 2.0 ** -124
+WQ = J - 15
 TW = C + C + 32
 PW = 2304
 DP = 4 * PW
-SC_B, SC_A = 12, (20, 20, 20)
-SORT_EVERY, SEARCH_AT, SEARCH_EVERY = 1, 2, 2
+SC_B, SC_A = (5, 5), (19, 18, 18)
+SORT_EVERY, SEARCH_AT, SEARCH_EVERY = 1, 3, 3
 MID, OWN, WW = 1024, 784, 2816
 RUNS = ((0, 192, 0, 4), (192, 384, 1280, 4), (384, 480, 2048, 8))
 GL = 256
@@ -26,11 +27,11 @@ _SB = {
     "qw": (512, X4), "sw": (512, U8), "qe": (512, X4), "se": (512, U8), "et": (2048, BF), "one": (128, BF),
     "qz": (C, X4), "sz": (C, U8), "qb": (H, X4), "sq": (H, U8), "qt%d" % R: (C, X4), "st%d" % R: (C, U8),
     "pi": (16, I32), "cf": (32, F32), "upi": (16, I32), "upk": (16, U16),
-    "r16": (C, BF), "md": (C, BF), "kz": (C, BF), "k0": (TW, BF), "kb": (W16 * NS, BF),
+    "r16": (H, BF), "md": (H, BF), "kz": (H, BF), "k0": (TW, BF), "kb": (W16 * NS, BF),
     "iot": (C, F32), "sm": (192, F32), "tab": (J, BF), "cc": (J, BF),
-    "msk": (C, F32), "ha": (C, F32), "hb": (C, F32), "eq": (C, BF), "ea": (C, BF), "eb": (C, BF),
+    "msk": (H, F32), "wq": (WQ, F32), "wr": (C - 15, F32), "hb": (H, F32), "eq": (H, BF), "eb": (H, BF),
     "fl": (4 * C, BF), "ca": (W16 * H, BF), "cb": (W16 * H, BF), "sg": (3 * C, BF), "lha": (32, F32), "lhb": (32, F32),
-    "ii": (128, I32), "wa": (J, F32), "wb": (J, F32), "gap": (J, F32), "zp": (C + 32, F32), "zt": (TW, F32), "fp": (C + 32, BF), "ft": (TW, BF), "fs": (TW, BF),
+    "ii": (160, I32), "wa": (J, F32), "wb": (J, F32), "gap": (J, F32), "zp": (C + 32, F32), "zt": (TW, F32), "fp": (C + 32, BF), "ft": (TW, BF), "fs": (TW, BF),
     "f1": (W16 * NS, BF), "s1": (W16 * NS, BF), "fq": (3 * C, BF),
     "r1": (C, BF), "r2": (C, BF), "inv": (C, BF), "vni": (C, BF), "ks": (C, BF), "yb": (64, BF), "w9": (J, BF), "x9": (J, BF), "x2": (C, BF), "xx": (1024, BF),
     "w0": (WW, BF), "w1": (WW, BF), "wd": (C, BF),
@@ -39,7 +40,7 @@ _SB = {
 }
 _PART = {"tb_": ("wb", H, C)}
 for _b, _d, _names in (("sf", F32, "rs64 sp64 sq64 sr88 sb88 yy64 kw64 t164 t264 jw32"),
-                       ("lu", U16, "cl2 se18 l132 l284 lw32 lp32 la32 lv32 lb32 ly32 pk64")):
+                       ("lu", U16, "cl2 se24 l132 l284 lw32 lp32 la32 lx32 lv32 lb32 ly32 pk64")):
     _at = 0
     for _x in _names.split():
         _PART[_x[:2] + "_"] = (_b, _at, int(_x[2:]))
@@ -55,7 +56,7 @@ for _t in range(R):
 SCRATCH = {k: ("sbuf", [128, n], d) for k, (n, d) in _SB.items()}
 SCRATCH["ps"] = ("psum", [128, 4096], F32)
 SEMAPHORES = ["cp", "cv", "cs", "cg", "sent", "dx", "dz", "du", "dv", "dl", "dol", "doc", "dy", "m5_%d" % (R - 1)] + \
-    ["m%d_%d" % (m, t) for m in range(5) for t in range(R)]
+    ["m%d_%d" % (m, t) for m in range(5) for t in range(R)] + ["d%s%d" % (x, t) for x in "ab" for t in range(R)]
 
 ADD, SUB, MUL, MAX, MIN = AluOpType.add, AluOpType.subtract, AluOpType.mult, AluOpType.max, AluOpType.min
 GE, GT, EQ, NE, LT = AluOpType.is_ge, AluOpType.is_gt, AluOpType.is_equal, AluOpType.not_equal, AluOpType.is_lt
@@ -198,7 +199,7 @@ def rank_program(g, core, T, topo):
         return rec("v", lambda q: q.tensor_scalar(ap(out), ap(a), ap(s1), ap(s2), op0, op1), [a, s1, s2], [out])
 
     def scan(out, d0, d1, init, op0, op1):
-        return rec("v", lambda q: q.tensor_tensor_scan(ap(out), ap(d0), ap(d1), init, op0, op1), [d0, d1], [out])
+        return rec("v", lambda q: q.tensor_tensor_scan(ap(out), ap(d0), ap(d1), ap(init), op0, op1), [d0, d1, init], [out])
 
     def fill(out, c):
         return rec("v", lambda q: q.memset(ap(out), c), [], [out])
@@ -260,8 +261,8 @@ def rank_program(g, core, T, topo):
     dma("y", "dl", lambda: (ap(A("sw")), T.ws[:]), [], [A("sw")])
 
     ups = [1 if rank & STEP[t] else 0 for t in range(R)]
-    Q, P32, PAR, ODD, QHALF, KEEP, FAR, X1, X2, X3, X5, X6 = range(12)
-    SD, SM, SR, SH, SK, SS = 0, 2, 4, 6, 8, 10
+    Q, P32, PAR, ODD, QHALF, KEEP, FAR, X1, X2, X3, X5, X6, SUMS, P2, P4, P8 = range(16)
+    SD, SM, SR, SH, SK, SS = 0, 4, 8, 12, 14, 16
 
     def sel(k, up=0):
         k += 6 * up
@@ -269,10 +270,8 @@ def rank_program(g, core, T, topo):
 
     iota(A("pi", 0, 1), [[1, 1]], 0, 1)
     iota(A("upi"), [[-8, 2], [16, 8]], 8, 0)
-    iota(A("r16"), [[0, W16], [1, 16]], 0, 0)
     iota(A("sm", 8, 40), [[16, 32]], 0, 0)
-    iota(A("iot"), [[1, C]], 0, 0)
-    iota(A("one"), [[0, 128]], 1, 0)
+    iota(A("r16"), [[0, RUN], [1, 16]], 0, 0)
     p = A("pi", 0, 1)
     ts(A("pi", 1, 2), p, 15, AND)
     ts(A("pi", 2, 3), p, 31, AND)
@@ -293,13 +292,12 @@ def rank_program(g, core, T, topo):
             iota(v, [[0, v[2] - v[1]]], 0, 0)
 
     def later_constants():
-        iota(A("k0"), [[0, TW // 16], [64, 16]], 0, 0)
         zeros(A("yb"), *[A("pa%d" % t, 56, 64) for t in range(R)])
         zeros(A("et"))
         for b in range(4):
             out = A("et", 512 * b + b, 512 * (b + 1), 4)
             rec("g", lambda q, out=out: q.affine_select(ap(out), ap(A("one")), [[-1, 128]], EQ, 0.0, 0, 1), [A("one")], [out])
-        zeros(A("x2"), A("xx"), A("mm"), A("ew", 384, 512), A("ew", PW), A("rr%d" % (R - 1), 112),
+        zeros(A("x2"), A("mm", 0, 16), A("mm", C + 16), A("ew", 384, 512), A("ew", PW), A("rr%d" % (R - 1), 112),
               *[A(w, a, a + 16) for w in ("w0", "w1") for a in (OWN - 16, OWN + C)])
 
     def side_lists(up):
@@ -324,19 +322,16 @@ def rank_program(g, core, T, topo):
         copy(sel(SS, up), A("sm", 4, 6))
 
     def late_constants():
-        iota(A("sm", 112, 140), [[32, 14], [C, 2]], -C, 0)
-        iota(A("sm", 140, 168), [[32, 14], [0, 2]], -256, 0)
-        iota(A("sm", 88, 102), [[32, 14]], OWN - MID, 0)
-        for a, b, to, step in RUNS:
-            iota(A("sm", 40 + a // 32, 40 + b // 32), [[32 * step, (b - a) // 32]], to - MID, 0)
-            iota(A("sm", 56 + a // 32, 56 + b // 32), [[0, (b - a) // 32]], step, 0)
+        iota(A("iot"), [[1, C]], 0, 0)
+        iota(A("one"), [[0, 128]], 1, 0)
         zeros(A("zp", 0, 16), A("zp", C + 16), *[A("z%d" % t, a, a + 8) for t in range(R) for a in (32, 88)])
-        zeros(A("w9"), A("x9"))
         for l in (EV, ER):
             iota(A("w9", l, J, 16), [[0, 14], [1, 2], [0, 2]], 0, 0)
         zeros(A("rs_", 48, 64), A("fp", 0, 16), A("fp", C + 16))
         iota(A("sb_", 0, 84), [[RUN, 2], [0, RUN], [RUN, 3]], 2, 0)
         iota(A("kb"), [[0, 3 * W16], [64, RUN]], 0, 0)
+        iota(A("k0"), [[0, TW // 16], [64, 16]], 0, 0)
+        zeros(A("xx"))
 
     def fixed_lists():
         ts(col(X1), col(X1), float(C), MUL, col(X3), ADD)
@@ -350,53 +345,56 @@ def rank_program(g, core, T, topo):
         ts(t2(2, 2), A("jw_", 0, 2), 16.0, MUL)
         ts(col(X5), col(X5), col(PAR), MUL, col(X6), ADD)
         ts(t1(0, 2), A("sm", 8, 40, 16), col(X1), ADD, float(TW - 1), MIN)
+        yield
         ts(col(KEEP), col(Q), float(EN), EQ)
         ts(col(X2), col(Q), float(PL), EQ)
         tt(A("sm", 0, 2), t2(0, 2), t2(2, 2), ADD)
         ts(t1(2, 2), A("sm", 8, 10), 0.5, MUL, col(X5), ADD)
         copy(A("cl_"), t1(0, 2))
         tt(col(KEEP), col(KEEP), col(X2), ADD)
-        ts(col(X6), col(Q), float(EV), EQ)
+        yield
+        ts(col(SUMS), col(Q), float(EV), EQ)
         ts(t1(4, 2), t1(2, 2), 32.0, MUL, col(X3), ADD)
-        ts(A("ks"), A("r16"), 0.0, MUL, col(X6), ADD)
         ts(col(FAR), col(KEEP), -BIG, MUL, BIG, ADD)
-        ts(sel(SD), t1(4, 2), col(PAR), ADD)
-        ts(sel(SM), t1(4, 2), float(EV), ADD)
-        ts(sel(SR), t1(4, 2), float(ER), ADD)
+        ts(A("se_", SD, SD + 4, 2), t1(4, 2), col(PAR), ADD)
+        ts(A("se_", SM, SM + 4, 2), t1(4, 2), float(EV), ADD)
+        ts(A("se_", SR, SR + 4, 2), t1(4, 2), float(ER), ADD)
 
     def tables():
-        ts(A("sm", 72, 87), A("sm", 56, 71), col(P32), MUL)
-        ts(A("sm", 88, 102), A("sm", 88, 102), col(P32), ADD)
-        ts(A("sm", 112, 168), A("sm", 112, 168), col(P32), ADD)
-        yield
-        tt(A("sm", 72, 87), A("sm", 72, 87), A("sm", 40, 55), ADD)
+        times = {1: P32, 2: P2, 4: P4, 8: P8}
+
+        def put(name, at, step, a, b, k):
+            act(A(name, at, at + step * (b - a - 1) + 1, step), A("sm", a, b), FN.Identity, bias=col(times[k]))
+        iota(A("sm", 88, 102), [[32, 14]], OWN - MID, 0)
+        iota(A("sm", 140, 168), [[32, 14], [0, 2]], -256, 0)
+        for a, b, to, step in RUNS:
+            iota(A("sm", 40 + a // 32, 40 + b // 32), [[32 * step, (b - a) // 32]], to - MID, 0)
         for h in range(2):
-            copy(A("w9", 32 + 16 * h + HL, J, 64), A("sm", 88, 102))
-            copy(A("w9", 16 * h + HU, J, 64), A("sm", 88, 102))
-        y = A("sm", 112, 140)
-        ts(t1(0, W16), y, -256.0, MAX, 256.0, MIN)
-        ts(t1(32, W16), y, -384.0, MAX, 384.0, MIN)
-        ts(t2(32, W16), y, 4.0, MUL)
-        for h in range(2):
-            copy(A("w9", 16 * h + HL, J, 64), A("sm", 73, 87))
-            copy(A("w9", 32 + 16 * h + HU, J, 64), A("sm", 72, 86))
-        tt(t1(0, W16), t1(0, W16), t1(32, W16), ADD)
-        tt(t2(32, W16), t2(32, W16), t1(32, W16), SUB)
+            put("w9", 32 + 16 * h + HL, 64, 88, 102, 1)
+            put("w9", 16 * h + HU, 64, 88, 102, 1)
+            for at, first in ((16 * h + HL, 1), (32 + 16 * h + HU, 0)):
+                put("w9", at, 64, 40 + first, 52, 4)
+                put("w9", at + 64 * (12 - first), 64, 52, 54 + first, 8)
         for a in (JA, C + JE):
-            copy(A("x9", a, a // C * C + C, 16), A("sm", 140, 168))
-        turn(A("tab"), A("w9"))
-        tt(A("x9", EN, C, 16), t2(32, W16), t1(0, W16), SUB)
-        yield
-        turn(A("cc"), A("x9"))
-        for _ in side_lists(ups[0]):
-            yield
+            put("x9", a, 16, 140, 168, 1)
+        for h, a, b, k, first in ((0, 0, 2, 4, -768), (0, 2, 6, 2, -512), (0, 6, 14, 1, -256),
+                                  (1, 0, 8, 1, 0), (1, 8, 12, 2, 256), (1, 12, 14, 4, 512)):
+            iota(A("sm", 112 + 14 * h + a, 112 + 14 * h + b), [[32 * k, b - a]], first, 0)
+            put("x9", 32 * a + 16 * h + EN, 32, 112 + 14 * h + a, 112 + 14 * h + b, k)
 
     def run(x):
         for _ in x:
             pass
 
-    fixed_lists()
+    for name, k in ((P2, 2.0), (P4, 4.0), (P8, 8.0)):
+        ts(col(name), col(P32), k, MUL)
+    fill(A("w9"), 0.0)
+    fill(A("x9"), 0.0)
+    tables()
+    fixed = fixed_lists()
+    next(fixed)
     quant(A("qu"), A("su"), A("ub"))
+    quant(A("qt0", 0, H), A("st0", 0, H), A("x0", 0, J))
     rec("v", lambda q: q.tensor_copy(ap(A("qur")).bitcast(dt.uint32), ap(A("qu")).bitcast(dt.uint32).indirect(ap(A("upk")))),
         [A("qu"), A("upk")], [A("qur")])
     rec("s", lambda q: q.activation(ap(A("sur")), ap(IND(A("su"), A("upk"))), FN.Copy), [A("su"), A("upk")], [A("sur")])
@@ -417,16 +415,24 @@ def rank_program(g, core, T, topo):
         return (src[0], src[1] + a, src[1] + b, 1)
 
     def rivals(src, c, w):
-        a = 16 * c + 16 + 16 * c // w * w
-        return A(src, a, a + w), 16 * c < w
+        if w == C:
+            return A("wq", 16 * c + 1, 16 * c + 1 + w), True
+        if c < RUN:
+            return A("wr", 16 * c + 1, 16 * c + 1 + w), True
+        return A("wb", 16 * c + 16 + H, 16 * c + 16 + C), False
+
+    def mine(h, c):
+        if h is None:
+            return A("wq", C + 16 * c, C + 16 * c + 1)
+        return A("wr", H + 16 * c, H + 16 * c + 1) if c < RUN else A("hb", 16 * c - H + 15, 16 * c - H + 16)
 
     def vector_counts(src, h, out, blocks, w):
         last, m = None, w // 2
-        for n, c in enumerate(list(range(blocks)) + [None]):
+        for n, c in enumerate(list(blocks) + [None]):
             f = C * (n % 4)
             if c is not None:
                 row, first = rivals(src, c, w)
-                ts(A("fl", f, f + w), row, A(h, 16 * c + 15, 16 * c + 16), GE if first else GT, 0.5, SUB)
+                ts(A("fl", f, f + w), row, mine(h, c), GE if first else GT, 0.5, SUB)
             yield
             if last is not None:
                 scan(A(out, last[1] * m, last[1] * m + m), A("fl", last[0], last[0] + m), A("fl", last[0] + m, last[0] + w),
@@ -441,28 +447,18 @@ def rank_program(g, core, T, topo):
 
     def scalar_counts(src, h, lh, out, blocks, w):
         last = None
-        for n, c in enumerate(list(range(W16 - blocks, W16)) + [None]):
+        for n, c in enumerate([c for a, b in blocks for c in range(a, b)] + [None]):
             f = C * (n % 3)
             if c is not None:
-                act(A("sg", f, f + w), rivals(src, c, w)[0], FN.Sign, bias=A(h, 16 * c + 15, 16 * c + 16), scale=-1.0)
+                act(A("sg", f, f + w), rivals(src, c, w)[0], FN.Sign, bias=mine(h, c), scale=-1.0)
             if last is not None:
                 a = A("sg", last[0], last[0] + w)
                 act(a, a, FN.Sign, bias=0.5 if rivals(src, last[1], w)[1] else -0.5, scale=-1.0, acc=A(lh, last[1], last[1] + 1))
             last = (f, c)
-        a, m = W16 - blocks, w // 2
-        act(A(out, a * m + m - 1, W16 * m, m), A(lh, a, W16), FN.Copy, scale=0.5)
-
-    def own_scores(src, h):
-        tt(A("msk"), src, A("md"), MUL)
-        yield
-        scan(A(h), A("kz"), A("msk"), 0.0, MUL, ADD)
-        yield
-
-    def ties(src, h, out):
-        tt(A("eq"), src, A(h), EQ)
-        yield
-        scan(A(out), A("kz"), A("eq"), 0.0, MUL, ADD)
-        yield
+            yield
+        m = w // 2
+        for a, b in blocks:
+            act(A(out, a * m + m - 1, b * m, m), A(lh, a, b), FN.Copy, scale=0.5)
 
     def unpack(codes, scales, at, step):
         for b in range(4):
@@ -476,8 +472,8 @@ def rank_program(g, core, T, topo):
         turn(out, A(via, 32 - 32 * to, 64 - 32 * to))
         yield
 
-    def lane(h, l):
-        return A("xx", 16 + 16 * h + l, 16 + C, 32)
+    def lane(h, l, a=0, b=C):
+        return A("xx", 16 + a + 16 * h + l, 16 + b, 32)
 
     def cols(name, s):
         return A("q" + name, H * s, H * s + H), A("s" + name, H * s, H * s + H)
@@ -485,30 +481,42 @@ def rank_program(g, core, T, topo):
     SBV, SBS, SAV, SAS = [PS(4, H), PS(6, H)], [PS(5, H), PS(7, H)], PS(0), PS(1)
 
     def scores_b(t, s):
-        mm(SBS[s], *stat("ur", 0), *cols("t%d" % t, s))
-        mm(SBV[s], *stat("ur", 0), *cols("t%d" % t, s))
+        for out in (SBV[s], SBS[s]) if s else (SBS[s], SBV[s]):
+            mm(out, *stat("ur", 0), *cols("t%d" % t, s))
 
     def store(s):
         codes, scales = cols("t%d" % R, s)
         mm(PS(4 + s, H), A("qv"), A("sv"), codes, scales)
         dma("y", "doc", lambda: (T.oc[:, J * s:J * s + J], u8(codes)), [codes], [])
 
-    quant(*cols("t0", 0), A("x0", 0, J))
+    def rows_b(s):
+        act(A("gap", H * s, H * s + H), SBS[s], FN.Abs, bias=TINY, scale=ULP)
+        act(A("tb_", H * s, H * s + H), SBS[s], FN.Copy)
+
+    def early_b(t):
+        tt(A("wb", 0, H), SBV[0], A("gap", 0, H), SUB)
+        for q in range(16):
+            dma("y", "db%d" % t, lambda q=q: (T.wr[q::16, :], T.wb[q::16, q:q + C - 15]), [half("wb", 0)], [] if q else [A("wr")])
+
     scores_b(0, 0)
+    rows_b(0)
     quant(*cols("t0", 1), A("x0", J, 2 * J))
+    next(fixed)
+    early_b(0)
+    run(fixed)
     for t in range(R):
         peer = T.cores[rank ^ STEP[t]]
         up = ups[t]
         before = GE if up else GT
         z, rb, rbp, pa, rr = ["%s%d" % (n, t) for n in ("z", "rb", "rbp", "pa", "rr")]
         QT = (A("qt%d" % t), A("st%d" % t))
-        exchange(peer, 3, t, ["qt", "st"])
         scores_b(t, 1)
         mm(SAS, *stat("ur", 1), *QT)
         mm(SAV, *stat("ur", 1), *QT)
 
         def sort_b():
-            tt(t1(0, W16), A("cb", H // 2 - 1, W16 * H // 2, H // 2), A("eb", 15, C, 16), SUB)
+            ts(t1(0, RUN), A("cb", H // 2 - 1, RUN * H // 2, H // 2), 1.0, SUB)
+            tt(t1(RUN, RUN), A("cb", (RUN + 1) * H // 2 - 1, W16 * H // 2, H // 2), A("eb", 15, H, 16), SUB)
             yield
             for r in range(2):
                 ts(A("l1_", RUN * r, RUN * r + RUN), t1(RUN * r, RUN), float(H // 2 + H * r), ADD)
@@ -540,38 +548,34 @@ def rank_program(g, core, T, topo):
             yield
             turn(A("sp_", 0, 64), A("sq_", 0, 64))
             yield
-            fill(A("sp_", 1 + RUN, 64, RUN), -FARTHEST)
-            yield
             for c in range(W16):
                 a = 2 + c // RUN * RUN
-                ts(A("f1", NS * c, NS * c + NS), A("sp_", a, a + NS), A("hb", 16 * c + 15, 16 * c + 16), before)
+                ts(A("f1", NS * c, NS * c + NS), A("sp_", a, a + NS), mine("hb", c), before)
+            for a in (0, RUN * NS):
+                scan(A("s1", a, a + RUN * NS), A("kb", a, a + RUN * NS), A("f1", a, a + RUN * NS), 0.0, MIN, ADD)
             yield
-            scan(A("s1"), A("kb"), A("f1"), 0.0, MIN, ADD)
-            yield
-            found = [A("s1", RUN * s + RUN - 1, W16 * NS, NS) for s in range(3)]
-            tt(A("sr_", 0, 84), A("s1", RUN - 1, W16 * NS, RUN), A("sb_", 0, 84), ADD)
+            found = [A("s1", RUN * s + RUN - 2, W16 * NS, NS) for s in range(3)]
+            tt(A("sr_", 0, 84), A("s1", RUN - 2, W16 * NS, RUN), A("sb_", 0, 84), ADD)
             tt(t2(0, W16), found[0], found[1], ADD)
-            yield
             for s in range(3):
                 copy(A("l2_", W16 * s, W16 * s + W16), A("sr_", s, 84, 3))
             tt(t2(0, W16), t2(0, W16), found[2], ADD)
-            yield
             win = A(z, 32, 96)
             tt(half("fq", 0), IND(win, A("l2_", 0, W16)), A("tb_"), before)
             ts(t2(0, W16), t2(0, W16), 16.0, MUL)
-            yield
             tt(half("fq", C), IND(win, A("l2_", W16, 2 * W16)), A("tb_"), before)
             tt(A("rs_", 32, 32 + W16), t2(0, W16), A("rs_", 0, W16), ADD)
-            yield
-            tt(half("fq", 2 * C), IND(win, A("l2_", 2 * W16, 3 * W16)), A("tb_"), before)
             tt(half("fq", 0), half("fq", 0), half("fq", C), ADD)
-            yield
-            tt(half("fp", 16), half("fq", 0), half("fq", 2 * C), ADD)
-            yield
-            turn(half("ft", 0), half("fp", 16))
+            for a in (0, H):
+                tt(A("fq", 2 * C + a, 2 * C + a + H), IND(win, A("l2_", 2 * W16 + a // 16, 2 * W16 + a // 16 + RUN)),
+                   A("tb_", a, a + H), before)
+            for a in (0, H):
+                tt(A("fp", 16 + a, 16 + a + H), A("fq", a, a + H), A("fq", 2 * C + a, 2 * C + a + H), ADD)
+            for a in (0, H):
+                turn(A("ft", a, a + H), A("fp", 16 + a, 16 + a + H))
             turn(A("ft", C, TW), A("fp"))
-            yield
-            scan(A("fs"), A("k0"), A("ft"), 0.0, MIN, ADD)
+            scan(half("fs", 0), half("k0", 0), half("ft", 0), 0.0, MIN, ADD)
+            scan(A("fs", C), A("k0", C), A("ft", C), 0.0, MIN, ADD)
             yield
             tt(A("kw_", 0, 32), IND(A("fs"), A("cl_")), A("rs_", 32, 64), ADD)
             yield
@@ -580,60 +584,53 @@ def rank_program(g, core, T, topo):
             copy(A(rb, 0, W16), t2(0, W16))
             exchange(peer, 2, t, ["rb"], W16)
 
-        for s in range(2):
-            act(A("gap", H * s, H * s + H), SBS[s], FN.Abs, bias=TINY, scale=ULP)
-            act(A("tb_", H * s, H * s + H), SBS[s], FN.Copy)
+        rows_b(1)
         act(half("gap", C), SAS, FN.Abs, bias=TINY, scale=ULP)
-        act(half("wa", C), SAS, FN.Copy)
-        tt(A("msk", 0, H), SBV[0], A("md", 0, H), MUL)
-        tt(A("wb", 0, H), SBV[0], A("gap", 0, H), SUB)
-        tt(A("msk", H, C), SBV[1], A("md", H, C), MUL)
-        tt(A("wb", 3 * H, J), SBV[1], A("gap", H, C), ADD)
+        tt(A("msk"), SBV[1], A("md"), MUL)
         scan(A("hb"), A("kz"), A("msk"), 0.0, MUL, ADD)
-        scalar_counts("wb", "hb", "lhb", "cb", SC_B, H)
-
-        def moved_a():
-            tt(half("wa", 0), SAV, half("gap", C), SUB)
-            yield
-
-        def ties_b():
-            for s in range(2):
-                tt(A("eq", H * s, H * s + H), SBV[s], A("hb", H * s, H * s + H), EQ)
-            yield
-            scan(A("eb"), A("kz"), A("eq"), 0.0, MUL, ADD)
-            yield
-        side = [own_scores(SAV, "ha"), moved_a(), ties_b()]
+        tt(A("wb", 3 * H, J), SBV[1], A("gap", H, C), ADD)
+        x = scalar_counts("wb", "hb", "lhb", "cb", [(RUN, RUN + SC_B[1]), (0, SC_B[0])], H)
+        next(x)
+        act(half("wa", C), SAS, FN.Copy)
+        run(x)
+        counts = vector_counts("wb", "hb", "cb", list(range(RUN + SC_B[1], W16)) + list(range(SC_B[0], RUN)), H)
+        tt(A("eq"), SBV[1], A("hb"), EQ)
+        next(counts)
+        tt(half("wa", 0), SAV, half("gap", C), SUB)
+        for q in range(16):
+            dma("y", "da%d" % t, lambda q=q: (T.wq[q::16, :], T.wa[q::16, q:q + WQ]), [A("wa")], [] if q else [A("wq")])
+        scan(A("eb"), A("kz"), A("eq"), 0.0, MUL, ADD)
         if t == 0:
             late_constants()
-        side = chain(*side)
-        weave(vector_counts("wb", "hb", "cb", W16 - SC_B, H), side, 1)
-        run(side)
-        va = W16 - SC_A[t]
-        scalar_counts("wa", "ha", "lha", "ca", W16 - va, C)
-        counts = vector_counts("wa", "ha", "ca", va, C)
+        run(counts)
+        run(scalar_counts("wq", None, "lha", "ca", [(0, SC_A[t])], C))
+        counts = vector_counts("wq", None, "ca", range(SC_A[t], W16), C)
+        next(counts)
         weave(sort_b(), counts, SORT_EVERY)
         if t == 0:
             later_constants()
-        weave(chain(ties(SAV, "ha", "ea"), tables() if t == 0 else idle(SEARCH_AT)), counts, 1)
+            turn(A("tab"), A("w9"))
+            turn(A("cc"), A("x9"))
+        weave(idle(SEARCH_AT - (2 if t == 0 else 0)), counts, 1)
         weave(search(), counts, SEARCH_EVERY)
+        if t == 0:
+            weave(side_lists(up), counts, 1)
         run(counts)
         if t == 0:
             act(A("w9"), A("tab"), FN.Copy, scale=0.0)
-        theirs = chain(unpack(*QT, 0, PW), unpack(A("qtp%d" % t), A("stp%d" % t), DP, C))
+            act(A("ks"), A("iot"), FN.Identity, bias=col(SUMS), scale=0.0)
+        own = unpack(*QT, 0, PW)
 
-        tt(A(pa, 32, 32 + W16), A("ca", H - 1, W16 * H, H), A("ea", 15, C, 16), SUB)
-        copy(A("kw_", 32, 32 + W16), A(rbp, 0, W16))
-        x = cross(A(pa, 0, 32), A(pa, 32, 64), up, "yb")
-        next(x)
-        copy(I(0, 32), IND(A("kw_"), sel(SH, up)))
-        next(x)
+        ts(A(pa, 32, 32 + W16), A("ca", H - 1, W16 * H, H), 1.0, SUB)
+        run(cross(A(pa, 0, 32), A(pa, 32, 64), up, "yb"))
         exchange(peer, 1, t, [(A(pa, 0, 32), A(pa, 64, 96))])
+        exchange(peer, 3, t, ["qt", "st"])
+        copy(A("kw_", 32, 32 + W16), A(rbp, 0, W16))
+        copy(I(0, 32), IND(A("kw_"), sel(SH, up)))
         ts(I(32, 32), I(0, 32), 1, AND)
         ts(I(64, 32), I(0, 32), 1, SHR, 31, AND)
-        ts(I(96, 32), I(0, 32), 1, SHR)
         ts(t2(0, 32), I(32, 32), 31.0, MUL)
         tt(t2(32, 32), I(0, 32), I(64, 32), SUB)
-        copy(A("lp_"), I(96, 32))
         tt(t1(32, 32), t2(0, 32), t2(32, 32), ADD)
         copy(A("lw_"), t1(32, 32))
         lw = A("lw_", 0, W16)
@@ -641,56 +638,102 @@ def rank_program(g, core, T, topo):
         if t == 0:
             quant(A("qe"), A("se"), A("et"))
 
-        la = A("la_", 0, W16)
+        parts = ((0, GL), (GL, C))
+        short = ((0, 16), (16, 32))
         ts(A("la_"), IND(A(pa, 32, 96), sel(SH, up)), float(H), ADD)
-        copy(IND(A("inv"), la), A("r1"))
-        act(A("vni", 1, C, 2), A("inv", 0, C, 2), FN.Copy)
-        copy(A("vni", 0, C, 2), A("inv", 1, C, 2))
-        tt(A("r2"), IND(A("vni"), la), half("cc", C), ADD)
+        ts(I(96, 32), I(0, 32), 1, SHR)
+        copy(IND(A("inv"), A("la_", 0, W16)), A("r1"))
+        copy(A("lp_"), I(96, 32))
+        for e in range(2):
+            copy(A("vni", e, C, 2), A("inv", 1 - e, C, 2))
+        tt(A("r2"), IND(A("vni"), A("la_", 0, W16)), half("cc", C), ADD)
         copy(IND(A("w9"), lw), A("r2"))
-        turn(A("x9"), A("w9"))
-        for l in (HL, HU, EN):
-            tt(A("xx", 16 + l, 16 + C, 16), A("x9", l, J, 32), A("x9", 16 + l, J, 32), ADD)
+        for a, b in parts:
+            turn(A("x9", 2 * a, 2 * b), A("w9", 2 * a, 2 * b))
+
+        def join(l, a, b):
+            tt(A("xx", 16 + a + l, 16 + b, 16), A("x9", 2 * a + l, 2 * b, 32), A("x9", 2 * a + 16 + l, 2 * b, 32), ADD)
+        join(HL, 0, GL)
+        join(HU, 0, C)
+        join(EN, 0, C)
         for h in range(2):
             a = 32 * (1 - h) + EN
             tt(lane(h, PL), A("x9", a, J, 64), A("x9", a + 16, J, 64), ADD)
-        turn(half("w0", OWN), half("xx", 16))
+        join(HL, GL, C)
+        turn(A("w0", OWN, OWN + GL), A("xx", 16, 16 + GL))
+        turn(A("w0", OWN + GL, OWN + C), A("xx", 16 + GL, 16 + C))
 
-        parts = ((0, GL), (GL, C))
         for k in range(STEPS):
             wc, wn, pk = "w%d" % (k % 2), "w%d" % (1 - k % 2), 32 * (k % 2)
+
+            def other(n):
+                a, b, to, step = RUNS[n]
+                turn(A(wc, to, to + step * (b - a), step), A("xx", a, b))
+
+            def offsets(n):
+                ts(A("pk_", pk + 16 * n, pk + 16 * n + 16), IND(A("xx"), A("se_", SD + 2 * n, SD + 2 * n + 1)), float(MID), ADD)
             for a, b in parts:
                 act(A("wd", a, b), A(wc, OWN + a, OWN + b), FN.Identity, bias=col(FAR), scale=col(KEEP))
-            next(theirs, None)
+            next(own, None)
+            if k == 0:
+                other(0)
             turn(A("xx", 496, 976), A(wc, OWN - 16, OWN + C + 16))
             if k:
                 turn(A("xx", 16 + GL, 16 + C), A(wc, OWN + GL, OWN + C))
-            for n, (a, b, to, step) in enumerate(RUNS):
-                turn(A(wc, to, to + step * (b - a), step), A("xx", a, b))
-                if n == 0:
-                    ts(A("pk_", pk, pk + 32), IND(A("xx"), sel(SD)), float(MID), ADD)
+                other(0)
+            other(1)
+            offsets(0)
+            other(2)
+            offsets(1)
             for a, b in parts:
                 tt(A(wn, OWN + a, OWN + b), IND(A(wc), A("pk_", pk + a // 16, pk + b // 16)), A("wd", a, b), MIN)
             turn(A("xx", 16, 16 + GL), A(wn, OWN, OWN + GL))
         turn(A("xx", 16 + GL, 16 + C), A(wn, OWN + GL, OWN + C))
 
-        tt(t1(0, 14), lane(0, PL), lane(1, EN), MIN)
-        tt(t1(14, 14), lane(0, EN), lane(1, PL), MIN)
-        for a in (EV, ER, 16 + EV, 16 + ER):
-            tt(A("x2", a, C, 32), t1(0, 14), t1(14, 14), LT)
-        turn(A("inv"), A("x2"))
-        tt(A("red"), IND(A("inv"), A("lp_", 0, W16)), A("r1"), NE)
+        run(unpack(A("qtp%d" % t), A("stp%d" % t), DP, C))
+
+        for a, b in parts:
+            tt(t1(a // 32, (b - a) // 32), lane(0, PL, a, b), lane(1, EN, a, b), MIN)
+            tt(t1(16 + a // 32, (b - a) // 32), lane(0, EN, a, b), lane(1, PL, a, b), MIN)
+
+        def flags(l, a, b):
+            tt(A("x2", a + l, b, 32), t1(a // 32, (b - a) // 32), t1(16 + a // 32, (b - a) // 32), LT)
+        flags(EV, 0, GL)
+        for l in (ER, 16 + EV, 16 + ER):
+            flags(l, 0, C)
+        flags(EV, GL, C)
+        for a, b in parts:
+            turn(A("inv", a, b), A("x2", a, b))
+        thirds = ((0, 160), (160, 320), (320, C))
+
+        def colour(n):
+            a, b = thirds[n]
+            tt(A("red", a, b), IND(A("inv"), A("lp_", a // 16, b // 16)), A("r1", a, b), NE)
+
+        def number(n):
+            a, b = thirds[n]
+            scan(A("mm", 16 + a, 16 + b), A("ks", a, b), A("red", a, b), A("mm", 15 + a, 16 + a), MUL, ADD)
+
+        def turned(n):
+            a, b = thirds[n]
+            turn(A("xx", 16 + a, 16 + b), A("mm", 16 + a, 16 + b))
+        for f, n in ((colour, 0), (colour, 1), (number, 0), (colour, 2), (number, 1), (turned, 0), (number, 2), (turned, 1)):
+            f(n)
         if t < R - 1:
             act(A("w9"), A("tab"), FN.Copy, scale=0.0)
-        scan(half("mm", 16), A("ks"), A("red"), 0.0, MUL, ADD)
-        turn(half("xx", 16), half("mm", 16))
         turn(A("xx", 496, 976), A("mm"))
-        ts(t1(0, 32), IND(A("xx"), sel(SM)), 8.0, MUL, 504.0, ADD)
-        tt(t1(32, 32), IND(A("xx"), sel(SR)), t1(0, 32), MUL)
-        tt(t2(0, 32), t1(32, 32), A("jw_"), MAX)
-        copy(A("lv_"), t2(0, 32))
-        ts(A("x3", C, C + 32), t2(0, 32), 256.0, SUB)
+        turned(2)
+        for n, (a, b) in enumerate(short):
+            ts(t1(a, 16), IND(A("xx"), A("se_", SM + 2 * n, SM + 2 * n + 1)), 8.0, MUL, 504.0, ADD)
+        for n, (a, b) in enumerate(short):
+            tt(t1(32 + a, 16), IND(A("xx"), A("se_", SR + 2 * n, SR + 2 * n + 1)), t1(a, 16), MUL)
+        for a, b in short:
+            tt(t2(a, 16), t1(32 + a, 16), A("jw_", a, b), MAX)
+        for a, b in short:
+            copy(A("lv_", a, b), t2(a, 16))
+        ts(A("x3", C, C + 16), t2(0, 16), 256.0, SUB)
         copy(IND(A("ew", 0, PW), A("lv_", 0, W16)), A("r2"))
+        ts(A("x3", C + 16, C + 32), t2(16, 16), 256.0, SUB)
         turn(A("x3", 0, H), A("ew", 512, PW, 8))
         a = 640 - 256 * up
         turn(A("x3", H, C), A("ew", a, a + 8 * H, 8))
@@ -705,53 +748,62 @@ def rank_program(g, core, T, topo):
                 run(side_lists(ups[1]))
         ts(A("lb_"), IND(A(rr, 0, 64), sel(SH, up)), 256.0, ADD)
 
+        for b in range(1, 4):
+            act(A("bh", H * b, H * b + H), IND(half("dw", DP + C * b), A("lb_", 0, RUN)), FN.Copy)
+        x = cross(A("x3", C + 32, C + 64), A(rr, 32, 64), 1 - up, "yb")
+        next(x)
+        copy(A("bh", 0, H), IND(half("dw", DP), A("lb_", 0, RUN)))
+        next(x)
         for b in range(4):
-            act(A("bh", H * b, H * b + H), IND(half("dw", DP + C * b), A("lb_", 0, 14)), FN.Copy)
-        run(cross(A("x3", C + 32, C + 64), A(rr, 32, 64), 1 - up, "yb"))
-        for b in range(4):
-            tt(A("bt", b, 4 * H, 4), IND(half("dw", DP + C * b), A("lb_", 14, W16)), A("bh", H * b, H * b + H), ADD)
+            tt(A("bt", b, 4 * H, 4), IND(half("dw", DP + C * b), A("lb_", RUN, W16)), A("bh", H * b, H * b + H), ADD)
+        ts(A("ly_"), IND(A("x3", C, C + 64), sel(SH, up)), 256.0, ADD)
         quant(A("qb"), A("sq"), A("bt"))
         for b in range(4):
             mm(PS(b, H), *stat("e", b), A("qb"), A("sq"))
-        ts(A("ly_"), IND(A("x3", C, C + 64), sel(SH, up)), 256.0, ADD)
 
         def pick(b, s):
             a = PW * b
-            came = A("dw", a + 512, a + PW, 8)
             win, out = IND(A("dw", a, a + PW), A("ly_", RUN * s, RUN * s + RUN)), A("yt", J * s + b, J * s + J, 4)
             if b % 2 == 0:
-                if s == 0:
-                    ts(came, PS(b, H), 0.5, MUL)
                 ts(out, win, 2.0, MUL)
             else:
-                if s == 0:
-                    act(came, PS(b, H), FN.Copy, scale=0.5)
                 act(out, win, FN.Copy, scale=2.0)
 
         def products(s, order):
             for name, b in order:
                 mm(PS(b + (4 if name == "w" else 0), H), *stat(name, b), *cols("z", s))
 
+        for b in range(4):
+            came = A("dw", PW * b + 512, PW * b + PW, 8)
+            if b % 2 == 0:
+                ts(came, PS(b, H), 0.5, MUL)
+            else:
+                act(came, PS(b, H), FN.Copy, scale=0.5)
+
         for b, s in ((0, 0), (1, 0), (2, 0), (3, 0), (0, 1), (1, 1), (3, 1)):
             pick(b, s)
         quant(*cols("z", 0), A("yt", 0, J))
         products(0, [("w", 0), ("e", 0), ("w", 1), ("e", 1), ("w", 2), ("e", 2), ("w", 3), ("e", 3)])
         pick(2, 1)
-        quant(*cols("z", 1), A("yt", J, 2 * J))
-        if t == R - 1:
-            ts(A("lv_"), IND(A(rr, 64, 128), sel(SH, up)), 256.0, ADD)
         for s in range(2):
             for b in range(4):
                 rl = A("rl", C * b + H * s, C * b + H * s + H)
-                act(rl, PS(4 + b, H), FN.Relu, scale=0.03125)
+                if (s, b) == (0, 0):
+                    ts(rl, PS(4, H), 0.0, MAX, 0.03125, MUL)
+                    quant(*cols("z", 1), A("yt", J, 2 * J))
+                else:
+                    act(rl, PS(4 + b, H), FN.Relu, scale=0.03125)
                 tt(A("xt", J * s + b, J * s + J, 4), PS(b, H), rl, ADD)
                 if s == 0:
                     products(1, [("w", b), ("e", b)])
                 if (s, b) == (1, 0):
                     quant(*cols("t%d" % (t + 1), 0), A("xt", 0, J))
+                if (s, b) == (1, 1) and t < R - 1:
+                    scores_b(t + 1, 0)
         if t < R - 1:
-            scores_b(t + 1, 0)
+            rows_b(0)
         else:
+            ts(A("lv_"), IND(A(rr, 64, 128), sel(SH, up)), 256.0, ADD)
             act(A("eo"), IND(A("iot"), A("lv_", 0, RUN)), FN.Copy)
             for k in range(8):
                 dma("y", "dol", lambda k=k: (T.ol[k:k + 1, :], T.eo[16 * k:16 * k + 1, :]), [A("eo")], [])
@@ -759,6 +811,8 @@ def rank_program(g, core, T, topo):
             act(A("yo", 0, H), PS(4, H), FN.Copy)
             dma("s", "dy", lambda: (T.y[:, 0:H], ap(A("yo", 0, H))), [A("yo", 0, H)], [])
         quant(*cols("t%d" % (t + 1), 1), A("xt", J, 2 * J))
+        if t < R - 1:
+            early_b(t + 1)
 
     store(1)
     for k in range(4):

@@ -11,8 +11,8 @@ WQ = J - 15
 TW = C + C + 32
 PW = 2304
 DP = 4 * PW
-SC_B, SC_A = (5, 5), (19, 18, 18)
-SORT_EVERY, SEARCH_AT, SEARCH_EVERY = 1, 3, 3
+SC_B, SC_A = (5, 4), (19, 18, 18)
+SORT_EVERY, SEARCH_AT, SEARCH_EVERY = 1, 2, 1
 MID, OWN, WW = 1024, 784, 2816
 RUNS = ((0, 192, 0, 4), (192, 384, 1280, 4), (384, 480, 2048, 8))
 GL = 256
@@ -22,15 +22,15 @@ HL, HU, EN, PL, JA, JE, EV, ER = range(8)
 F32, BF, I32, U16, X4, U8 = "float32", "bfloat16", "int32", "uint16", "float8_e4m3fn_x4", "uint8"
 
 _SB = {
-    "x0": (4 * C, BF), "ub": (512, BF), "vb": (512, BF), "xt": (4 * C, BF), "yt": (4 * C, BF), "bt": (4 * H, BF),
+    "x0": (4 * C, BF), "ub": (512, BF), "vb": (512, BF), "xt": (4 * C, BF), "yt": (4 * C, BF), "bt": (1024, BF),
     "qu": (128, X4), "su": (128, U8), "qur": (256, X4), "sur": (256, U8), "qv": (128, X4), "sv": (128, U8),
     "qw": (512, X4), "sw": (512, U8), "qe": (512, X4), "se": (512, U8), "et": (2048, BF), "one": (128, BF),
-    "qz": (C, X4), "sz": (C, U8), "qb": (H, X4), "sq": (H, U8), "qt%d" % R: (C, X4), "st%d" % R: (C, U8),
+    "qz": (C, X4), "sz": (C, U8), "qb": (256, X4), "sq": (256, U8), "qt%d" % R: (C, X4), "st%d" % R: (C, U8),
     "pi": (16, I32), "cf": (32, F32), "upi": (16, I32), "upk": (16, U16),
     "r16": (H, BF), "md": (H, BF), "kz": (H, BF), "k0": (TW, BF), "kb": (W16 * NS, BF),
     "iot": (C, F32), "sm": (192, F32), "tab": (J, BF), "cc": (J, BF),
     "msk": (H, F32), "wq": (WQ, F32), "wr": (C - 15, F32), "hb": (H, F32), "eq": (H, BF), "eb": (H, BF),
-    "fl": (4 * C, BF), "ca": (W16 * H, BF), "cb": (W16 * H, BF), "sg": (3 * C, BF), "lha": (32, F32), "lhb": (32, F32),
+    "fl": (4 * C, BF), "ca": (32 * H, BF), "cb": (W16 * H // 2, BF), "sg": (3 * C, BF), "lha": (32, F32), "lhb": (32, F32),
     "ii": (160, I32), "wa": (J, F32), "wb": (J, F32), "gap": (J, F32), "zp": (C + 32, F32), "zt": (TW, F32), "fp": (C + 32, BF), "ft": (TW, BF), "fs": (TW, BF),
     "f1": (W16 * NS, BF), "s1": (W16 * NS, BF), "fq": (3 * C, BF),
     "r1": (C, BF), "r2": (C, BF), "inv": (C, BF), "vni": (C, BF), "ks": (C, BF), "yb": (64, BF), "w9": (J, BF), "x9": (J, BF), "x2": (C, BF), "xx": (1024, BF),
@@ -40,7 +40,7 @@ _SB = {
 }
 _PART = {"tb_": ("wb", H, C)}
 for _b, _d, _names in (("sf", F32, "rs64 sp64 sq64 sr88 sb88 yy64 kw64 t164 t264 jw32"),
-                       ("lu", U16, "cl2 se24 l132 l284 lw32 lp32 la32 lx32 lv32 lb32 ly32 pk64")):
+                       ("lu", U16, "cl2 cx2 se24 l132 l284 lw32 lp32 la32 lx32 lv32 lb32 ly32 pk64")):
     _at = 0
     for _x in _names.split():
         _PART[_x[:2] + "_"] = (_b, _at, int(_x[2:]))
@@ -56,7 +56,7 @@ for _t in range(R):
 SCRATCH = {k: ("sbuf", [128, n], d) for k, (n, d) in _SB.items()}
 SCRATCH["ps"] = ("psum", [128, 4096], F32)
 SEMAPHORES = ["cp", "cv", "cs", "cg", "sent", "dx", "dz", "du", "dv", "dl", "dol", "doc", "dy", "m5_%d" % (R - 1)] + \
-    ["m%d_%d" % (m, t) for m in range(5) for t in range(R)] + ["d%s%d" % (x, t) for x in "ab" for t in range(R)]
+    ["m%d_%d" % (m, t) for m in (0, 1, 2, 3, 4, 6) for t in range(R)] + ["d%s%d" % (x, t) for x in "ab" for t in range(R)]
 
 ADD, SUB, MUL, MAX, MIN = AluOpType.add, AluOpType.subtract, AluOpType.mult, AluOpType.max, AluOpType.min
 GE, GT, EQ, NE, LT = AluOpType.is_ge, AluOpType.is_gt, AluOpType.is_equal, AluOpType.not_equal, AluOpType.is_lt
@@ -292,7 +292,8 @@ def rank_program(g, core, T, topo):
             iota(v, [[0, v[2] - v[1]]], 0, 0)
 
     def later_constants():
-        zeros(A("yb"), *[A("pa%d" % t, 56, 64) for t in range(R)])
+        zeros(A("yb"), A("bt", 4 * H))
+        iota(A("ca", (W16 + 1) * H - 1, 32 * H, H), [[0, 32 - W16]], 0, 0)
         zeros(A("et"))
         for b in range(4):
             out = A("et", 512 * b + b, 512 * (b + 1), 4)
@@ -326,7 +327,7 @@ def rank_program(g, core, T, topo):
         iota(A("one"), [[0, 128]], 1, 0)
         zeros(A("zp", 0, 16), A("zp", C + 16), *[A("z%d" % t, a, a + 8) for t in range(R) for a in (32, 88)])
         for l in (EV, ER):
-            iota(A("w9", l, J, 16), [[0, 14], [1, 2], [0, 2]], 0, 0)
+            iota(A("w9", l, J, 16), [[1, 2], [0, W16]], 0, 0)
         zeros(A("rs_", 48, 64), A("fp", 0, 16), A("fp", C + 16))
         iota(A("sb_", 0, 84), [[RUN, 2], [0, RUN], [RUN, 3]], 2, 0)
         iota(A("kb"), [[0, 3 * W16], [64, RUN]], 0, 0)
@@ -350,8 +351,10 @@ def rank_program(g, core, T, topo):
         ts(col(X2), col(Q), float(PL), EQ)
         tt(A("sm", 0, 2), t2(0, 2), t2(2, 2), ADD)
         ts(t1(2, 2), A("sm", 8, 10), 0.5, MUL, col(X5), ADD)
+        ts(col(X6), col(PAR), -32.0, MUL, 16.0, ADD)
         copy(A("cl_"), t1(0, 2))
         tt(col(KEEP), col(KEEP), col(X2), ADD)
+        ts(A("cx_"), t1(0, 2), col(X6), ADD, float(TW - 1), MIN)
         yield
         ts(col(SUMS), col(Q), float(EV), EQ)
         ts(t1(4, 2), t1(2, 2), 32.0, MUL, col(X3), ADD)
@@ -370,11 +373,11 @@ def rank_program(g, core, T, topo):
         for a, b, to, step in RUNS:
             iota(A("sm", 40 + a // 32, 40 + b // 32), [[32 * step, (b - a) // 32]], to - MID, 0)
         for h in range(2):
-            put("w9", 32 + 16 * h + HL, 64, 88, 102, 1)
-            put("w9", 16 * h + HU, 64, 88, 102, 1)
-            for at, first in ((16 * h + HL, 1), (32 + 16 * h + HU, 0)):
-                put("w9", at, 64, 40 + first, 52, 4)
-                put("w9", at + 64 * (12 - first), 64, 52, 54 + first, 8)
+            put("w9", C + 16 * h + HL, 32, 88, 102, 1)
+            put("w9", 16 * h + HU, 32, 88, 102, 1)
+            for at, first in ((16 * h + HL, 1), (C + 16 * h + HU, 0)):
+                put("w9", at, 32, 40 + first, 52, 4)
+                put("w9", at + 32 * (12 - first), 32, 52, 54 + first, 8)
         for a in (JA, C + JE):
             put("x9", a, 16, 140, 168, 1)
         for h, a, b, k, first in ((0, 0, 2, 4, -768), (0, 2, 6, 2, -512), (0, 6, 14, 1, -256),
@@ -510,6 +513,8 @@ def rank_program(g, core, T, topo):
         before = GE if up else GT
         z, rb, rbp, pa, rr = ["%s%d" % (n, t) for n in ("z", "rb", "rbp", "pa", "rr")]
         QT = (A("qt%d" % t), A("st%d" % t))
+        if t == 0:
+            exchange(peer, 6, t, ["st"])
         scores_b(t, 1)
         mm(SAS, *stat("ur", 1), *QT)
         mm(SAV, *stat("ur", 1), *QT)
@@ -565,10 +570,13 @@ def rank_program(g, core, T, topo):
             ts(t2(0, W16), t2(0, W16), 16.0, MUL)
             tt(half("fq", C), IND(win, A("l2_", W16, 2 * W16)), A("tb_"), before)
             tt(A("rs_", 32, 32 + W16), t2(0, W16), A("rs_", 0, W16), ADD)
-            tt(half("fq", 0), half("fq", 0), half("fq", C), ADD)
+            x = cross(t2(32, 32), A("rs_", 32, 64), up, "yy_")
             for a in (0, H):
                 tt(A("fq", 2 * C + a, 2 * C + a + H), IND(win, A("l2_", 2 * W16 + a // 16, 2 * W16 + a // 16 + RUN)),
                    A("tb_", a, a + H), before)
+                next(x)
+                if a == 0:
+                    tt(half("fq", 0), half("fq", 0), half("fq", C), ADD)
             for a in (0, H):
                 tt(A("fp", 16 + a, 16 + a + H), A("fq", a, a + H), A("fq", 2 * C + a, 2 * C + a + H), ADD)
             for a in (0, H):
@@ -577,10 +585,9 @@ def rank_program(g, core, T, topo):
             scan(half("fs", 0), half("k0", 0), half("ft", 0), 0.0, MIN, ADD)
             scan(A("fs", C), A("k0", C), A("ft", C), 0.0, MIN, ADD)
             yield
+            tt(t2(0, 32), IND(A("fs"), A("cx_")), t2(32, 32), ADD)
             tt(A("kw_", 0, 32), IND(A("fs"), A("cl_")), A("rs_", 32, 64), ADD)
             yield
-            for _ in cross(t2(0, 32), A("kw_", 0, 32), up, "yy_"):
-                yield
             copy(A(rb, 0, W16), t2(0, W16))
             exchange(peer, 2, t, ["rb"], W16)
 
@@ -609,7 +616,8 @@ def rank_program(g, core, T, topo):
         weave(sort_b(), counts, SORT_EVERY)
         if t == 0:
             later_constants()
-            turn(A("tab"), A("w9"))
+            for e in range(2):
+                turn(A("tab", e, J, 2), half("w9", C * e))
             turn(A("cc"), A("x9"))
         weave(idle(SEARCH_AT - (2 if t == 0 else 0)), counts, 1)
         weave(search(), counts, SEARCH_EVERY)
@@ -621,18 +629,15 @@ def rank_program(g, core, T, topo):
             act(A("ks"), A("iot"), FN.Identity, bias=col(SUMS), scale=0.0)
         own = unpack(*QT, 0, PW)
 
-        ts(A(pa, 32, 32 + W16), A("ca", H - 1, W16 * H, H), 1.0, SUB)
-        run(cross(A(pa, 0, 32), A(pa, 32, 64), up, "yb"))
+        x = cross(A(pa, 0, 32), A("ca", H - 1, 32 * H, H), up, "yb")
+        next(x)
+        copy(A(pa, 32, 64), A("ca", H - 1, 32 * H, H))
+        next(x)
         exchange(peer, 1, t, [(A(pa, 0, 32), A(pa, 64, 96))])
-        exchange(peer, 3, t, ["qt", "st"])
+        exchange(peer, 3, t, ["qt", "st"] if t else ["qt"])
         copy(A("kw_", 32, 32 + W16), A(rbp, 0, W16))
+        copy(A("lw_"), IND(A("kw_"), sel(SH, up)))
         copy(I(0, 32), IND(A("kw_"), sel(SH, up)))
-        ts(I(32, 32), I(0, 32), 1, AND)
-        ts(I(64, 32), I(0, 32), 1, SHR, 31, AND)
-        ts(t2(0, 32), I(32, 32), 31.0, MUL)
-        tt(t2(32, 32), I(0, 32), I(64, 32), SUB)
-        tt(t1(32, 32), t2(0, 32), t2(32, 32), ADD)
-        copy(A("lw_"), t1(32, 32))
         lw = A("lw_", 0, W16)
         tt(A("r1"), IND(A("tab"), lw), half("cc", 0), ADD)
         if t == 0:
@@ -640,7 +645,7 @@ def rank_program(g, core, T, topo):
 
         parts = ((0, GL), (GL, C))
         short = ((0, 16), (16, 32))
-        ts(A("la_"), IND(A(pa, 32, 96), sel(SH, up)), float(H), ADD)
+        ts(A("la_"), IND(A(pa, 32, 96), sel(SH, up)), float(H - 1), ADD)
         ts(I(96, 32), I(0, 32), 1, SHR)
         copy(IND(A("inv"), A("la_", 0, W16)), A("r1"))
         copy(A("lp_"), I(96, 32))
@@ -648,18 +653,11 @@ def rank_program(g, core, T, topo):
             copy(A("vni", e, C, 2), A("inv", 1 - e, C, 2))
         tt(A("r2"), IND(A("vni"), A("la_", 0, W16)), half("cc", C), ADD)
         copy(IND(A("w9"), lw), A("r2"))
-        for a, b in parts:
-            turn(A("x9", 2 * a, 2 * b), A("w9", 2 * a, 2 * b))
-
-        def join(l, a, b):
-            tt(A("xx", 16 + a + l, 16 + b, 16), A("x9", 2 * a + l, 2 * b, 32), A("x9", 2 * a + 16 + l, 2 * b, 32), ADD)
-        join(HL, 0, GL)
-        join(HU, 0, C)
-        join(EN, 0, C)
         for h in range(2):
-            a = 32 * (1 - h) + EN
-            tt(lane(h, PL), A("x9", a, J, 64), A("x9", a + 16, J, 64), ADD)
-        join(HL, GL, C)
+            turn(half("x9", C * h), A("w9", h, J, 2))
+        for h in range(2):
+            for to, l in ((lane(h, HL), HL), (lane(h, HU), HU), (lane(h, EN), EN), (lane(1 - h, PL), EN)):
+                tt(to, A("x9", C * h + l, C * h + C, 32), A("x9", C * h + 16 + l, C * h + C, 32), ADD)
         turn(A("w0", OWN, OWN + GL), A("xx", 16, 16 + GL))
         turn(A("w0", OWN + GL, OWN + C), A("xx", 16 + GL, 16 + C))
 
@@ -675,15 +673,16 @@ def rank_program(g, core, T, topo):
             for a, b in parts:
                 act(A("wd", a, b), A(wc, OWN + a, OWN + b), FN.Identity, bias=col(FAR), scale=col(KEEP))
             next(own, None)
+            if k:
+                turn(A("xx", 16 + GL, 16 + C), A(wc, OWN + GL, OWN + C))
             if k == 0:
                 other(0)
             turn(A("xx", 496, 976), A(wc, OWN - 16, OWN + C + 16))
-            if k:
-                turn(A("xx", 16 + GL, 16 + C), A(wc, OWN + GL, OWN + C))
-                other(0)
             other(1)
-            offsets(0)
             other(2)
+            offsets(0)
+            if k:
+                other(0)
             offsets(1)
             for a, b in parts:
                 tt(A(wn, OWN + a, OWN + b), IND(A(wc), A("pk_", pk + a // 16, pk + b // 16)), A("wd", a, b), MIN)
@@ -748,18 +747,34 @@ def rank_program(g, core, T, topo):
                 run(side_lists(ups[1]))
         ts(A("lb_"), IND(A(rr, 0, 64), sel(SH, up)), 256.0, ADD)
 
-        for b in range(1, 4):
-            act(A("bh", H * b, H * b + H), IND(half("dw", DP + C * b), A("lb_", 0, RUN)), FN.Copy)
+        pieces = ((0, 128), (128, H))
+        for a, e in pieces:
+            for b in range(0 if a else 1, 4):
+                act(A("bh", H * b + a, H * b + e), IND(half("dw", DP + C * b), A("lb_", a // 16, e // 16)), FN.Copy)
         x = cross(A("x3", C + 32, C + 64), A(rr, 32, 64), 1 - up, "yb")
         next(x)
-        copy(A("bh", 0, H), IND(half("dw", DP), A("lb_", 0, RUN)))
+        copy(A("bh", 0, 128), IND(half("dw", DP), A("lb_", 0, 8)))
         next(x)
+        for a, e in pieces:
+            for b in range(4):
+                tt(A("bt", 4 * a + b, 4 * e, 4), IND(half("dw", DP + C * b), A("lb_", RUN + a // 16, RUN + e // 16)),
+                   A("bh", H * b + a, H * b + e), ADD)
+                if a and b == 0:
+                    quant(A("qb", 0, 128), A("sq", 0, 128), A("bt", 0, 512))
+                    for d in range(4):
+                        mm(PS(4 + d, 128), *stat("e", d), A("qb", 0, 128), A("sq", 0, 128))
+        if t == R - 1:
+            ts(A("lv_"), IND(A(rr, 64, 128), sel(SH, up)), 256.0, ADD)
+            act(A("eo"), IND(A("iot"), A("lv_", 0, RUN)), FN.Copy)
+            for k in range(8):
+                dma("y", "dol", lambda k=k: (T.ol[k:k + 1, :], T.eo[16 * k:16 * k + 1, :]), [A("eo")], [])
+        else:
+            ts(A("ly_"), IND(A("x3", C, C + 64), sel(SH, up)), 256.0, ADD)
+        quant(A("qb", 128, 256), A("sq", 128, 256), A("bt", 512, 1024))
+        if t == R - 1:
+            ts(A("ly_"), IND(A("x3", C, C + 64), sel(SH, up)), 256.0, ADD)
         for b in range(4):
-            tt(A("bt", b, 4 * H, 4), IND(half("dw", DP + C * b), A("lb_", RUN, W16)), A("bh", H * b, H * b + H), ADD)
-        ts(A("ly_"), IND(A("x3", C, C + 64), sel(SH, up)), 256.0, ADD)
-        quant(A("qb"), A("sq"), A("bt"))
-        for b in range(4):
-            mm(PS(b, H), *stat("e", b), A("qb"), A("sq"))
+            mm(PS(b, 128), *stat("e", b), A("qb", 128, 256), A("sq", 128, 256))
 
         def pick(b, s):
             a = PW * b
@@ -773,12 +788,13 @@ def rank_program(g, core, T, topo):
             for name, b in order:
                 mm(PS(b + (4 if name == "w" else 0), H), *stat(name, b), *cols("z", s))
 
-        for b in range(4):
-            came = A("dw", PW * b + 512, PW * b + PW, 8)
-            if b % 2 == 0:
-                ts(came, PS(b, H), 0.5, MUL)
-            else:
-                act(came, PS(b, H), FN.Copy, scale=0.5)
+        for (a, e), bank in zip(pieces, (4, 0)):
+            for b in range(4):
+                came = A("dw", PW * b + 512 + 8 * a, PW * b + 512 + 8 * e, 8)
+                if b % 2 == 0:
+                    ts(came, PS(bank + b, e - a), 0.5, MUL)
+                else:
+                    act(came, PS(bank + b, e - a), FN.Copy, scale=0.5)
 
         for b, s in ((0, 0), (1, 0), (2, 0), (3, 0), (0, 1), (1, 1), (3, 1)):
             pick(b, s)
@@ -803,10 +819,6 @@ def rank_program(g, core, T, topo):
         if t < R - 1:
             rows_b(0)
         else:
-            ts(A("lv_"), IND(A(rr, 64, 128), sel(SH, up)), 256.0, ADD)
-            act(A("eo"), IND(A("iot"), A("lv_", 0, RUN)), FN.Copy)
-            for k in range(8):
-                dma("y", "dol", lambda k=k: (T.ol[k:k + 1, :], T.eo[16 * k:16 * k + 1, :]), [A("eo")], [])
             store(0)
             act(A("yo", 0, H), PS(4, H), FN.Copy)
             dma("s", "dy", lambda: (T.y[:, 0:H], ap(A("yo", 0, H))), [A("yo", 0, H)], [])

from concourse.mybir import dt, AluOpType, ActivationFunctionType

C, H, J, R = 448, 224, 896, 3
STEP = [1, 2, 1]
W16 = C // 16
RUN = W16 // 2
NS = 3 * RUN
ZP = 48
ULP, TINY = 0.6 * 2.0 ** -23, 2.0 ** -124
WQ = J - 15
TW = C + C + 32
PW = 2304
DP = 4 * PW
SC_B, SC_A = (5, 4), (19, 18, 18)
SORT_EVERY, SEARCH_AT, SEARCH_EVERY = 1, 2, 1
MID, OWN, WW = 1024, 784, 2816
RUNS = ((0, 192, 0, 4), (192, 384, 1280, 4), (384, 480, 2048, 8))
GL = 256
STEPS = 8
BIG = 65536.0
HL, HU, EN, PL, JA, JE, EV, ER = range(8)
F32, BF, I32, U16, X4, U8 = "float32", "bfloat16", "int32", "uint16", "float8_e4m3fn_x4", "uint8"

_SB = {
    "x0": (4 * C, BF), "ub": (512, BF), "vb": (512, BF), "xt": (4 * C, BF), "yt": (4 * C, BF), "bt": (1024, BF),
    "qu": (128, X4), "su": (128, U8), "qur": (256, X4), "sur": (256, U8), "qv": (128, X4), "sv": (128, U8),
    "qw": (512, X4), "sw": (512, U8), "qe": (512, X4), "se": (512, U8), "et": (2048, BF), "one": (128, BF),
    "qz": (C, X4), "sz": (C, U8), "qb": (256, X4), "sq": (256, U8), "qt%d" % R: (C, X4), "st%d" % R: (C, U8),
    "pi": (16, I32), "cf": (32, F32), "upi": (16, I32), "upk": (16, U16),
    "r16": (H, BF), "md": (H, BF), "kz": (H, BF), "k0": (TW, BF), "kb": (W16 * NS, BF),
    "iot": (C, F32), "sm": (192, F32), "tab": (J, BF), "cc": (J, BF),
    "msk": (H, F32), "wq": (WQ, F32), "wr": (C - 15, F32), "hb": (H, F32), "eq": (H, BF), "eb": (H, BF),
    "fl": (4 * C, BF), "ca": (32 * H, BF), "cb": (W16 * H // 2, BF), "sg": (3 * C, BF), "lha": (32, F32), "lhb": (32, F32),
    "ii": (160, I32), "wa": (J, F32), "wb": (J, F32), "gap": (J, F32), "zp": (C + 32, F32), "zt": (TW, F32), "fp": (C + 32, BF), "ft": (TW, BF), "fs": (TW, BF),
    "f1": (W16 * NS, BF), "s1": (W16 * NS, BF), "fq": (3 * C, BF),
    "r1": (C, BF), "r2": (C, BF), "inv": (C, BF), "vni": (C, BF), "ks": (C, BF), "yb": (64, BF), "w9": (J, BF), "x9": (J, BF), "x2": (C, BF), "xx": (1024, BF),
    "w0": (WW, BF), "w1": (WW, BF), "wd": (C, BF),
    "red": (C, BF), "mm": (C + 32, BF), "ew": (PW + 128, BF), "x3": (C + 64, BF), "eo": (H, F32),
    "dw": (DP + 4 * C, BF), "bh": (4 * H, F32), "rl": (4 * C, F32), "yo": (C, F32),
}
_PART = {"tb_": ("wb", H, C)}
for _b, _d, _names in (("sf", F32, "rs64 sp64 sq64 sr88 sb88 yy64 kw64 t164 t264 jw32"),
                       ("lu", U16, "cl2 cx2 se24 l132 l284 lw32 lp32 la32 lx32 lv32 lb32 ly32 pk64")):
    _at = 0
    for _x in _names.split():
        _PART[_x[:2] + "_"] = (_b, _at, int(_x[2:]))
        _at += int(_x[2:])
    _SB[_b] = (_at, _d)
for _t in range(R):
    _SB["z%d" % _t] = (96, F32)
    _SB["pa%d" % _t] = (96, BF)
    _SB["rr%d" % _t] = (128, BF)
    for _n, _w, _d in (("rb", 32, U16), ("qt", C, X4), ("st", C, U8)):
        _SB["%s%d" % (_n, _t)] = (_w, _d)
        _SB["%sp%d" % (_n, _t)] = (_w, _d)
SCRATCH = {k: ("sbuf", [128, n], d) for k, (n, d) in _SB.items()}
SCRATCH["ps"] = ("psum", [128, 4096], F32)
SEMAPHORES = ["cp", "cv", "cs", "cg", "sent", "dx", "dz", "du", "dv", "dl", "dol", "doc", "dy", "m5_%d" % (R - 1)] + \
    ["m%d_%d" % (m, t) for m in (0, 1, 2, 3, 4, 6) for t in range(R)] + ["d%s%d" % (x, t) for x in "ab" for t in range(R)]

ADD, SUB, MUL, MAX, MIN = AluOpType.add, AluOpType.subtract, AluOpType.mult, AluOpType.max, AluOpType.min
GE, GT, EQ, NE, LT = AluOpType.is_ge, AluOpType.is_gt, AluOpType.is_equal, AluOpType.not_equal, AluOpType.is_lt
AND, SHR = AluOpType.bitwise_and, AluOpType.logical_shift_right
FN = ActivationFunctionType


def A(name, a=0, b=None, s=1):
    if name in _PART:
        buf, at, n = _PART[name]
        return (buf, at + a, at + (n if b is None else b), s)
    return (name, a, _SB[name][0] if b is None else b, s)


def PS(bank, n=C):
    return ("ps", 512 * bank, 512 * bank + n, 1)


def IND(win, off):
    return ("ind", win, off)


def bits(v):
    if v[0] == "ps":
        return 1 << (v[1] // 512)
    if v[3] == 1:
        return ((1 << (v[2] - v[1])) - 1) << v[1]
    m = 0
    for i in range(v[1], v[2], v[3]):
        m |= 1 << i
    return m


def emit(ops, g, T):
    queue = {"p": g.tensor, "v": g.vector, "s": g.scalar, "g": g, "y": g.sync}
    log, known, count = {}, {e: {} for e in queue}, {}
    for o in ops:
        e = o["q"]
        deps = {}
        for v, wr in [(v, False) for v in o["r"]] + [(v, True) for v in o["w"]]:
            m = bits(v)
            for (m2, wr2, d) in log.get(v[0], []):
                if m & m2 and (wr or wr2 or (v[0] == "ps" and d["lane"] != o["lane"])) and d is not o:
                    if d["lane"] not in deps or deps[d["lane"]]["n"] < d["n"]:
                        deps[d["lane"]] = d
        for d in o.get("after", []):
            deps[d["lane"]] = d
        count[o["lane"]] = count.get(o["lane"], 0) + 1
        o["n"] = count[o["lane"]]
        o["waits"] = []
        if e is not None:
            for d in sorted(deps.values(), key=lambda d: -d["k"]):
                if known[e].get(d["lane"], 0) < d["n"]:
                    o["waits"].append(d)
                    d["inc"] = True
                    for l, n in d["clock"].items():
                        if known[e].get(l, 0) < n:
                            known[e][l] = n
            o["clock"] = dict(known[e])
        else:
            o["clock"] = {}
        o["clock"][o["lane"]] = o["n"]
        for v, wr in [(v, False) for v in o["r"]] + [(v, True) for v in o["w"]]:
            m = bits(v)
            old = log.get(v[0], [])
            if wr:
                old = [x for x in old if x[0] & ~m]
            else:
                old = [x for x in old if not (x[2]["lane"] == o["lane"] and not x[1] and not x[0] & ~m)]
            log[v[0]] = old + [(m, wr, o)]
    total = {}
    for o in ops:
        if o["lane"] in queue:
            if o.get("inc"):
                total[o["lane"]] = total.get(o["lane"], 0) + 1
                o["sem"], o["val"] = "c" + o["lane"], total[o["lane"]]
        elif o["lane"] != "none":
            total[o["lane"]] = total.get(o["lane"], 0) + o["add"]
            o["sem"] = o["lane"]
    for o in ops:
        if o["q"] is None:
            continue
        q = queue[o["q"]]
        for d in o["waits"]:
            q.wait_ge(T.sem[d["sem"]], d["val"] if d["lane"] in queue else total[d["lane"]])
        if o["fn"] is None:
            continue
        ins = o["fn"](q)
        if o["lane"] in queue:
            if o.get("inc"):
                ins.then_inc(T.sem[o["sem"]], 1)
        elif o.get("dma"):
            ins.then_inc(T.sem[o["sem"]], 16)


def rank_program(g, core, T, topo):
    rank = T.rank_of(core)
    if rank is None:
        return
    ops = []

    def ap(v):
        if not isinstance(v, tuple):
            return v
        if v[0] == "ind":
            return ap(v[1]).indirect(ap(v[2]))
        return T[v[0]][:, v[1]:v[2]:v[3]] if v[3] > 1 else T[v[0]][:, v[1]:v[2]]

    def flat(vs):
        out = []
        for v in vs:
            if isinstance(v, tuple):
                out += [v[1], v[2]] if v[0] == "ind" else [v]
        return out

    def rec(q, fn, r, w, lane=None, **kw):
        r, w2 = flat(r), []
        for v in w:
            if v[0] == "ind":
                w2.append(v[1])
                r.append(v[2])
            else:
                w2.append(v)
        o = dict(q=q, fn=fn, r=r, w=w2, lane=lane or q, k=len(ops), **kw)
        ops.append(o)
        return o

    def copy(out, in_):
        return rec("v", lambda q: q.tensor_copy(ap(out), ap(in_)), [in_], [out])

    def turn(out, in_):
        return rec("v", lambda q: q.transpose(ap(out), ap(in_)), [in_], [out])

    def tt(out, a, b, op):
        return rec("v", lambda q: q.tensor_tensor(ap(out), ap(a), ap(b), op), [a, b], [out])

    def ts(out, a, s1, op0, s2=None, op1=None):
        if s2 is None:
            return rec("v", lambda q: q.tensor_scalar(ap(out), ap(a), ap(s1), None, op0), [a, s1], [out])
        return rec("v", lambda q: q.tensor_scalar(ap(out), ap(a), ap(s1), ap(s2), op0, op1), [a, s1, s2], [out])

    def scan(out, d0, d1, init, op0, op1):
        return rec("v", lambda q: q.tensor_tensor_scan(ap(out), ap(d0), ap(d1), ap(init), op0, op1), [d0, d1, init], [out])

    def fill(out, c):
        return rec("v", lambda q: q.memset(ap(out), c), [], [out])

    def quant(codes, scales, in_):
        return rec("v", lambda q: q.quantize_mx(ap(codes), ap(scales), ap(in_)), [in_], [codes, scales])

    def act(out, in_, fn, bias=0.0, scale=1.0, acc=None):
        if acc is None:
            return rec("s", lambda q: q.activation(ap(out), ap(in_), fn, bias=ap(bias), scale=ap(scale)), [in_, bias, scale], [out])
        return rec("s", lambda q: q.activation(ap(out), ap(in_), fn, bias=ap(bias), scale=scale, accum_out=ap(acc)),
                   [in_, bias], [out, acc])

    def mm(out, lc, ls, rc, rs):
        return rec("p", lambda q: q.matmul_mx(ap(out), ap(lc), ap(ls), ap(rc), ap(rs), True, True), [lc, ls, rc, rs], [out])

    def iota(out, pattern, base, cm):
        if _SB[out[0]][1] == I32:
            return rec("g", lambda q: q.iota(ap(out), pattern, base, cm), [], [out])
        return rec("g", lambda q: q.iota(ap(out), pattern, base, cm, allow_small_or_imprecise_dtypes=True), [], [out])

    def dma(q, sem, mk, r, w):
        return rec(q, lambda e: e.dma_start(*mk()), r, w, lane=sem, dma=True, add=16)

    def u8(v):
        return ap(v).bitcast(dt.uint8) if _SB[v[0]][1] == X4 else ap(v)

    def exchange(peer, m, t, names, width=None):
        rid, pid, _ = topo.addr(peer)
        mask, n = topo.mask(core, peer), len(topo.engines(core, peer))
        sem = "m%d_%d" % (m, t)
        pairs = [x if width is None and len(x[0]) == 4 else (A("%s%d" % (x, t), 0, width), A("%sp%d" % (x, t), 0, width))
                 for x in names]
        for src, dst in pairs:
            rec("g", lambda q, src=src, dst=dst: q.remote_dma(u8(dst), u8(src), T.sem[sem], T.sem.sent, pid, rid, mask),
                [src], [], lane="sent", add=n)
        rec(None, None, [], [dst for _, dst in pairs], lane=sem, add=len(topo.engines(peer, core)) * len(names))

    def col(k):
        return A("cf", k, k + 1)

    def I(a, n):
        return A("ii", a, a + n)

    def half(name, a):
        return A(name, a, a + C)

    def t1(a, n):
        return A("t1_", a, a + n)

    def t2(a, n):
        return A("t2_", a, a + n)

    dma("s", "du", lambda: (ap(A("ub")), T.u[:]), [], [A("ub")])
    dma("y", "dx", lambda: (ap(A("x0", 0, J)), T.x[:, 0:J]), [], [A("x0", 0, J)])
    dma("s", "dz", lambda: (ap(A("x0", J)), T.x[:, J:2 * J]), [], [A("x0", J)])
    dma("y", "dv", lambda: (ap(A("vb")), T.v[:]), [A("x0")], [A("vb")])
    dma("y", "dl", lambda: (u8(A("qw")), T.wc[:]), [], [A("qw")])
    dma("y", "dl", lambda: (ap(A("sw")), T.ws[:]), [], [A("sw")])

    ups = [1 if rank & STEP[t] else 0 for t in range(R)]
    Q, P32, PAR, ODD, QHALF, KEEP, FAR, X1, X2, X3, X5, X6, SUMS, P2, P4, P8 = range(16)
    SD, SM, SR, SH, SK, SS = 0, 4, 8, 12, 14, 16

    def sel(k, up=0):
        k += 6 * up
        return A("se_", k, k + 2)

    iota(A("pi", 0, 1), [[1, 1]], 0, 1)
    iota(A("upi"), [[-8, 2], [16, 8]], 8, 0)
    iota(A("sm", 8, 40), [[16, 32]], 0, 0)
    iota(A("r16"), [[0, RUN], [1, 16]], 0, 0)
    p = A("pi", 0, 1)
    ts(A("pi", 1, 2), p, 15, AND)
    ts(A("pi", 2, 3), p, 31, AND)
    ts(A("pi", 3, 4), p, 4, SHR, 1, AND)
    ts(A("pi", 4, 5), p, 1, AND)
    ts(A("pi", 5, 6), p, 1, SHR, 7, AND)
    copy(A("upk"), A("upi"))
    copy(A("cf", 0, 5), A("pi", 1, 6))
    fill(("sf", _PART["yy_"][1], _PART["jw_"][1], 1), 0.0)
    tt(col(X1), col(ODD), col(PAR), NE)
    tt(col(X2), col(ODD), col(PAR), GT)
    ts(col(X3), col(QHALF), 32.0, MUL, 15.0, ADD)
    ts(A("md"), A("r16"), col(Q), EQ)
    ts(A("kz"), A("r16"), col(Q), NE)

    def zeros(*views):
        for v in views:
            iota(v, [[0, v[2] - v[1]]], 0, 0)

    def later_constants():
        zeros(A("yb"), A("bt", 4 * H))
        iota(A("ca", (W16 + 1) * H - 1, 32 * H, H), [[0, 32 - W16]], 0, 0)
        zeros(A("et"))
        for b in range(4):
            out = A("et", 512 * b + b, 512 * (b + 1), 4)
            rec("g", lambda q, out=out: q.affine_select(ap(out), ap(A("one")), [[-1, 128]], EQ, 0.0, 0, 1), [A("one")], [out])
        zeros(A("x2"), A("mm", 0, 16), A("mm", C + 16), A("ew", 384, 512), A("ew", PW), A("rr%d" % (R - 1), 112),
              *[A(w, a, a + 16) for w in ("w0", "w1") for a in (OWN - 16, OWN + C)])

    def side_lists(up):
        ts(col(X1), col(PAR), float(up), NE, 32.0, MUL)
        ts(col(X2), col(ODD), float(up), NE, 14.0, MUL)
        ts(col(X3), col(PAR), float(up), EQ)
        ts(col(X5), col(PAR), float(up), NE)
        ts(sel(SH, up), A("jw_", 0, 2), col(X1), ADD)
        tt(col(X2), col(X2), col(ODD), SUB)
        ts(A("sm", 2, 4), A("jw_", 0, 2), float(C), ADD, col(X5), MUL)
        yield
        ts(col(X6), col(X2), 16.0, MUL, 16.0 * (1 - up) + JE, ADD)
        ts(col(X2), col(X2), 16.0, MUL, 16.0 * up + JE, ADD)
        yield
        ts(sel(SK, up), A("sm", 0, 2), col(X6), ADD, float(C), MIN)
        ts(A("sm", 4, 6), A("sm", 0, 2), col(X2), ADD, float(C), MIN)
        yield
        ts(A("sm", 6, 8), A("sm", 4, 6), col(X3), MUL)
        yield
        tt(A("sm", 4, 6), A("sm", 6, 8), A("sm", 2, 4), ADD)
        yield
        copy(sel(SS, up), A("sm", 4, 6))

    def late_constants():
        iota(A("iot"), [[1, C]], 0, 0)
        iota(A("one"), [[0, 128]], 1, 0)
        zeros(A("zp", 0, 16), A("zp", C + 16), *[A("z%d" % t, a, a + 8) for t in range(R) for a in (32, 88)])
        for l in (EV, ER):
            iota(A("w9", l, J, 16), [[1, 2], [0, W16]], 0, 0)
        zeros(A("rs_", 48, 64), A("fp", 0, 16), A("fp", C + 16))
        iota(A("sb_", 0, 84), [[RUN, 2], [0, RUN], [RUN, 3]], 2, 0)
        iota(A("kb"), [[0, 3 * W16], [64, RUN]], 0, 0)
        iota(A("k0"), [[0, TW // 16], [64, 16]], 0, 0)
        zeros(A("xx"))

    def fixed_lists():
        ts(col(X1), col(X1), float(C), MUL, col(X3), ADD)
        ts(col(X2), col(X2), 2.0, MUL, col(PAR), ADD)
        ts(A("jw_"), A("sm", 8, 40), col(Q), ADD)
        ts(col(X5), col(ODD), -31.0, MUL, 47.0, ADD)
        ts(col(X6), col(ODD), 16.0, MUL, col(QHALF), ADD)
        ts(col(X1), col(X2), 16.0, MUL, col(X1), ADD)
        ts(col(X3), col(PAR), -1008.0, MUL, 16.0, ADD)
        ts(t2(0, 2), A("jw_", 0, 2), 14.0, GE, float(JA - JE - H), MUL)
        ts(t2(2, 2), A("jw_", 0, 2), 16.0, MUL)
        ts(col(X5), col(X5), col(PAR), MUL, col(X6), ADD)
        ts(t1(0, 2), A("sm", 8, 40, 16), col(X1), ADD, float(TW - 1), MIN)
        yield
        ts(col(KEEP), col(Q), float(EN), EQ)
        ts(col(X2), col(Q), float(PL), EQ)
        tt(A("sm", 0, 2), t2(0, 2), t2(2, 2), ADD)
        ts(t1(2, 2), A("sm", 8, 10), 0.5, MUL, col(X5), ADD)
        ts(col(X6), col(PAR), -32.0, MUL, 16.0, ADD)
        copy(A("cl_"), t1(0, 2))
        tt(col(KEEP), col(KEEP), col(X2), ADD)
        ts(A("cx_"), t1(0, 2), col(X6), ADD, float(TW - 1), MIN)
        yield
        ts(col(SUMS), col(Q), float(EV), EQ)
        ts(t1(4, 2), t1(2, 2), 32.0, MUL, col(X3), ADD)
        ts(col(FAR), col(KEEP), -BIG, MUL, BIG, ADD)
        ts(A("se_", SD, SD + 4, 2), t1(4, 2), col(PAR), ADD)
        ts(A("se_", SM, SM + 4, 2), t1(4, 2), float(EV), ADD)
        ts(A("se_", SR, SR + 4, 2), t1(4, 2), float(ER), ADD)

    def tables():
        times = {1: P32, 2: P2, 4: P4, 8: P8}

        def put(name, at, step, a, b, k):
            act(A(name, at, at + step * (b - a - 1) + 1, step), A("sm", a, b), FN.Identity, bias=col(times[k]))
        iota(A("sm", 88, 102), [[32, 14]], OWN - MID, 0)
        iota(A("sm", 140, 168), [[32, 14], [0, 2]], -256, 0)
        for a, b, to, step in RUNS:
            iota(A("sm", 40 + a // 32, 40 + b // 32), [[32 * step, (b - a) // 32]], to - MID, 0)
        for h in range(2):
            put("w9", C + 16 * h + HL, 32, 88, 102, 1)
            put("w9", 16 * h + HU, 32, 88, 102, 1)
            for at, first in ((16 * h + HL, 1), (C + 16 * h + HU, 0)):
                put("w9", at, 32, 40 + first, 52, 4)
                put("w9", at + 32 * (12 - first), 32, 52, 54 + first, 8)
        for a in (JA, C + JE):
            put("x9", a, 16, 140, 168, 1)
        for h, a, b, k, first in ((0, 0, 2, 4, -768), (0, 2, 6, 2, -512), (0, 6, 14, 1, -256),
                                  (1, 0, 8, 1, 0), (1, 8, 12, 2, 256), (1, 12, 14, 4, 512)):
            iota(A("sm", 112 + 14 * h + a, 112 + 14 * h + b), [[32 * k, b - a]], first, 0)
            put("x9", 32 * a + 16 * h + EN, 32, 112 + 14 * h + a, 112 + 14 * h + b, k)

    def run(x):
        for _ in x:
            pass

    for name, k in ((P2, 2.0), (P4, 4.0), (P8, 8.0)):
        ts(col(name), col(P32), k, MUL)
    fill(A("w9"), 0.0)
    fill(A("x9"), 0.0)
    tables()
    fixed = fixed_lists()
    next(fixed)
    quant(A("qu"), A("su"), A("ub"))
    quant(A("qt0", 0, H), A("st0", 0, H), A("x0", 0, J))
    rec("v", lambda q: q.tensor_copy(ap(A("qur")).bitcast(dt.uint32), ap(A("qu")).bitcast(dt.uint32).indirect(ap(A("upk")))),
        [A("qu"), A("upk")], [A("qur")])
    rec("s", lambda q: q.activation(ap(A("sur")), ap(IND(A("su"), A("upk"))), FN.Copy), [A("su"), A("upk")], [A("sur")])

    def stat(name, b):
        return A("q" + name, 128 * b, 128 * b + 128), A("s" + name, 128 * b, 128 * b + 128)

    def chain(*gens):
        for x in gens:
            for _ in x:
                yield

    def idle(n):
        for _ in range(n):
            yield

    def part(src, a, b):
        return (src[0], src[1] + a, src[1] + b, 1)

    def rivals(src, c, w):
        if w == C:
            return A("wq", 16 * c + 1, 16 * c + 1 + w), True
        if c < RUN:
            return A("wr", 16 * c + 1, 16 * c + 1 + w), True
        return A("wb", 16 * c + 16 + H, 16 * c + 16 + C), False

    def mine(h, c):
        if h is None:
            return A("wq", C + 16 * c, C + 16 * c + 1)
        return A("wr", H + 16 * c, H + 16 * c + 1) if c < RUN else A("hb", 16 * c - H + 15, 16 * c - H + 16)

    def vector_counts(src, h, out, blocks, w):
        last, m = None, w // 2
        for n, c in enumerate(list(blocks) + [None]):
            f = C * (n % 4)
            if c is not None:
                row, first = rivals(src, c, w)
                ts(A("fl", f, f + w), row, mine(h, c), GE if first else GT, 0.5, SUB)
            yield
            if last is not None:
                scan(A(out, last[1] * m, last[1] * m + m), A("fl", last[0], last[0] + m), A("fl", last[0] + m, last[0] + w),
                     0.0, ADD, ADD)
                yield
            last = (f, c)

    def weave(steps, filler, every):
        for n, _ in enumerate(steps):
            if n % every == every - 1:
                next(filler, None)

    def scalar_counts(src, h, lh, out, blocks, w):
        last = None
        for n, c in enumerate([c for a, b in blocks for c in range(a, b)] + [None]):
            f = C * (n % 3)
            if c is not None:
                act(A("sg", f, f + w), rivals(src, c, w)[0], FN.Sign, bias=mine(h, c), scale=-1.0)
            if last is not None:
                a = A("sg", last[0], last[0] + w)
                act(a, a, FN.Sign, bias=0.5 if rivals(src, last[1], w)[1] else -0.5, scale=-1.0, acc=A(lh, last[1], last[1] + 1))
            last = (f, c)
            yield
        m = w // 2
        for a, b in blocks:
            act(A(out, a * m + m - 1, b * m, m), A(lh, a, b), FN.Copy, scale=0.5)

    def unpack(codes, scales, at, step):
        for b in range(4):
            mm(PS(4 + b), *stat("e", b), codes, scales)
            act(half("dw", at + step * b), PS(4 + b), FN.Copy, scale=0.5)
            yield

    def cross(out, src, to, via):
        turn(A(via, 16, 48), src)
        yield
        turn(out, A(via, 32 - 32 * to, 64 - 32 * to))
        yield

    def lane(h, l, a=0, b=C):
        return A("xx", 16 + a + 16 * h + l, 16 + b, 32)

    def cols(name, s):
        return A("q" + name, H * s, H * s + H), A("s" + name, H * s, H * s + H)

    SBV, SBS, SAV, SAS = [PS(4, H), PS(6, H)], [PS(5, H), PS(7, H)], PS(0), PS(1)

    def scores_b(t, s):
        for out in (SBV[s], SBS[s]) if s else (SBS[s], SBV[s]):
            mm(out, *stat("ur", 0), *cols("t%d" % t, s))

    def store(s):
        codes, scales = cols("t%d" % R, s)
        mm(PS(4 + s, H), A("qv"), A("sv"), codes, scales)
        dma("y", "doc", lambda: (T.oc[:, J * s:J * s + J], u8(codes)), [codes], [])

    def rows_b(s):
        act(A("gap", H * s, H * s + H), SBS[s], FN.Abs, bias=TINY, scale=ULP)
        act(A("tb_", H * s, H * s + H), SBS[s], FN.Copy)

    def early_b(t):
        tt(A("wb", 0, H), SBV[0], A("gap", 0, H), SUB)
        for q in range(16):
            dma("y", "db%d" % t, lambda q=q: (T.wr[q::16, :], T.wb[q::16, q:q + C - 15]), [half("wb", 0)], [] if q else [A("wr")])

    scores_b(0, 0)
    rows_b(0)
    quant(*cols("t0", 1), A("x0", J, 2 * J))
    next(fixed)
    early_b(0)
    run(fixed)
    for t in range(R):
        peer = T.cores[rank ^ STEP[t]]
        up = ups[t]
        before = GE if up else GT
        z, rb, rbp, pa, rr = ["%s%d" % (n, t) for n in ("z", "rb", "rbp", "pa", "rr")]
        QT = (A("qt%d" % t), A("st%d" % t))
        if t == 0:
            exchange(peer, 6, t, ["st"])
        scores_b(t, 1)
        mm(SAS, *stat("ur", 1), *QT)
        mm(SAV, *stat("ur", 1), *QT)

        def sort_b():
            ts(t1(0, RUN), A("cb", H // 2 - 1, RUN * H // 2, H // 2), 1.0, SUB)
            tt(t1(RUN, RUN), A("cb", (RUN + 1) * H // 2 - 1, W16 * H // 2, H // 2), A("eb", 15, H, 16), SUB)
            yield
            for r in range(2):
                ts(A("l1_", RUN * r, RUN * r + RUN), t1(RUN * r, RUN), float(H // 2 + H * r), ADD)
            ts(A("rs_", 0, W16), t1(0, W16), float(H // 2), ADD)
            yield
            copy(IND(half("zp", 16), A("l1_", 0, W16)), A("tb_"))
            yield
            turn(half("zt", 0), half("zp", 16))
            turn(A("zt", C, TW), A("zp"))
            yield
            copy(A(z, 0, 32), IND(A("zt"), A("cl_")))
            exchange(peer, 0, t, [(A(z, 0, W16), A(z, ZP, ZP + W16))])
            yield
            moved, home = A(z, RUN * up, RUN * up + RUN), [ZP + W16, ZP - RUN]
            ts(t2(0, RUN), moved, ULP, MUL, TINY, ADD)
            ts(t2(16, RUN), moved, -ULP, MUL, TINY, ADD)
            copy(A(z, home[1 - up], home[1 - up] + RUN), A(z, RUN * (1 - up), RUN * (2 - up)))
            yield
            tt(t2(32, RUN), t2(0, RUN), t2(16, RUN), MAX)
            yield
            tt(A(z, home[up], home[up] + RUN), moved, t2(32, RUN), SUB if up else ADD)
            yield

        def search():
            turn(A("sp_", 0, 64), A(z, 32, 96))
            yield
            for k in range(4):
                ts(A("sq_", 16 * k, 16 * k + 16), A("iot", 0, 16), 0.0, MUL, A("sp_", 16 * k + 15, 16 * k + 16), ADD)
            yield
            turn(A("sp_", 0, 64), A("sq_", 0, 64))
            yield
            for c in range(W16):
                a = 2 + c // RUN * RUN
                ts(A("f1", NS * c, NS * c + NS), A("sp_", a, a + NS), mine("hb", c), before)
            for a in (0, RUN * NS):
                scan(A("s1", a, a + RUN * NS), A("kb", a, a + RUN * NS), A("f1", a, a + RUN * NS), 0.0, MIN, ADD)
            yield
            found = [A("s1", RUN * s + RUN - 2, W16 * NS, NS) for s in range(3)]
            tt(A("sr_", 0, 84), A("s1", RUN - 2, W16 * NS, RUN), A("sb_", 0, 84), ADD)
            tt(t2(0, W16), found[0], found[1], ADD)
            for s in range(3):
                copy(A("l2_", W16 * s, W16 * s + W16), A("sr_", s, 84, 3))
            tt(t2(0, W16), t2(0, W16), found[2], ADD)
            win = A(z, 32, 96)
            tt(half("fq", 0), IND(win, A("l2_", 0, W16)), A("tb_"), before)
            ts(t2(0, W16), t2(0, W16), 16.0, MUL)
            tt(half("fq", C), IND(win, A("l2_", W16, 2 * W16)), A("tb_"), before)
            tt(A("rs_", 32, 32 + W16), t2(0, W16), A("rs_", 0, W16), ADD)
            x = cross(t2(32, 32), A("rs_", 32, 64), up, "yy_")
            for a in (0, H):
                tt(A("fq", 2 * C + a, 2 * C + a + H), IND(win, A("l2_", 2 * W16 + a // 16, 2 * W16 + a // 16 + RUN)),
                   A("tb_", a, a + H), before)
                next(x)
                if a == 0:
                    tt(half("fq", 0), half("fq", 0), half("fq", C), ADD)
            for a in (0, H):
                tt(A("fp", 16 + a, 16 + a + H), A("fq", a, a + H), A("fq", 2 * C + a, 2 * C + a + H), ADD)
            for a in (0, H):
                turn(A("ft", a, a + H), A("fp", 16 + a, 16 + a + H))
            turn(A("ft", C, TW), A("fp"))
            scan(half("fs", 0), half("k0", 0), half("ft", 0), 0.0, MIN, ADD)
            scan(A("fs", C), A("k0", C), A("ft", C), 0.0, MIN, ADD)
            yield
            tt(t2(0, 32), IND(A("fs"), A("cx_")), t2(32, 32), ADD)
            tt(A("kw_", 0, 32), IND(A("fs"), A("cl_")), A("rs_", 32, 64), ADD)
            yield
            copy(A(rb, 0, W16), t2(0, W16))
            exchange(peer, 2, t, ["rb"], W16)

        rows_b(1)
        act(half("gap", C), SAS, FN.Abs, bias=TINY, scale=ULP)
        tt(A("msk"), SBV[1], A("md"), MUL)
        scan(A("hb"), A("kz"), A("msk"), 0.0, MUL, ADD)
        tt(A("wb", 3 * H, J), SBV[1], A("gap", H, C), ADD)
        x = scalar_counts("wb", "hb", "lhb", "cb", [(RUN, RUN + SC_B[1]), (0, SC_B[0])], H)
        next(x)
        act(half("wa", C), SAS, FN.Copy)
        run(x)
        counts = vector_counts("wb", "hb", "cb", list(range(RUN + SC_B[1], W16)) + list(range(SC_B[0], RUN)), H)
        tt(A("eq"), SBV[1], A("hb"), EQ)
        next(counts)
        tt(half("wa", 0), SAV, half("gap", C), SUB)
        for q in range(16):
            dma("y", "da%d" % t, lambda q=q: (T.wq[q::16, :], T.wa[q::16, q:q + WQ]), [A("wa")], [] if q else [A("wq")])
        scan(A("eb"), A("kz"), A("eq"), 0.0, MUL, ADD)
        if t == 0:
            late_constants()
        run(counts)
        run(scalar_counts("wq", None, "lha", "ca", [(0, SC_A[t])], C))
        counts = vector_counts("wq", None, "ca", range(SC_A[t], W16), C)
        next(counts)
        weave(sort_b(), counts, SORT_EVERY)
        if t == 0:
            later_constants()
            for e in range(2):
                turn(A("tab", e, J, 2), half("w9", C * e))
            turn(A("cc"), A("x9"))
        weave(idle(SEARCH_AT - (2 if t == 0 else 0)), counts, 1)
        weave(search(), counts, SEARCH_EVERY)
        if t == 0:
            weave(side_lists(up), counts, 1)
        run(counts)
        if t == 0:
            act(A("w9"), A("tab"), FN.Copy, scale=0.0)
            act(A("ks"), A("iot"), FN.Identity, bias=col(SUMS), scale=0.0)
        own = unpack(*QT, 0, PW)

        x = cross(A(pa, 0, 32), A("ca", H - 1, 32 * H, H), up, "yb")
        next(x)
        copy(A(pa, 32, 64), A("ca", H - 1, 32 * H, H))
        next(x)
        exchange(peer, 1, t, [(A(pa, 0, 32), A(pa, 64, 96))])
        exchange(peer, 3, t, ["qt", "st"] if t else ["qt"])
        copy(A("kw_", 32, 32 + W16), A(rbp, 0, W16))
        copy(A("lw_"), IND(A("kw_"), sel(SH, up)))
        copy(I(0, 32), IND(A("kw_"), sel(SH, up)))
        lw = A("lw_", 0, W16)
        tt(A("r1"), IND(A("tab"), lw), half("cc", 0), ADD)
        if t == 0:
            quant(A("qe"), A("se"), A("et"))

        parts = ((0, GL), (GL, C))
        short = ((0, 16), (16, 32))
        ts(A("la_"), IND(A(pa, 32, 96), sel(SH, up)), float(H - 1), ADD)
        ts(I(96, 32), I(0, 32), 1, SHR)
        copy(IND(A("inv"), A("la_", 0, W16)), A("r1"))
        copy(A("lp_"), I(96, 32))
        for e in range(2):
            copy(A("vni", e, C, 2), A("inv", 1 - e, C, 2))
        tt(A("r2"), IND(A("vni"), A("la_", 0, W16)), half("cc", C), ADD)
        copy(IND(A("w9"), lw), A("r2"))
        for h in range(2):
            turn(half("x9", C * h), A("w9", h, J, 2))
        for h in range(2):
            for to, l in ((lane(h, HL), HL), (lane(h, HU), HU), (lane(h, EN), EN), (lane(1 - h, PL), EN)):
                tt(to, A("x9", C * h + l, C * h + C, 32), A("x9", C * h + 16 + l, C * h + C, 32), ADD)
        turn(A("w0", OWN, OWN + GL), A("xx", 16, 16 + GL))
        turn(A("w0", OWN + GL, OWN + C), A("xx", 16 + GL, 16 + C))

        for k in range(STEPS):
            wc, wn, pk = "w%d" % (k % 2), "w%d" % (1 - k % 2), 32 * (k % 2)

            def other(n):
                a, b, to, step = RUNS[n]
                turn(A(wc, to, to + step * (b - a), step), A("xx", a, b))

            def offsets(n):
                ts(A("pk_", pk + 16 * n, pk + 16 * n + 16), IND(A("xx"), A("se_", SD + 2 * n, SD + 2 * n + 1)), float(MID), ADD)
            for a, b in parts:
                act(A("wd", a, b), A(wc, OWN + a, OWN + b), FN.Identity, bias=col(FAR), scale=col(KEEP))
            next(own, None)
            if k:
                turn(A("xx", 16 + GL, 16 + C), A(wc, OWN + GL, OWN + C))
            if k == 0:
                other(0)
            turn(A("xx", 496, 976), A(wc, OWN - 16, OWN + C + 16))
            other(1)
            other(2)
            offsets(0)
            if k:
                other(0)
            offsets(1)
            for a, b in parts:
                tt(A(wn, OWN + a, OWN + b), IND(A(wc), A("pk_", pk + a // 16, pk + b // 16)), A("wd", a, b), MIN)
            turn(A("xx", 16, 16 + GL), A(wn, OWN, OWN + GL))
        turn(A("xx", 16 + GL, 16 + C), A(wn, OWN + GL, OWN + C))

        run(unpack(A("qtp%d" % t), A("stp%d" % t), DP, C))

        for a, b in parts:
            tt(t1(a // 32, (b - a) // 32), lane(0, PL, a, b), lane(1, EN, a, b), MIN)
            tt(t1(16 + a // 32, (b - a) // 32), lane(0, EN, a, b), lane(1, PL, a, b), MIN)

        def flags(l, a, b):
            tt(A("x2", a + l, b, 32), t1(a // 32, (b - a) // 32), t1(16 + a // 32, (b - a) // 32), LT)
        flags(EV, 0, GL)
        for l in (ER, 16 + EV, 16 + ER):
            flags(l, 0, C)
        flags(EV, GL, C)
        for a, b in parts:
            turn(A("inv", a, b), A("x2", a, b))
        thirds = ((0, 160), (160, 320), (320, C))

        def colour(n):
            a, b = thirds[n]
            tt(A("red", a, b), IND(A("inv"), A("lp_", a // 16, b // 16)), A("r1", a, b), NE)

        def number(n):
            a, b = thirds[n]
            scan(A("mm", 16 + a, 16 + b), A("ks", a, b), A("red", a, b), A("mm", 15 + a, 16 + a), MUL, ADD)

        def turned(n):
            a, b = thirds[n]
            turn(A("xx", 16 + a, 16 + b), A("mm", 16 + a, 16 + b))
        for f, n in ((colour, 0), (colour, 1), (number, 0), (colour, 2), (number, 1), (turned, 0), (number, 2), (turned, 1)):
            f(n)
        if t < R - 1:
            act(A("w9"), A("tab"), FN.Copy, scale=0.0)
        turn(A("xx", 496, 976), A("mm"))
        turned(2)
        for n, (a, b) in enumerate(short):
            ts(t1(a, 16), IND(A("xx"), A("se_", SM + 2 * n, SM + 2 * n + 1)), 8.0, MUL, 504.0, ADD)
        for n, (a, b) in enumerate(short):
            tt(t1(32 + a, 16), IND(A("xx"), A("se_", SR + 2 * n, SR + 2 * n + 1)), t1(a, 16), MUL)
        for a, b in short:
            tt(t2(a, 16), t1(32 + a, 16), A("jw_", a, b), MAX)
        for a, b in short:
            copy(A("lv_", a, b), t2(a, 16))
        ts(A("x3", C, C + 16), t2(0, 16), 256.0, SUB)
        copy(IND(A("ew", 0, PW), A("lv_", 0, W16)), A("r2"))
        ts(A("x3", C + 16, C + 32), t2(16, 16), 256.0, SUB)
        turn(A("x3", 0, H), A("ew", 512, PW, 8))
        a = 640 - 256 * up
        turn(A("x3", H, C), A("ew", a, a + 8 * H, 8))
        copy(A(rr, 64, 96), IND(A("x3", 0, C + 32), sel(SS, up)))
        exchange(peer, 4, t, [(A(rr, 64, 96), A(rr, 32, 64))])
        copy(A(rr, 0, 32), IND(A("x3", 0, C + 32), sel(SK, up)))
        if t == R - 1:
            exchange(peer, 5, t, [(A(rr, 0, 16), A(rr, 96, 112))])
        if t == 0:
            quant(A("qv"), A("sv"), A("vb"))
            if ups[1] != up:
                run(side_lists(ups[1]))
        ts(A("lb_"), IND(A(rr, 0, 64), sel(SH, up)), 256.0, ADD)

        pieces = ((0, 128), (128, H))
        for a, e in pieces:
            for b in range(0 if a else 1, 4):
                act(A("bh", H * b + a, H * b + e), IND(half("dw", DP + C * b), A("lb_", a // 16, e // 16)), FN.Copy)
        x = cross(A("x3", C + 32, C + 64), A(rr, 32, 64), 1 - up, "yb")
        next(x)
        copy(A("bh", 0, 128), IND(half("dw", DP), A("lb_", 0, 8)))
        next(x)
        for a, e in pieces:
            for b in range(4):
                tt(A("bt", 4 * a + b, 4 * e, 4), IND(half("dw", DP + C * b), A("lb_", RUN + a // 16, RUN + e // 16)),
                   A("bh", H * b + a, H * b + e), ADD)
                if a and b == 0:
                    quant(A("qb", 0, 128), A("sq", 0, 128), A("bt", 0, 512))
                    for d in range(4):
                        mm(PS(4 + d, 128), *stat("e", d), A("qb", 0, 128), A("sq", 0, 128))
        if t == R - 1:
            ts(A("lv_"), IND(A(rr, 64, 128), sel(SH, up)), 256.0, ADD)
            act(A("eo"), IND(A("iot"), A("lv_", 0, RUN)), FN.Copy)
            for k in range(8):
                dma("y", "dol", lambda k=k: (T.ol[k:k + 1, :], T.eo[16 * k:16 * k + 1, :]), [A("eo")], [])
        else:
            ts(A("ly_"), IND(A("x3", C, C + 64), sel(SH, up)), 256.0, ADD)
        quant(A("qb", 128, 256), A("sq", 128, 256), A("bt", 512, 1024))
        if t == R - 1:
            ts(A("ly_"), IND(A("x3", C, C + 64), sel(SH, up)), 256.0, ADD)
        for b in range(4):
            mm(PS(b, 128), *stat("e", b), A("qb", 128, 256), A("sq", 128, 256))

        def pick(b, s):
            a = PW * b
            win, out = IND(A("dw", a, a + PW), A("ly_", RUN * s, RUN * s + RUN)), A("yt", J * s + b, J * s + J, 4)
            if b % 2 == 0:
                ts(out, win, 2.0, MUL)
            else:
                act(out, win, FN.Copy, scale=2.0)

        def products(s, order):
            for name, b in order:
                mm(PS(b + (4 if name == "w" else 0), H), *stat(name, b), *cols("z", s))

        for (a, e), bank in zip(pieces, (4, 0)):
            for b in range(4):
                came = A("dw", PW * b + 512 + 8 * a, PW * b + 512 + 8 * e, 8)
                if b % 2 == 0:
                    ts(came, PS(bank + b, e - a), 0.5, MUL)
                else:
                    act(came, PS(bank + b, e - a), FN.Copy, scale=0.5)

        for b, s in ((0, 0), (1, 0), (2, 0), (3, 0), (0, 1), (1, 1), (3, 1)):
            pick(b, s)
        quant(*cols("z", 0), A("yt", 0, J))
        products(0, [("w", 0), ("e", 0), ("w", 1), ("e", 1), ("w", 2), ("e", 2), ("w", 3), ("e", 3)])
        pick(2, 1)
        for s in range(2):
            for b in range(4):
                rl = A("rl", C * b + H * s, C * b + H * s + H)
                if (s, b) == (0, 0):
                    ts(rl, PS(4, H), 0.0, MAX, 0.03125, MUL)
                    quant(*cols("z", 1), A("yt", J, 2 * J))
                else:
                    act(rl, PS(4 + b, H), FN.Relu, scale=0.03125)
                tt(A("xt", J * s + b, J * s + J, 4), PS(b, H), rl, ADD)
                if s == 0:
                    products(1, [("w", b), ("e", b)])
                if (s, b) == (1, 0):
                    quant(*cols("t%d" % (t + 1), 0), A("xt", 0, J))
                if (s, b) == (1, 1) and t < R - 1:
                    scores_b(t + 1, 0)
        if t < R - 1:
            rows_b(0)
        else:
            store(0)
            act(A("yo", 0, H), PS(4, H), FN.Copy)
            dma("s", "dy", lambda: (T.y[:, 0:H], ap(A("yo", 0, H))), [A("yo", 0, H)], [])
        quant(*cols("t%d" % (t + 1), 1), A("xt", J, 2 * J))
        if t < R - 1:
            early_b(t + 1)

    store(1)
    for k in range(4):
        dma("ys"[k % 2], "doc", lambda k=k: (T.osc[4 * k:4 * k + 4, :], T["st%d" % R][32 * k:32 * k + 4, :]), [A("st%d" % R)], [])
    copy(A("yo", H, C), PS(5, H))
    dma("s", "dy", lambda: (T.y[:, H:C], ap(A("yo", H, C))), [A("yo", H, C)], [])
    ends = {}
    for o in ops:
        if o["lane"] in ("dol", "doc", "dy", "sent"):
            ends[o["lane"]] = o
    rec("y", None, [], [], lane="none", after=list(ends.values()))
    emit(ops, g, T)
